import numpy as np
import ml_dtypes


def mxq(x, axis, fmt="e4m3"):
    dtype, down = {"e4m3": (ml_dtypes.float8_e4m3fn, 7), "e5m2": (ml_dtypes.float8_e5m2, 14)}[fmt]
    v = np.moveaxis(np.asarray(x, np.float32).astype(ml_dtypes.bfloat16).astype(np.float64), axis, -1)
    blocks = v.reshape(v.shape[:-1] + (-1, 32))
    amax = np.abs(blocks).max(-1, keepdims=True)
    byte = np.maximum(np.where(amax > 0, np.frexp(amax)[1] - 1 + 127, 0) - down, 1)
    scale = np.exp2(byte - 127.0)
    codes = (blocks / scale).astype(np.float32).astype(dtype).astype(np.float64)
    return np.moveaxis((codes * scale).reshape(v.shape), -1, axis)


WIDE = False


def mx_kscale(k):
    if not WIDE:
        return np.ones(k)
    levels = np.array([18, -18])
    if k % 512:
        return np.exp2(np.random.permutation(np.resize(levels, k // 32))).repeat(32)
    a = np.empty((k // 512, 16))
    for p in range(k // 512):
        a[p, :8] = np.random.permutation(np.resize(levels, 8))
        for g in range(8):
            far = levels[np.abs(levels - a[p, g]) >= 10]
            a[p, g + 8] = far[np.random.randint(len(far))]
    return np.exp2(a.ravel()).repeat(32)


def f64(x):
    return np.asarray(x).astype(np.float64)


def striped(idx):
    return np.tile(np.asarray(idx).reshape(-1, 16).T, (8, 1)).astype(np.uint16)


def unstriped(offs):
    return offs[:16].T.reshape(-1).astype(np.int64)


B, N, T, D, R = 2, 512, 2048, 512, 512


def setup_inputs():
    n = np.random.standard_normal
    idx = np.random.permutation(T)[:B * N]
    u = np.ones(T)
    u[idx] = mx_kscale(B * N)
    us = u[idx].reshape(B, N)
    act = n((B, R, N))
    s = mx_kscale(D)
    return {
        "zT": (act.transpose(0, 2, 1) * us[:, :, None]).astype(np.float32),
        "wT": (n((D, T)) / np.sqrt(N) / u * s[:, None]).astype(np.float32),
        "xm": (n((B, R, D)) * s).astype(np.float32),
        "wt": (np.random.uniform(0.5, 1.5, (B, R, 1)) / np.sqrt(R)).astype(np.float32),
        "cs": np.tile(np.random.uniform(0.5, 1.5, D) / s, (128, 1)).astype(np.float32),
        "offs": striped(idx),
    }


def reference(zT, wT, xm, wt, cs, offs):
    idx = unstriped(offs)
    pick = lambda x: x[:, idx].reshape(x.shape[0], B, N).transpose(1, 0, 2)
    w = pick(f64(wT))
    rec = mxq(f64(zT), 1, "e4m3").transpose(0, 2, 1) @ mxq(w, 2, "e4m3").transpose(0, 2, 1)
    q = f64(cs)[:1] * (rec - f64(xm))
    e = f64(wt) * f64(cs)[:1] * q / (1.0 + q * q)
    gz = mxq(e, 2, "e5m2") @ mxq(w, 1, "e4m3")
    return gz

@@ -1,0 +1,268 @@
+from contextlib import ExitStack
+
+import concourse.mybir as mybir
+from concourse.masks import make_identity
+
+B, N, T, D, R = 2, 512, 2048, 512, 512
+FLOPS = 2 * 2 * B * R * N * D
+
+F32 = mybir.dt.float32
+BF16 = mybir.dt.bfloat16
+U32 = mybir.dt.uint32
+U16 = mybir.dt.uint16
+U8 = mybir.dt.uint8
+E4M3 = mybir.dt.float8_e4m3fn_x4
+E5M2 = mybir.dt.float8_e5m2_x4
+ALU = mybir.AluOpType
+ACT = mybir.ActivationFunctionType
+
+P = 128
+PACK = 4
+CHUNKS = R // P
+LIST_COLS = N // 16
+SCALAR_SQUARES = (0, 2, 4, 5)
+W_PIECES = [(0, 0, 1024, "scalar"), (0, 1024, 1024, "vector"), (1, 0, 1024, "scalar"), (1, 1024, 512, "vector"), (1, 1536, 512, "vector")]
+
+
+def tile_attend_gdi_cau_z_kernel(tc, zT, wT, xm, wt, cs, offs, out):
+    nc = tc.nc
+    with ExitStack() as ctx:
+        keep = ctx.enter_context(tc.tile_pool(name="keep", bufs=1))
+        work = ctx.enter_context(tc.tile_pool(name="work", bufs=3))
+        psum = ctx.enter_context(tc.psum_pool(name="psum", bufs=2))
+
+        offsets = keep.tile([P, B * LIST_COLS], U16, name="offsets")
+        nc.sync.dma_start(offsets[:], offs)
+
+        wt_rows = keep.tile([P, P], F32, name="wt_rows")
+        nc.gpsimd.memset(wt_rows[:], 0.0)
+        ident = keep.tile([P, P], F32, name="ident")
+        make_identity(nc, ident[:])
+        c_cols = keep.tile([P, PACK], F32, name="c_cols")
+        nc.scalar.dma_start(out=c_cols[:], in_=cs[0, :].rearrange("(p t) -> p t", t=PACK))
+        nc.scalar.dma_start(out=wt_rows[0 : B * CHUNKS, :], in_=wt.rearrange("b (j p) o -> (b j) (p o)", p=P))
+        warm = keep.tile([P, 1], F32, name="warm")
+        nc.scalar.activation(warm[:], ident[:, 0:1], ACT.Abs_reciprocal_sqrt, bias=1.0)
+
+        w_planes = wT.rearrange("(p t) c -> p t c", t=PACK)
+        w_raw = []
+        for n, (u, c0, width, engine) in enumerate(W_PIECES):
+            raw = keep.tile([P, 2, width], F32, name=f"w_raw{n}")
+            nc.sync.dma_start(out=raw[:], in_=w_planes[:, 2 * u : 2 * u + 2, c0 : c0 + width])
+            w_raw.append(raw)
+        z_raw = {}
+        x_raw = {}
+        for b in range(B):
+            z_raw[b] = keep.tile([P, PACK, R], F32, name=f"z_raw{b}")
+            nc.sync.dma_start(out=z_raw[b][:], in_=zT[b].rearrange("(p t) r -> p t r", t=PACK))
+            for h in range(2):
+                x_raw[b, h] = keep.tile([P, 2, D], F32, name=f"x_raw{b}{h}")
+                nc.sync.dma_start(out=x_raw[b, h][:], in_=xm[b, 256 * h : 256 * h + 256, :].rearrange("(j p) d -> p j d", p=P))
+
+        wt_ps = psum.tile([P, PACK, P], F32, name="wt_ps", tag="res")
+        nc.tensor.transpose(wt_ps[:, 0, :], wt_rows[:], ident[:])
+        wt_cols = keep.tile([P, B * CHUNKS], F32, name="wt_cols")
+        nc.vector.tensor_copy(out=wt_cols[:], in_=wt_ps[:, 0, 0 : B * CHUNKS])
+        c_sq = keep.tile([P, PACK], F32, name="c_sq")
+        nc.vector.tensor_tensor(c_sq[:], c_cols[:], c_cols[:], ALU.mult)
+        wt_safe = keep.tile([P, B * CHUNKS], F32, name="wt_safe")
+        nc.vector.scalar_tensor_tensor(wt_safe[:], wt_cols[:], 0.0, wt_cols[:], ALU.is_equal, ALU.add)
+        noise_sq = keep.tile([P, PACK], F32, name="noise_sq")
+        nc.vector.reciprocal(noise_sq[:], c_sq[:])
+        wt_inv = keep.tile([P, B * CHUNKS], F32, name="wt_inv")
+        nc.vector.reciprocal(wt_inv[:], wt_safe[:])
+
+        pairs = [keep.tile([P, T, 2], BF16, name=f"pairs{u}") for u in range(2)]
+        picked = [keep.tile([P, 2, N], U32, name=f"picked{b}") for b in range(B)]
+        wi_bf = [keep.tile([P, D, PACK], BF16, name=f"wi_bf{b}", align_bytes=64) for b in range(B)]
+        wd_bf = [keep.tile([P, N, PACK], BF16, name=f"wd_bf{b}", align_bytes=64) for b in range(B)]
+        z_bf = [keep.tile([P, R, PACK], BF16, name=f"z_bf{b}", align_bytes=64) for b in range(B)]
+        wi_codes = [keep.tile([P, D], U32, name=f"wi_codes{b}", align_bytes=64) for b in range(B)]
+        wi_scales = [keep.tile([P, D], U8, name=f"wi_scales{b}", align_bytes=64) for b in range(B)]
+        wd_codes = [keep.tile([P, N], U32, name=f"wd_codes{b}", align_bytes=64) for b in range(B)]
+        wd_scales = [keep.tile([P, N], U8, name=f"wd_scales{b}", align_bytes=64) for b in range(B)]
+        z_codes = [keep.tile([P, R], U32, name=f"z_codes{b}", align_bytes=64) for b in range(B)]
+        z_scales = [keep.tile([P, R], U8, name=f"z_scales{b}", align_bytes=64) for b in range(B)]
+
+        def cast_piece(n):
+            u, c0, width, engine = W_PIECES[n]
+            dst = pairs[u][:, c0 : c0 + width, :]
+            src = w_raw[n][:].rearrange("p e c -> p c e")
+            if engine == "scalar":
+                nc.scalar.activation(dst, src, ACT.Copy)
+            else:
+                nc.vector.tensor_copy(out=dst, in_=src)
+
+        def gather(b, u):
+            window = pairs[u][:].rearrange("p c e -> p (c e)").bitcast(U32)
+            nc.vector.tensor_copy(picked[b][:, u, :], window.indirect(offsets[:, b * LIST_COLS : (b + 1) * LIST_COLS]))
+
+        def turn(b, u):
+            bank = psum.tile([P, PACK, P], F32, name="w_bank", tag="res")
+            words = picked[b][:, u, :].bitcast(F32)
+            for s in range(PACK):
+                nc.tensor.transpose(bank[:, s, :], words[:, s:N:PACK], ident[:])
+            src = bank[:].rearrange("m s p -> m (s p)").bitcast(BF16).rearrange("m (s p e) -> m e p s", s=PACK, e=2)
+            dst = wi_bf[b][:, 256 * u : 256 * u + 256, :].rearrange("m (e p) s -> m e p s", e=2)
+            nc.scalar.copy(dst, src)
+
+        def quant_wi(b, u):
+            cols = slice(256 * u, 256 * u + 256)
+            nc.vector.quantize_mx(out=wi_codes[b][:, cols].bitcast(E4M3), scales=wi_scales[b][:, cols],
+                                  in_=wi_bf[b][:, cols, :].rearrange("m c s -> m (c s)"))
+
+        def lay_wd(b):
+            dst = wd_bf[b][:].rearrange("p i t -> p (i t)").bitcast(F32).rearrange("p (i u) -> p i u", u=2)
+            src = picked[b][:].bitcast(F32).rearrange("p u i -> p i u")
+            nc.vector.tensor_copy(out=dst, in_=src)
+
+        def quant_wd(b):
+            nc.vector.quantize_mx(out=wd_codes[b][:].bitcast(E4M3), scales=wd_scales[b][:],
+                                  in_=wd_bf[b][:].rearrange("p i t -> p (i t)"))
+
+        def cast_z(b):
+            dst = z_bf[b][:].rearrange("p (c i) t -> p c t i", i=4)
+            src = z_raw[b][:].rearrange("p t (c i) -> p c t i", i=4)
+            if b == 0:
+                nc.scalar.activation(dst[:, 0:64], src[:, 0:64], ACT.Copy)
+                nc.vector.tensor_copy(out=dst[:, 64:128], in_=src[:, 64:128])
+            else:
+                nc.vector.tensor_copy(out=dst, in_=src)
+
+        def quant_z(b):
+            nc.vector.quantize_mx(out=z_codes[b][:].bitcast(E4M3), scales=z_scales[b][:],
+                                  in_=z_bf[b][:].rearrange("p r t -> p (r t)"))
+
+        st = {}
+
+        def weigh_x(k):
+            b, j = divmod(k, CHUNKS)
+            xw = work.tile([P, PACK, P], F32, name="xw")
+            nc.vector.tensor_scalar(xw[:].rearrange("r t p -> r p t"),
+                                    x_raw[b, j // 2][:, j % 2, :].rearrange("r (p t) -> r p t", t=PACK),
+                                    wt_cols[:, k : k + 1], None, ALU.mult)
+            st["xw", k] = xw
+
+        def rebuild(k):
+            b, j = divmod(k, CHUNKS)
+            rows = slice(P * j, P * j + P)
+            rec = psum.tile([P, D], F32, name="rec")
+            nc.tensor.matmul_mx(out=rec[:], lhsT=z_codes[b][:, rows].bitcast(E4M3), lhsT_scale=z_scales[b][:, rows],
+                                rhs=wi_codes[b][:].bitcast(E4M3), rhs_scale=wi_scales[b][:], start=True, stop=True)
+            st["rec", k] = rec
+
+        def residual(k):
+            wd = work.tile([P, D], F32, name="wd")
+            nc.vector.scalar_tensor_tensor(wd[:], st["rec", k][:], wt_cols[:, k : k + 1],
+                                           st["xw", k][:].rearrange("r t p -> r (t p)"), ALU.mult, ALU.subtract)
+            st["wd", k] = wd
+
+        def square(k):
+            sq = work.tile([P, D], F32, name="sq")
+            nc.scalar.activation(sq[:], st["wd", k][:], ACT.Square, scale=wt_inv[:, k : k + 1])
+            st["sq", k] = sq
+
+        def turn_chunk(kind, k):
+            bank = psum.tile([P, PACK, P], F32, name=kind + "_bank")
+            for t in range(PACK):
+                nc.tensor.transpose(bank[:, t, :], st[kind, k][:, P * t : P * t + P], ident[:])
+            st[kind + "T", k] = bank
+
+        def root(k):
+            s = work.tile([P, PACK, P], F32, name="s")
+            for t in range(PACK):
+                nc.scalar.activation(s[:, t, :], st["sqT", k][:, t, :], ACT.Abs_reciprocal_sqrt, bias=noise_sq[:, t : t + 1])
+            st["s", k] = s
+
+        def half(k):
+            h = work.tile([P, PACK, P], F32, name="h")
+            if k in SCALAR_SQUARES:
+                nc.scalar.activation(h[:], st["s", k][:], ACT.Square)
+                st["last", k] = st["wdT", k]
+            else:
+                nc.vector.tensor_tensor(h[:], st["wdT", k][:], st["s", k][:], ALU.mult)
+                st["last", k] = st["s", k]
+            st["h", k] = h
+
+        def whole(k):
+            e = work.tile([P, P, PACK], BF16, name="e", align_bytes=64)
+            nc.vector.tensor_tensor(e[:].rearrange("p (c i) t -> p c t i", i=4),
+                                    st["last", k][:].rearrange("p t (c i) -> p c t i", i=4),
+                                    st["h", k][:].rearrange("p t (c i) -> p c t i", i=4), ALU.mult)
+            st["e", k] = e
+
+        def quant_e(k):
+            codes = work.tile([P, P], U32, name="e_codes", align_bytes=64)
+            scales = work.tile([P, P], U8, name="e_scales", align_bytes=64)
+            nc.vector.quantize_mx(out=codes[:].bitcast(E5M2), scales=scales[:], in_=st["e", k][:].rearrange("p r t -> p (r t)"))
+            st["eq", k] = (codes, scales)
+
+        def project(k):
+            b = k // CHUNKS
+            codes, scales = st["eq", k]
+            res = psum.tile([P, PACK, P], F32, name="res", tag="res")
+            nc.tensor.matmul_mx(out=res[:].rearrange("r a c -> r (a c)"), lhsT=codes[:].bitcast(E5M2), lhsT_scale=scales[:],
+                                rhs=wd_codes[b][:].bitcast(E4M3), rhs_scale=wd_scales[b][:], start=True, stop=True)
+            st["res", k] = res
+
+        def emit(k):
+            b, j = divmod(k, CHUNKS)
+            staged = work.tile([P, N], F32, name="staged")
+            nc.scalar.copy(staged[:], st["res", k][:].rearrange("r a c -> r (a c)"))
+            nc.sync.dma_start(out=out[b, P * j : P * j + P, :], in_=staged[:])
+
+        cast_piece(0)
+        cast_piece(1)
+        gather(0, 0)
+        turn(0, 0)
+        gather(1, 0)
+        cast_piece(2)
+        cast_piece(3)
+        cast_piece(4)
+        gather(0, 1)
+        turn(0, 1)
+        quant_wi(0, 0)
+        cast_z(0)
+        gather(1, 1)
+        quant_z(0)
+        quant_wi(0, 1)
+        weigh_x(0)
+
+        extras = {
+            0: [lambda: lay_wd(0), lambda: turn(1, 0)],
+            1: [lambda: quant_wd(0), lambda: turn(1, 1), lambda: cast_z(1)],
+            2: [lambda: quant_wi(1, 0), lambda: quant_wi(1, 1), lambda: quant_z(1)],
+            4: [lambda: lay_wd(1)],
+            5: [lambda: quant_wd(1)],
+        }
+        total = B * CHUNKS
+        rebuild(0)
+        for step in range(total + 4):
+            def live(k):
+                return 0 <= k < total
+            if live(step):
+                residual(step)
+            if live(step + 1):
+                weigh_x(step + 1)
+            if live(step - 4):
+                emit(step - 4)
+            if live(step):
+                square(step)
+            if live(step - 1):
+                root(step - 1)
+            if live(step - 2):
+                half(step - 2)
+            for extra in extras.get(step, []):
+                extra()
+            if live(step - 3):
+                quant_e(step - 3)
+            if live(step - 2):
+                whole(step - 2)
+            if live(step):
+                turn_chunk("sq", step)
+            if live(step - 1):
+                turn_chunk("wd", step - 1)
+            if live(step + 1):
+                rebuild(step + 1)
+            if live(step - 3):
+                project(step - 3)

@@ -20,7 +20,7 @@ P = 128
 PACK = 4
 CHUNKS = R // P
 LIST_COLS = N // 16
-SCALAR_SQUARES = (0, 2, 4, 5)
+SCALAR_SQUARES = (0, 1, 2, 4, 5, 7)
 W_PIECES = [(0, 0, 1024, "scalar"), (0, 1024, 1024, "vector"), (1, 0, 1024, "scalar"), (1, 1024, 512, "vector"), (1, 1536, 512, "vector")]
 
 
@@ -35,12 +35,12 @@ def tile_attend_gdi_cau_z_kernel(tc, zT, wT, xm, wt, cs, offs, out):
         nc.sync.dma_start(offsets[:], offs)
 
         wt_rows = keep.tile([P, P], F32, name="wt_rows")
-        nc.gpsimd.memset(wt_rows[:], 0.0)
+        nc.vector.memset(wt_rows[:], 0.0)
         ident = keep.tile([P, P], F32, name="ident")
         make_identity(nc, ident[:])
         c_cols = keep.tile([P, PACK], F32, name="c_cols")
-        nc.scalar.dma_start(out=c_cols[:], in_=cs[0, :].rearrange("(p t) -> p t", t=PACK))
-        nc.scalar.dma_start(out=wt_rows[0 : B * CHUNKS, :], in_=wt.rearrange("b (j p) o -> (b j) (p o)", p=P))
+        nc.sync.dma_start(out=c_cols[:], in_=cs[0, :].rearrange("(p t) -> p t", t=PACK))
+        nc.sync.dma_start(out=wt_rows[0 : B * CHUNKS, :], in_=wt.rearrange("b (j p) o -> (b j) (p o)", p=P))
         warm = keep.tile([P, 1], F32, name="warm")
         nc.scalar.activation(warm[:], ident[:, 0:1], ACT.Abs_reciprocal_sqrt, bias=1.0)
 
@@ -59,18 +59,43 @@ def tile_attend_gdi_cau_z_kernel(tc, zT, wT, xm, wt, cs, offs, out):
                 x_raw[b, h] = keep.tile([P, 2, D], F32, name=f"x_raw{b}{h}")
                 nc.sync.dma_start(out=x_raw[b, h][:], in_=xm[b, 256 * h : 256 * h + 256, :].rearrange("(j p) d -> p j d", p=P))
 
-        wt_ps = psum.tile([P, PACK, P], F32, name="wt_ps", tag="res")
-        nc.tensor.transpose(wt_ps[:, 0, :], wt_rows[:], ident[:])
-        wt_cols = keep.tile([P, B * CHUNKS], F32, name="wt_cols")
-        nc.vector.tensor_copy(out=wt_cols[:], in_=wt_ps[:, 0, 0 : B * CHUNKS])
+        total = B * CHUNKS
         c_sq = keep.tile([P, PACK], F32, name="c_sq")
         nc.vector.tensor_tensor(c_sq[:], c_cols[:], c_cols[:], ALU.mult)
-        wt_safe = keep.tile([P, B * CHUNKS], F32, name="wt_safe")
-        nc.vector.scalar_tensor_tensor(wt_safe[:], wt_cols[:], 0.0, wt_cols[:], ALU.is_equal, ALU.add)
         noise_sq = keep.tile([P, PACK], F32, name="noise_sq")
         nc.vector.reciprocal(noise_sq[:], c_sq[:])
-        wt_inv = keep.tile([P, B * CHUNKS], F32, name="wt_inv")
-        nc.vector.reciprocal(wt_inv[:], wt_safe[:])
+        wt_ps = psum.tile([P, PACK, P], F32, name="wt_ps", tag="res")
+        nc.tensor.transpose(wt_ps[:, 0, :], wt_rows[:], ident[:])
+        noise_ps = psum.tile([P, PACK, P], F32, name="noise_ps", tag="res")
+        for t in range(PACK):
+            nc.tensor.transpose(noise_ps[:, t, :], noise_sq[:, t : t + 1].to_broadcast([P, P]), ident[:])
+        wt_cols = keep.tile([P, total], F32, name="wt_cols")
+        nc.vector.tensor_copy(out=wt_cols[:], in_=wt_ps[:, 0, 0:total])
+        wt_sign = keep.tile([P, total], F32, name="wt_sign")
+        nc.scalar.activation(wt_sign[:], wt_cols[:], ACT.Sign)
+        wt_safe = keep.tile([P, total], F32, name="wt_safe")
+        nc.vector.scalar_tensor_tensor(wt_safe[:], wt_cols[:], 0.0, wt_cols[:], ALU.is_equal, ALU.add)
+        wt_abs = keep.tile([P, total], F32, name="wt_abs")
+        nc.scalar.activation(wt_abs[:], wt_safe[:], ACT.Abs)
+        seed = keep.tile([P, total], F32, name="seed")
+        nc.scalar.activation(seed[:], wt_safe[:], ACT.Abs_reciprocal_sqrt)
+        noise_rows = keep.tile([P, D], F32, name="noise_rows")
+        nc.vector.tensor_copy(out=noise_rows[:], in_=noise_ps[:].rearrange("r t p -> r (t p)"))
+        seed_sq = keep.tile([P, total], F32, name="seed_sq")
+        nc.vector.tensor_tensor(seed_sq[:], seed[:], seed[:], ALU.mult)
+        gap = keep.tile([P, total], F32, name="gap")
+        nc.vector.scalar_tensor_tensor(gap[:], seed_sq[:], -0.5, wt_abs[:], ALU.mult, ALU.mult)
+        wt_rsqrt = keep.tile([P, total], F32, name="wt_rsqrt")
+        nc.vector.scalar_tensor_tensor(wt_rsqrt[:], gap[:], 1.5, seed[:], ALU.add, ALU.mult)
+        wt_inv = keep.tile([P, total], F32, name="wt_inv")
+        nc.vector.tensor_tensor(wt_inv[:], wt_rsqrt[:], wt_rsqrt[:], ALU.mult)
+        floors = [keep.tile([P, D], F32, name=f"floor{k}") for k in range(total)]
+
+        def make_floor(k, engine):
+            if engine == "scalar":
+                nc.scalar.activation(floors[k][:], noise_rows[:], ACT.Copy, scale=wt_inv[:, k : k + 1])
+            else:
+                nc.vector.tensor_scalar(floors[k][:], noise_rows[:], wt_inv[:, k : k + 1], None, ALU.mult)
 
         pairs = [keep.tile([P, T, 2], BF16, name=f"pairs{u}") for u in range(2)]
         picked = [keep.tile([P, 2, N], U32, name=f"picked{b}") for b in range(B)]
@@ -135,14 +160,6 @@ def tile_attend_gdi_cau_z_kernel(tc, zT, wT, xm, wt, cs, offs, out):
 
         st = {}
 
-        def weigh_x(k):
-            b, j = divmod(k, CHUNKS)
-            xw = work.tile([P, PACK, P], F32, name="xw")
-            nc.vector.tensor_scalar(xw[:].rearrange("r t p -> r p t"),
-                                    x_raw[b, j // 2][:, j % 2, :].rearrange("r (p t) -> r p t", t=PACK),
-                                    wt_cols[:, k : k + 1], None, ALU.mult)
-            st["xw", k] = xw
-
         def rebuild(k):
             b, j = divmod(k, CHUNKS)
             rows = slice(P * j, P * j + P)
@@ -152,26 +169,32 @@ def tile_attend_gdi_cau_z_kernel(tc, zT, wT, xm, wt, cs, offs, out):
             st["rec", k] = rec
 
         def residual(k):
+            b, j = divmod(k, CHUNKS)
             wd = work.tile([P, D], F32, name="wd")
-            nc.vector.scalar_tensor_tensor(wd[:], st["rec", k][:], wt_cols[:, k : k + 1],
-                                           st["xw", k][:].rearrange("r t p -> r (t p)"), ALU.mult, ALU.subtract)
+            nc.vector.tensor_tensor(wd[:].rearrange("r (t p) -> r p t", t=PACK), st["rec", k][:].rearrange("r (t p) -> r p t", t=PACK),
+                                    x_raw[b, j // 2][:, j % 2, :].rearrange("r (p t) -> r p t", t=PACK), ALU.subtract)
             st["wd", k] = wd
 
         def square(k):
             sq = work.tile([P, D], F32, name="sq")
-            nc.scalar.activation(sq[:], st["wd", k][:], ACT.Square, scale=wt_inv[:, k : k + 1])
+            nc.scalar.activation(sq[:], st["wd", k][:], ACT.Square, scale=wt_rsqrt[:, k : k + 1])
             st["sq", k] = sq
 
         def turn_chunk(kind, k):
             bank = psum.tile([P, PACK, P], F32, name=kind + "_bank")
-            for t in range(PACK):
-                nc.tensor.transpose(bank[:, t, :], st[kind, k][:, P * t : P * t + P], ident[:])
+            if kind == "sq":
+                for t in range(PACK):
+                    nc.tensor.matmul(bank[:, t, :], floors[k][:, P * t : P * t + P], ident[:], start=(t == 0), stop=False, is_transpose=True)
+                for t in range(PACK):
+                    nc.tensor.matmul(bank[:, t, :], st[kind, k][:, P * t : P * t + P], ident[:], start=False, stop=(t == PACK - 1), is_transpose=True)
+            else:
+                for t in range(PACK):
+                    nc.tensor.transpose(bank[:, t, :], st[kind, k][:, P * t : P * t + P], ident[:])
             st[kind + "T", k] = bank
 
         def root(k):
             s = work.tile([P, PACK, P], F32, name="s")
-            for t in range(PACK):
-                nc.scalar.activation(s[:, t, :], st["sqT", k][:, t, :], ACT.Abs_reciprocal_sqrt, bias=noise_sq[:, t : t + 1])
+            nc.scalar.activation(s[:], st["sqT", k][:], ACT.Abs_reciprocal_sqrt)
             st["s", k] = s
 
         def half(k):
@@ -208,10 +231,12 @@ def tile_attend_gdi_cau_z_kernel(tc, zT, wT, xm, wt, cs, offs, out):
         def emit(k):
             b, j = divmod(k, CHUNKS)
             staged = work.tile([P, N], F32, name="staged")
-            nc.scalar.copy(staged[:], st["res", k][:].rearrange("r a c -> r (a c)"))
+            nc.scalar.activation(staged[:], st["res", k][:].rearrange("r a c -> r (a c)"), ACT.Copy, scale=wt_sign[:, k : k + 1])
             nc.sync.dma_start(out=out[b, P * j : P * j + P, :], in_=staged[:])
 
         cast_piece(0)
+        for k in range(total):
+            make_floor(k, "vector")
         cast_piece(1)
         gather(0, 0)
         turn(0, 0)
@@ -226,7 +251,6 @@ def tile_attend_gdi_cau_z_kernel(tc, zT, wT, xm, wt, cs, offs, out):
         gather(1, 1)
         quant_z(0)
         quant_wi(0, 1)
-        weigh_x(0)
 
         extras = {
             0: [lambda: lay_wd(0), lambda: turn(1, 0)],
@@ -235,15 +259,12 @@ def tile_attend_gdi_cau_z_kernel(tc, zT, wT, xm, wt, cs, offs, out):
             4: [lambda: lay_wd(1)],
             5: [lambda: quant_wd(1)],
         }
-        total = B * CHUNKS
         rebuild(0)
         for step in range(total + 4):
             def live(k):
                 return 0 <= k < total
             if live(step):
                 residual(step)
-            if live(step + 1):
-                weigh_x(step + 1)
             if live(step - 4):
                 emit(step - 4)
             if live(step):

@@ -19,271 +19,257 @@ ACT = mybir.ActivationFunctionType
 P = 128
 PACK = 4
 CHUNKS = R // P
+LAST_CHUNK = B * CHUNKS - 1
 LIST_COLS = N // 16
-SCALAR_SQUARES = (0, 1, 2, 4, 5, 7)
-W_PIECES = [(0, 0, 1024, "scalar"), (0, 1024, 1024, "vector"), (1, 0, 1024, "scalar"), (1, 1024, 512, "vector"), (1, 1536, 512, "vector")]
+PIECE = 512
+PIECES_A_PAIR = T // PIECE
+HALF = 256
+WT_RUN = B * R // P
+RING = 16
+BANKS = 8
+SMALLEST_SQUARE = 2.0**-120
+VEC, SCA = "vector", "scalar"
 
 
 def tile_attend_gdi_cau_z_kernel(tc, zT, wT, xm, wt, cs, offs, out):
     nc = tc.nc
     with ExitStack() as ctx:
         keep = ctx.enter_context(tc.tile_pool(name="keep", bufs=1))
-        work = ctx.enter_context(tc.tile_pool(name="work", bufs=3))
-        psum = ctx.enter_context(tc.psum_pool(name="psum", bufs=2))
+        work = ctx.enter_context(tc.tile_pool(name="work", bufs=RING))
+        psum = ctx.enter_context(tc.psum_pool(name="psum", bufs=BANKS))
 
-        offsets = keep.tile([P, B * LIST_COLS], U16, name="offsets")
-        nc.sync.dma_start(offsets[:], offs)
+        def ring(engine, shape, dtype, name):
+            return work.tile(shape, dtype, name=name, tag=engine, align_bytes=64)
 
-        wt_rows = keep.tile([P, P], F32, name="wt_rows")
-        nc.vector.memset(wt_rows[:], 0.0)
-        ident = keep.tile([P, P], F32, name="ident")
-        make_identity(nc, ident[:])
-        c_cols = keep.tile([P, PACK], F32, name="c_cols")
-        nc.sync.dma_start(out=c_cols[:], in_=cs[0, :].rearrange("(p t) -> p t", t=PACK))
-        nc.sync.dma_start(out=wt_rows[0 : B * CHUNKS, :], in_=wt.rearrange("b (j p) o -> (b j) (p o)", p=P))
-        warm = keep.tile([P, 1], F32, name="warm")
-        nc.scalar.activation(warm[:], ident[:, 0:1], ACT.Abs_reciprocal_sqrt, bias=1.0)
+        def bank_tile(name):
+            return psum.tile([P, PACK, P], F32, name=name, tag="bank")
 
-        w_planes = wT.rearrange("(p t) c -> p t c", t=PACK)
-        w_raw = []
-        for n, (u, c0, width, engine) in enumerate(W_PIECES):
-            raw = keep.tile([P, 2, width], F32, name=f"w_raw{n}")
-            nc.sync.dma_start(out=raw[:], in_=w_planes[:, 2 * u : 2 * u + 2, c0 : c0 + width])
-            w_raw.append(raw)
-        z_raw = {}
-        x_raw = {}
-        for b in range(B):
-            z_raw[b] = keep.tile([P, PACK, R], F32, name=f"z_raw{b}")
-            nc.sync.dma_start(out=z_raw[b][:], in_=zT[b].rearrange("(p t) r -> p t r", t=PACK))
-            for h in range(2):
-                x_raw[b, h] = keep.tile([P, 2, D], F32, name=f"x_raw{b}{h}")
-                nc.sync.dma_start(out=x_raw[b, h][:], in_=xm[b, 256 * h : 256 * h + 256, :].rearrange("(j p) d -> p j d", p=P))
-
-        total = B * CHUNKS
-        c_sq = keep.tile([P, PACK], F32, name="c_sq")
-        nc.vector.tensor_tensor(c_sq[:], c_cols[:], c_cols[:], ALU.mult)
-        noise_sq = keep.tile([P, PACK], F32, name="noise_sq")
-        nc.vector.reciprocal(noise_sq[:], c_sq[:])
-        wt_ps = psum.tile([P, PACK, P], F32, name="wt_ps", tag="res")
-        nc.tensor.transpose(wt_ps[:, 0, :], wt_rows[:], ident[:])
-        noise_ps = psum.tile([P, PACK, P], F32, name="noise_ps", tag="res")
-        for t in range(PACK):
-            nc.tensor.transpose(noise_ps[:, t, :], noise_sq[:, t : t + 1].to_broadcast([P, P]), ident[:])
-        wt_cols = keep.tile([P, total], F32, name="wt_cols")
-        nc.vector.tensor_copy(out=wt_cols[:], in_=wt_ps[:, 0, 0:total])
-        wt_sign = keep.tile([P, total], F32, name="wt_sign")
-        nc.scalar.activation(wt_sign[:], wt_cols[:], ACT.Sign)
-        wt_safe = keep.tile([P, total], F32, name="wt_safe")
-        nc.vector.scalar_tensor_tensor(wt_safe[:], wt_cols[:], 0.0, wt_cols[:], ALU.is_equal, ALU.add)
-        wt_abs = keep.tile([P, total], F32, name="wt_abs")
-        nc.scalar.activation(wt_abs[:], wt_safe[:], ACT.Abs)
-        seed = keep.tile([P, total], F32, name="seed")
-        nc.scalar.activation(seed[:], wt_safe[:], ACT.Abs_reciprocal_sqrt)
-        noise_rows = keep.tile([P, D], F32, name="noise_rows")
-        nc.vector.tensor_copy(out=noise_rows[:], in_=noise_ps[:].rearrange("r t p -> r (t p)"))
-        seed_sq = keep.tile([P, total], F32, name="seed_sq")
-        nc.vector.tensor_tensor(seed_sq[:], seed[:], seed[:], ALU.mult)
-        gap = keep.tile([P, total], F32, name="gap")
-        nc.vector.scalar_tensor_tensor(gap[:], seed_sq[:], -0.5, wt_abs[:], ALU.mult, ALU.mult)
-        wt_rsqrt = keep.tile([P, total], F32, name="wt_rsqrt")
-        nc.vector.scalar_tensor_tensor(wt_rsqrt[:], gap[:], 1.5, seed[:], ALU.add, ALU.mult)
-        wt_inv = keep.tile([P, total], F32, name="wt_inv")
-        nc.vector.tensor_tensor(wt_inv[:], wt_rsqrt[:], wt_rsqrt[:], ALU.mult)
-        floors = [keep.tile([P, D], F32, name=f"floor{k}") for k in range(total)]
-
-        def make_floor(k, engine):
-            if engine == "scalar":
-                nc.scalar.activation(floors[k][:], noise_rows[:], ACT.Copy, scale=wt_inv[:, k : k + 1])
+        def move(engine, dst, src):
+            if engine == SCA:
+                nc.scalar.copy(dst, src)
             else:
-                nc.vector.tensor_scalar(floors[k][:], noise_rows[:], wt_inv[:, k : k + 1], None, ALU.mult)
+                nc.vector.tensor_copy(out=dst, in_=src)
 
-        pairs = [keep.tile([P, T, 2], BF16, name=f"pairs{u}") for u in range(2)]
-        picked = [keep.tile([P, 2, N], U32, name=f"picked{b}") for b in range(B)]
-        wi_bf = [keep.tile([P, D, PACK], BF16, name=f"wi_bf{b}", align_bytes=64) for b in range(B)]
-        wd_bf = [keep.tile([P, N, PACK], BF16, name=f"wd_bf{b}", align_bytes=64) for b in range(B)]
-        z_bf = [keep.tile([P, R, PACK], BF16, name=f"z_bf{b}", align_bytes=64) for b in range(B)]
-        wi_codes = [keep.tile([P, D], U32, name=f"wi_codes{b}", align_bytes=64) for b in range(B)]
-        wi_scales = [keep.tile([P, D], U8, name=f"wi_scales{b}", align_bytes=64) for b in range(B)]
-        wd_codes = [keep.tile([P, N], U32, name=f"wd_codes{b}", align_bytes=64) for b in range(B)]
-        wd_scales = [keep.tile([P, N], U8, name=f"wd_scales{b}", align_bytes=64) for b in range(B)]
-        z_codes = [keep.tile([P, R], U32, name=f"z_codes{b}", align_bytes=64) for b in range(B)]
-        z_scales = [keep.tile([P, R], U8, name=f"z_scales{b}", align_bytes=64) for b in range(B)]
-
-        def cast_piece(n):
-            u, c0, width, engine = W_PIECES[n]
-            dst = pairs[u][:, c0 : c0 + width, :]
-            src = w_raw[n][:].rearrange("p e c -> p c e")
-            if engine == "scalar":
+        def round_to_bf16(engine, dst, src):
+            if engine == SCA:
                 nc.scalar.activation(dst, src, ACT.Copy)
             else:
                 nc.vector.tensor_copy(out=dst, in_=src)
+
+        offsets = keep.tile([P, B * LIST_COLS], U16, name="offsets")
+        nc.sync.dma_start(offsets[:], offs)
+        wt_flat = keep.tile([P, WT_RUN], F32, name="wt_flat")
+        ident = keep.tile([P, P], F32, name="ident")
+        make_identity(nc, ident[:])
+        c_cols = keep.tile([P, PACK], F32, name="c_cols")
+        nc.scalar.dma_start(out=c_cols[:], in_=cs[0, :].rearrange("(p t) -> p t", t=PACK))
+        nc.scalar.dma_start(out=wt_flat[:], in_=wt.rearrange("b (q c) o -> (b q) (c o)", c=WT_RUN))
+
+        w_planes = wT.rearrange("(p t) c -> p t c", t=PACK)
+        w_raw = {}
+        z_raw = {}
+        x_raw = {}
+
+        def load_table(n, stage):
+            u, piece = divmod(n, PIECES_A_PAIR)
+            w_raw[n] = keep.tile([P, 2, PIECE], F32, name=f"w_raw{n}", tag=f"stage{stage}", align_bytes=64)
+            nc.sync.dma_start(out=w_raw[n][:], in_=w_planes[:, 2 * u : 2 * u + 2, PIECE * piece : PIECE * (piece + 1)])
+
+        def load_coefficients(b, stage):
+            z_raw[b] = keep.tile([P, PACK, R], F32, name=f"z_raw{b}", tag=f"stage{stage}", align_bytes=64)
+            nc.sync.dma_start(out=z_raw[b][:], in_=zT[b].rearrange("(p t) r -> p t r", t=PACK))
+
+        def load_targets(b, h, stage):
+            x_raw[b, h] = keep.tile([P, 2, D], F32, name=f"x_raw{b}{h}", tag=f"stage{stage}", align_bytes=64)
+            nc.sync.dma_start(out=x_raw[b, h][:], in_=xm[b, HALF * h : HALF * (h + 1), :].rearrange("(j p) d -> p j d", p=P))
+
+        last_piece = 2 * PIECES_A_PAIR - 1
+        for n in range(last_piece):
+            load_table(n, n)
+
+        c_sq = keep.tile([P, PACK], F32, name="c_sq")
+        nc.gpsimd.tensor_tensor(c_sq[:], c_cols[:], c_cols[:], ALU.mult)
+        c_safe = keep.tile([P, PACK], F32, name="c_safe")
+        nc.gpsimd.tensor_scalar(c_safe[:], c_sq[:], SMALLEST_SQUARE, None, ALU.max)
+        seed = keep.tile([P, PACK], F32, name="seed", tag="first", bufs=2)
+        nc.scalar.activation(seed[:], c_safe[:], ACT.Abs_reciprocal_sqrt)
+        seed_sq = keep.tile([P, PACK], F32, name="seed_sq")
+        nc.gpsimd.tensor_tensor(seed_sq[:], seed[:], seed[:], ALU.mult)
+        near_one = keep.tile([P, PACK], F32, name="near_one")
+        nc.gpsimd.tensor_tensor(near_one[:], seed_sq[:], c_safe[:], ALU.mult)
+        newton = keep.tile([P, PACK], F32, name="newton")
+        nc.gpsimd.tensor_scalar(newton[:], near_one[:], -0.5, 1.5, ALU.mult, ALU.add)
+        noise = keep.tile([P, PACK], F32, name="noise")
+        nc.gpsimd.tensor_tensor(noise[:], newton[:], seed[:], ALU.mult)
+        noise_sq = keep.tile([P, PACK], F32, name="noise_sq")
+        nc.gpsimd.tensor_tensor(noise_sq[:], noise[:], noise[:], ALU.mult)
+
+        wt_wide = keep.tile([P, B * R], F32, name="wt_wide", tag="first", bufs=2)
+        for c0 in range(0, WT_RUN, PACK):
+            wide_bank = bank_tile("wide_bank")
+            for c in range(PACK):
+                nc.tensor.transpose(wide_bank[:, c, :], wt_flat[:, c0 + c : c0 + c + 1].to_broadcast([P, P]), ident[:])
+            nc.scalar.copy(wt_wide[:].rearrange("p (q c) -> p q c", c=WT_RUN)[:, :, c0 : c0 + PACK],
+                           wide_bank[:].rearrange("p c q -> p q c"))
+
+        pairs = [keep.tile([P, T, 2], BF16, name=f"pairs{u}", align_bytes=64) for u in range(2)]
+        picked = [keep.tile([P, 2, N], U32, name=f"picked{b}") for b in range(B)]
+        by_feature = [keep.tile([P, N, PACK], BF16, name=f"by_feature{b}", align_bytes=64) for b in range(B)]
+        slot_codes = [keep.tile([P, D], U32, name=f"slot_codes{b}", align_bytes=64) for b in range(B)]
+        slot_scales = [keep.tile([P, D], U8, name=f"slot_scales{b}", align_bytes=64) for b in range(B)]
+        feature_codes = [keep.tile([P, N], U32, name=f"feature_codes{b}", align_bytes=64) for b in range(B)]
+        feature_scales = [keep.tile([P, N], U8, name=f"feature_scales{b}", align_bytes=64) for b in range(B)]
+        z_codes = [keep.tile([P, R], U32, name=f"z_codes{b}", align_bytes=64) for b in range(B)]
+        z_scales = [keep.tile([P, R], U8, name=f"z_scales{b}", align_bytes=64) for b in range(B)]
+        made = {}
+
+        def round_table(n, engine):
+            u, piece = divmod(n, PIECES_A_PAIR)
+            round_to_bf16(engine, pairs[u][:, PIECE * piece : PIECE * (piece + 1), :], w_raw[n][:].rearrange("p e c -> p c e"))
 
         def gather(b, u):
             window = pairs[u][:].rearrange("p c e -> p (c e)").bitcast(U32)
             nc.vector.tensor_copy(picked[b][:, u, :], window.indirect(offsets[:, b * LIST_COLS : (b + 1) * LIST_COLS]))
 
-        def turn(b, u):
-            bank = psum.tile([P, PACK, P], F32, name="w_bank", tag="res")
+        def turn_atoms(b, u, engine):
+            bank = bank_tile("atom_bank")
             words = picked[b][:, u, :].bitcast(F32)
             for s in range(PACK):
                 nc.tensor.transpose(bank[:, s, :], words[:, s:N:PACK], ident[:])
             src = bank[:].rearrange("m s p -> m (s p)").bitcast(BF16).rearrange("m (s p e) -> m e p s", s=PACK, e=2)
-            dst = wi_bf[b][:, 256 * u : 256 * u + 256, :].rearrange("m (e p) s -> m e p s", e=2)
-            nc.scalar.copy(dst, src)
+            made["by_slot", b, u] = ring(engine, [P, HALF, PACK], BF16, "by_slot")
+            move(engine, made["by_slot", b, u][:].rearrange("m (e p) s -> m e p s", e=2), src)
 
-        def quant_wi(b, u):
-            cols = slice(256 * u, 256 * u + 256)
-            nc.vector.quantize_mx(out=wi_codes[b][:, cols].bitcast(E4M3), scales=wi_scales[b][:, cols],
-                                  in_=wi_bf[b][:, cols, :].rearrange("m c s -> m (c s)"))
+        def quantise_by_slot(b, u):
+            cols = slice(HALF * u, HALF * (u + 1))
+            nc.vector.quantize_mx(out=slot_codes[b][:, cols].bitcast(E4M3), scales=slot_scales[b][:, cols],
+                                  in_=made["by_slot", b, u][:].rearrange("m c s -> m (c s)"))
 
-        def lay_wd(b):
-            dst = wd_bf[b][:].rearrange("p i t -> p (i t)").bitcast(F32).rearrange("p (i u) -> p i u", u=2)
-            src = picked[b][:].bitcast(F32).rearrange("p u i -> p i u")
-            nc.vector.tensor_copy(out=dst, in_=src)
+        def lay_atoms(b, engine):
+            dst = by_feature[b][:].rearrange("p i t -> p (i t)").bitcast(F32).rearrange("p (i u) -> p i u", u=2)
+            move(engine, dst, picked[b][:].bitcast(F32).rearrange("p u i -> p i u"))
 
-        def quant_wd(b):
-            nc.vector.quantize_mx(out=wd_codes[b][:].bitcast(E4M3), scales=wd_scales[b][:],
-                                  in_=wd_bf[b][:].rearrange("p i t -> p (i t)"))
+        def quantise_by_feature(b):
+            nc.vector.quantize_mx(out=feature_codes[b][:].bitcast(E4M3), scales=feature_scales[b][:],
+                                  in_=by_feature[b][:].rearrange("p i t -> p (i t)"))
 
-        def cast_z(b):
-            dst = z_bf[b][:].rearrange("p (c i) t -> p c t i", i=4)
-            src = z_raw[b][:].rearrange("p t (c i) -> p c t i", i=4)
-            if b == 0:
-                nc.scalar.activation(dst[:, 0:64], src[:, 0:64], ACT.Copy)
-                nc.vector.tensor_copy(out=dst[:, 64:128], in_=src[:, 64:128])
-            else:
-                nc.vector.tensor_copy(out=dst, in_=src)
+        def round_coefficients(b, h, engine):
+            made["z_bf", b, h] = ring(engine, [P, HALF, PACK], BF16, "z_bf")
+            runs = HALF // 4
+            round_to_bf16(engine, made["z_bf", b, h][:].rearrange("p (c i) t -> p c t i", i=4),
+                          z_raw[b][:].rearrange("p t (c i) -> p c t i", i=4)[:, runs * h : runs * (h + 1)])
 
-        def quant_z(b):
-            nc.vector.quantize_mx(out=z_codes[b][:].bitcast(E4M3), scales=z_scales[b][:],
-                                  in_=z_bf[b][:].rearrange("p r t -> p (r t)"))
-
-        st = {}
+        def quantise_coefficients(b, h):
+            cols = slice(HALF * h, HALF * (h + 1))
+            nc.vector.quantize_mx(out=z_codes[b][:, cols].bitcast(E4M3), scales=z_scales[b][:, cols],
+                                  in_=made["z_bf", b, h][:].rearrange("p r t -> p (r t)"))
 
         def rebuild(k):
             b, j = divmod(k, CHUNKS)
-            rows = slice(P * j, P * j + P)
-            rec = psum.tile([P, D], F32, name="rec")
-            nc.tensor.matmul_mx(out=rec[:], lhsT=z_codes[b][:, rows].bitcast(E4M3), lhsT_scale=z_scales[b][:, rows],
-                                rhs=wi_codes[b][:].bitcast(E4M3), rhs_scale=wi_scales[b][:], start=True, stop=True)
-            st["rec", k] = rec
+            rows = slice(P * j, P * (j + 1))
+            made["rec", k] = bank_tile("rec")
+            nc.tensor.matmul_mx(out=made["rec", k][:].rearrange("r t p -> r (t p)"), lhsT=z_codes[b][:, rows].bitcast(E4M3),
+                                lhsT_scale=z_scales[b][:, rows], rhs=slot_codes[b][:].bitcast(E4M3),
+                                rhs_scale=slot_scales[b][:], start=True, stop=True)
 
         def residual(k):
             b, j = divmod(k, CHUNKS)
-            wd = work.tile([P, D], F32, name="wd")
-            nc.vector.tensor_tensor(wd[:].rearrange("r (t p) -> r p t", t=PACK), st["rec", k][:].rearrange("r (t p) -> r p t", t=PACK),
+            made["gap", k] = ring(VEC, [P, D], F32, "gap")
+            nc.vector.tensor_tensor(made["gap", k][:].rearrange("r (t p) -> r p t", t=PACK),
+                                    made["rec", k][:].rearrange("r t p -> r p t"),
                                     x_raw[b, j // 2][:, j % 2, :].rearrange("r (p t) -> r p t", t=PACK), ALU.subtract)
-            st["wd", k] = wd
+
+        def turn_residual(k):
+            made["gap_bank", k] = bank_tile("gap_bank")
+            for t in range(PACK):
+                nc.tensor.transpose(made["gap_bank", k][:, t, :], made["gap", k][:, P * t : P * (t + 1)], ident[:])
 
         def square(k):
-            sq = work.tile([P, D], F32, name="sq")
-            nc.scalar.activation(sq[:], st["wd", k][:], ACT.Square, scale=wt_rsqrt[:, k : k + 1])
-            st["sq", k] = sq
+            made["gap_sq", k] = ring(SCA, [P, PACK, P], F32, "gap_sq")
+            nc.scalar.activation(made["gap_sq", k][:], made["gap_bank", k][:], ACT.Square)
 
-        def turn_chunk(kind, k):
-            bank = psum.tile([P, PACK, P], F32, name=kind + "_bank")
-            if kind == "sq":
-                for t in range(PACK):
-                    nc.tensor.matmul(bank[:, t, :], floors[k][:, P * t : P * t + P], ident[:], start=(t == 0), stop=False, is_transpose=True)
-                for t in range(PACK):
-                    nc.tensor.matmul(bank[:, t, :], st[kind, k][:, P * t : P * t + P], ident[:], start=False, stop=(t == PACK - 1), is_transpose=True)
-            else:
-                for t in range(PACK):
-                    nc.tensor.transpose(bank[:, t, :], st[kind, k][:, P * t : P * t + P], ident[:])
-            st[kind + "T", k] = bank
+        def weigh(k):
+            made["weighed", k] = ring(VEC, [P, PACK, P], F32, "weighed")
+            nc.vector.tensor_tensor(made["weighed", k][:], made["gap_bank", k][:],
+                                    wt_wide[:, P * k : P * (k + 1)].unsqueeze(1).to_broadcast([P, PACK, P]), ALU.mult)
 
         def root(k):
-            s = work.tile([P, PACK, P], F32, name="s")
-            nc.scalar.activation(s[:], st["sqT", k][:], ACT.Abs_reciprocal_sqrt)
-            st["s", k] = s
+            made["root", k] = ring(SCA, [P, PACK, P], F32, "root")
+            for t in range(PACK):
+                nc.scalar.activation(made["root", k][:, t, :], made["gap_sq", k][:, t, :], ACT.Abs_reciprocal_sqrt,
+                                     bias=noise_sq[:, t : t + 1])
 
-        def half(k):
-            h = work.tile([P, PACK, P], F32, name="h")
-            if k in SCALAR_SQUARES:
-                nc.scalar.activation(h[:], st["s", k][:], ACT.Square)
-                st["last", k] = st["wdT", k]
+        def inverse(k, engine):
+            made["inverse", k] = ring(engine, [P, PACK, P], F32, "inverse")
+            if engine == SCA:
+                nc.scalar.activation(made["inverse", k][:], made["root", k][:], ACT.Square)
             else:
-                nc.vector.tensor_tensor(h[:], st["wdT", k][:], st["s", k][:], ALU.mult)
-                st["last", k] = st["s", k]
-            st["h", k] = h
+                nc.vector.tensor_tensor(made["inverse", k][:], made["root", k][:], made["root", k][:], ALU.mult)
 
-        def whole(k):
-            e = work.tile([P, P, PACK], BF16, name="e", align_bytes=64)
-            nc.vector.tensor_tensor(e[:].rearrange("p (c i) t -> p c t i", i=4),
-                                    st["last", k][:].rearrange("p t (c i) -> p c t i", i=4),
-                                    st["h", k][:].rearrange("p t (c i) -> p c t i", i=4), ALU.mult)
-            st["e", k] = e
+        def gradient(k):
+            made["e", k] = ring(VEC, [P, P, PACK], BF16, "e")
+            nc.vector.tensor_tensor(made["e", k][:].rearrange("p (c i) t -> p c t i", i=4),
+                                    made["weighed", k][:].rearrange("p t (c i) -> p c t i", i=4),
+                                    made["inverse", k][:].rearrange("p t (c i) -> p c t i", i=4), ALU.mult)
 
-        def quant_e(k):
-            codes = work.tile([P, P], U32, name="e_codes", align_bytes=64)
-            scales = work.tile([P, P], U8, name="e_scales", align_bytes=64)
-            nc.vector.quantize_mx(out=codes[:].bitcast(E5M2), scales=scales[:], in_=st["e", k][:].rearrange("p r t -> p (r t)"))
-            st["eq", k] = (codes, scales)
+        def quantise_gradient(k):
+            made["e_codes", k] = ring(VEC, [P, P], U32, "e_codes")
+            made["e_scales", k] = work.tile([P, P], U8, name="e_scales", align_bytes=64)
+            nc.vector.quantize_mx(out=made["e_codes", k][:].bitcast(E5M2), scales=made["e_scales", k][:],
+                                  in_=made["e", k][:].rearrange("p r t -> p (r t)"))
 
         def project(k):
             b = k // CHUNKS
-            codes, scales = st["eq", k]
-            res = psum.tile([P, PACK, P], F32, name="res", tag="res")
-            nc.tensor.matmul_mx(out=res[:].rearrange("r a c -> r (a c)"), lhsT=codes[:].bitcast(E5M2), lhsT_scale=scales[:],
-                                rhs=wd_codes[b][:].bitcast(E4M3), rhs_scale=wd_scales[b][:], start=True, stop=True)
-            st["res", k] = res
+            made["sums", k] = bank_tile("sums")
+            nc.tensor.matmul_mx(out=made["sums", k][:].rearrange("r a c -> r (a c)"), lhsT=made["e_codes", k][:].bitcast(E5M2),
+                                lhsT_scale=made["e_scales", k][:], rhs=feature_codes[b][:].bitcast(E4M3),
+                                rhs_scale=feature_scales[b][:], start=True, stop=True)
 
-        def emit(k):
+        def store(k, engine):
             b, j = divmod(k, CHUNKS)
-            staged = work.tile([P, N], F32, name="staged")
-            nc.scalar.activation(staged[:], st["res", k][:].rearrange("r a c -> r (a c)"), ACT.Copy, scale=wt_sign[:, k : k + 1])
-            nc.sync.dma_start(out=out[b, P * j : P * j + P, :], in_=staged[:])
+            staged = ring(engine, [P, N], F32, "staged")
+            sums = made["sums", k][:].rearrange("r a c -> r (a c)")
+            width = N // 2 if k == LAST_CHUNK else N
+            for c0 in range(0, N, width):
+                move(engine, staged[:, c0 : c0 + width], sums[:, c0 : c0 + width])
+                nc.sync.dma_start(out=out[b, P * j : P * (j + 1), c0 : c0 + width], in_=staged[:, c0 : c0 + width])
 
-        cast_piece(0)
-        for k in range(total):
-            make_floor(k, "vector")
-        cast_piece(1)
-        gather(0, 0)
-        turn(0, 0)
-        gather(1, 0)
-        cast_piece(2)
-        cast_piece(3)
-        cast_piece(4)
-        gather(0, 1)
-        turn(0, 1)
-        quant_wi(0, 0)
-        cast_z(0)
-        gather(1, 1)
-        quant_z(0)
-        quant_wi(0, 1)
-
-        extras = {
-            0: [lambda: lay_wd(0), lambda: turn(1, 0)],
-            1: [lambda: quant_wd(0), lambda: turn(1, 1), lambda: cast_z(1)],
-            2: [lambda: quant_wi(1, 0), lambda: quant_wi(1, 1), lambda: quant_z(1)],
-            4: [lambda: lay_wd(1)],
-            5: [lambda: quant_wd(1)],
+        loads_behind = {
+            (round_table, 0): (load_table, last_piece, 0),
+            (round_table, 1): (load_coefficients, 0, 1),
+            (round_table, 2): (load_targets, 0, 0, 2),
+            (round_table, 3): (load_targets, 0, 1, 3),
+            (round_table, last_piece): (load_targets, 1, 0, 0),
+            (rebuild, 0): (load_coefficients, 1, 1),
+            (residual, 1): (load_targets, 1, 1, 2),
         }
-        rebuild(0)
-        for step in range(total + 4):
-            def live(k):
-                return 0 <= k < total
-            if live(step):
-                residual(step)
-            if live(step - 4):
-                emit(step - 4)
-            if live(step):
-                square(step)
-            if live(step - 1):
-                root(step - 1)
-            if live(step - 2):
-                half(step - 2)
-            for extra in extras.get(step, []):
-                extra()
-            if live(step - 3):
-                quant_e(step - 3)
-            if live(step - 2):
-                whole(step - 2)
-            if live(step):
-                turn_chunk("sq", step)
-            if live(step - 1):
-                turn_chunk("wd", step - 1)
-            if live(step + 1):
-                rebuild(step + 1)
-            if live(step - 3):
-                project(step - 3)
+
+        steps = [
+            (round_table, 0, VEC), (round_table, 1, VEC), (round_table, 2, VEC), (round_table, 3, VEC), (gather, 0, 0),
+            (round_table, 4, VEC), (round_coefficients, 0, 1, VEC), (round_table, 5, SCA), (turn_atoms, 0, 0, SCA),
+            (round_table, 6, SCA), (gather, 1, 0), (round_table, 7, VEC), (round_coefficients, 0, 0, VEC), (gather, 0, 1),
+            (gather, 1, 1), (turn_atoms, 1, 0, SCA), (quantise_coefficients, 0, 0), (turn_atoms, 0, 1, SCA),
+            (quantise_by_slot, 0, 0), (quantise_by_slot, 0, 1), (turn_atoms, 1, 1, SCA), (quantise_coefficients, 0, 1),
+            (rebuild, 0), (residual, 0), (rebuild, 1), (residual, 1), (rebuild, 2), (turn_residual, 0),
+            (round_coefficients, 1, 1, VEC), (round_coefficients, 1, 0, SCA), (quantise_coefficients, 1, 0),
+            (turn_residual, 1), (rebuild, 3), (square, 0), (square, 1), (residual, 2), (quantise_by_slot, 1, 0), (root, 0),
+            (lay_atoms, 1, SCA), (residual, 3), (root, 1), (turn_residual, 2), (quantise_by_slot, 1, 1), (rebuild, 4),
+            (inverse, 0, SCA), (rebuild, 5), (quantise_coefficients, 1, 1), (square, 2), (weigh, 0), (inverse, 1, SCA),
+            (turn_residual, 3), (weigh, 1), (residual, 4), (gradient, 0), (rebuild, 6), (turn_residual, 4), (root, 2),
+            (residual, 5), (square, 3), (weigh, 2), (rebuild, 7), (turn_residual, 5), (lay_atoms, 0, SCA), (residual, 6),
+            (square, 4), (inverse, 2, SCA), (quantise_by_feature, 0), (gradient, 1), (turn_residual, 6), (root, 3),
+            (root, 4), (gradient, 2), (inverse, 3, SCA), (quantise_gradient, 0), (quantise_gradient, 1), (weigh, 3),
+            (quantise_gradient, 2), (weigh, 4), (project, 0), (residual, 7), (project, 1), (quantise_by_feature, 1),
+            (square, 5), (store, 0, SCA), (weigh, 5), (gradient, 3), (inverse, 4, SCA), (store, 1, VEC), (root, 5),
+            (inverse, 5, VEC), (quantise_gradient, 3), (turn_residual, 7), (gradient, 4), (gradient, 5), (square, 6),
+            (project, 2), (weigh, 6), (square, 7), (quantise_gradient, 4), (project, 3), (root, 6), (root, 7),
+            (inverse, 6, SCA), (project, 4), (quantise_gradient, 5), (project, 5), (gradient, 6), (weigh, 7),
+            (inverse, 7, SCA), (store, 2, SCA), (quantise_gradient, 6), (gradient, 7), (store, 3, SCA),
+            (quantise_gradient, 7), (store, 4, SCA), (store, 5, SCA), (project, 6), (project, 7), (store, 6, VEC),
+            (store, 7, SCA),
+        ]
+        for step in steps:
+            step[0](*step[1:])
+            if step[:2] in loads_behind:
+                load = loads_behind[step[:2]]
+                load[0](*load[1:])

@@ -19,13 +19,12 @@ ACT = mybir.ActivationFunctionType
 P = 128
 PACK = 4
 CHUNKS = R // P
-LAST_CHUNK = B * CHUNKS - 1
+ALL_CHUNKS = B * CHUNKS
 LIST_COLS = N // 16
-PIECE = 512
-PIECES_A_PAIR = T // PIECE
 HALF = 256
-WT_RUN = B * R // P
-RING = 16
+RING_BUFS = {"vector": 50, "scalar": 20}
+STORES_ON_VECTOR = 4
+UNGATED = (6,)
 BANKS = 8
 SMALLEST_SQUARE = 2.0**-120
 VEC, SCA = "vector", "scalar"
@@ -35,11 +34,11 @@ def tile_attend_gdi_cau_z_kernel(tc, zT, wT, xm, wt, cs, offs, out):
     nc = tc.nc
     with ExitStack() as ctx:
         keep = ctx.enter_context(tc.tile_pool(name="keep", bufs=1))
-        work = ctx.enter_context(tc.tile_pool(name="work", bufs=RING))
+        work = ctx.enter_context(tc.tile_pool(name="work", bufs=1))
         psum = ctx.enter_context(tc.psum_pool(name="psum", bufs=BANKS))
 
         def ring(engine, shape, dtype, name):
-            return work.tile(shape, dtype, name=name, tag=engine, align_bytes=64)
+            return work.tile(shape, dtype, name=name, tag=engine, bufs=RING_BUFS[engine], align_bytes=64)
 
         def bank_tile(name):
             return psum.tile([P, PACK, P], F32, name=name, tag="bank")
@@ -58,119 +57,132 @@ def tile_attend_gdi_cau_z_kernel(tc, zT, wT, xm, wt, cs, offs, out):
 
         offsets = keep.tile([P, B * LIST_COLS], U16, name="offsets")
         nc.sync.dma_start(offsets[:], offs)
-        wt_flat = keep.tile([P, WT_RUN], F32, name="wt_flat")
+        wt_cols = keep.tile([P, ALL_CHUNKS], F32, name="wt_cols")
         ident = keep.tile([P, P], F32, name="ident")
         make_identity(nc, ident[:])
         c_cols = keep.tile([P, PACK], F32, name="c_cols")
         nc.scalar.dma_start(out=c_cols[:], in_=cs[0, :].rearrange("(p t) -> p t", t=PACK))
-        nc.scalar.dma_start(out=wt_flat[:], in_=wt.rearrange("b (q c) o -> (b q) (c o)", c=WT_RUN))
+        nc.scalar.dma_start(out=wt_cols[:].rearrange("m (g j) -> m g j", j=2),
+                            in_=wt.rearrange("b (h m j) o -> m (b h) (j o)", m=P, j=2))
 
         w_planes = wT.rearrange("(p t) c -> p t c", t=PACK)
-        w_raw = {}
+        planes = {}
         z_raw = {}
         x_raw = {}
 
-        def load_table(n, stage):
-            u, piece = divmod(n, PIECES_A_PAIR)
-            w_raw[n] = keep.tile([P, 2, PIECE], F32, name=f"w_raw{n}", tag=f"stage{stage}", align_bytes=64)
-            nc.sync.dma_start(out=w_raw[n][:], in_=w_planes[:, 2 * u : 2 * u + 2, PIECE * piece : PIECE * (piece + 1)])
+        def load_plane(t):
+            planes[t] = keep.tile([P, T], F32, name=f"plane{t}", align_bytes=64)
+            nc.sync.dma_start(out=planes[t][:], in_=w_planes[:, t, :])
 
-        def load_coefficients(b, stage):
-            z_raw[b] = keep.tile([P, PACK, R], F32, name=f"z_raw{b}", tag=f"stage{stage}", align_bytes=64)
-            nc.sync.dma_start(out=z_raw[b][:], in_=zT[b].rearrange("(p t) r -> p t r", t=PACK))
+        def load_coefficients(b, h, halves):
+            raw = keep.tile([P, PACK, halves * HALF], F32, name=f"z_raw{b}{h}", align_bytes=64)
+            nc.sync.dma_start(out=raw[:], in_=zT[b].rearrange("(p t) r -> p t r", t=PACK)[:, :, HALF * h : HALF * (h + halves)])
+            for i in range(halves):
+                z_raw[b, h + i] = raw[:, :, HALF * i : HALF * (i + 1)]
 
-        def load_targets(b, h, stage):
-            x_raw[b, h] = keep.tile([P, 2, D], F32, name=f"x_raw{b}{h}", tag=f"stage{stage}", align_bytes=64)
-            nc.sync.dma_start(out=x_raw[b, h][:], in_=xm[b, HALF * h : HALF * (h + 1), :].rearrange("(j p) d -> p j d", p=P))
+        def load_targets(b, h):
+            x_raw[b, h] = keep.tile([P, 2, D], F32, name=f"x_raw{b}{h}", align_bytes=64)
+            nc.sync.dma_start(out=x_raw[b, h][:], in_=xm[b, HALF * h : HALF * (h + 1), :].rearrange("(p j) d -> p j d", j=2))
 
-        last_piece = 2 * PIECES_A_PAIR - 1
-        for n in range(last_piece):
-            load_table(n, n)
+        for t in range(PACK):
+            load_plane(t)
+        load_coefficients(0, 0, 1)
+        load_targets(0, 0)
+        load_coefficients(0, 1, 1)
+        load_coefficients(1, 0, 2)
+        load_targets(0, 1)
+        load_targets(1, 0)
+        load_targets(1, 1)
 
         c_sq = keep.tile([P, PACK], F32, name="c_sq")
-        nc.gpsimd.tensor_tensor(c_sq[:], c_cols[:], c_cols[:], ALU.mult)
+        nc.vector.tensor_tensor(c_sq[:], c_cols[:], c_cols[:], ALU.mult)
         c_safe = keep.tile([P, PACK], F32, name="c_safe")
-        nc.gpsimd.tensor_scalar(c_safe[:], c_sq[:], SMALLEST_SQUARE, None, ALU.max)
-        seed = keep.tile([P, PACK], F32, name="seed", tag="first", bufs=2)
+        nc.vector.tensor_scalar(c_safe[:], c_sq[:], SMALLEST_SQUARE, None, ALU.max)
+        seed = keep.tile([P, PACK], F32, name="seed")
         nc.scalar.activation(seed[:], c_safe[:], ACT.Abs_reciprocal_sqrt)
         seed_sq = keep.tile([P, PACK], F32, name="seed_sq")
-        nc.gpsimd.tensor_tensor(seed_sq[:], seed[:], seed[:], ALU.mult)
+        nc.vector.tensor_tensor(seed_sq[:], seed[:], seed[:], ALU.mult)
         near_one = keep.tile([P, PACK], F32, name="near_one")
-        nc.gpsimd.tensor_tensor(near_one[:], seed_sq[:], c_safe[:], ALU.mult)
+        nc.vector.tensor_tensor(near_one[:], seed_sq[:], c_safe[:], ALU.mult)
         newton = keep.tile([P, PACK], F32, name="newton")
-        nc.gpsimd.tensor_scalar(newton[:], near_one[:], -0.5, 1.5, ALU.mult, ALU.add)
+        nc.vector.tensor_scalar(newton[:], near_one[:], -0.5, 1.5, ALU.mult, ALU.add)
         noise = keep.tile([P, PACK], F32, name="noise")
-        nc.gpsimd.tensor_tensor(noise[:], newton[:], seed[:], ALU.mult)
+        nc.vector.tensor_tensor(noise[:], newton[:], seed[:], ALU.mult)
         noise_sq = keep.tile([P, PACK], F32, name="noise_sq")
-        nc.gpsimd.tensor_tensor(noise_sq[:], noise[:], noise[:], ALU.mult)
+        nc.vector.tensor_tensor(noise_sq[:], noise[:], noise[:], ALU.mult)
 
-        wt_wide = keep.tile([P, B * R], F32, name="wt_wide", tag="first", bufs=2)
-        for c0 in range(0, WT_RUN, PACK):
-            wide_bank = bank_tile("wide_bank")
-            for c in range(PACK):
-                nc.tensor.transpose(wide_bank[:, c, :], wt_flat[:, c0 + c : c0 + c + 1].to_broadcast([P, P]), ident[:])
-            nc.scalar.copy(wt_wide[:].rearrange("p (q c) -> p q c", c=WT_RUN)[:, :, c0 : c0 + PACK],
-                           wide_bank[:].rearrange("p c q -> p q c"))
-
-        pairs = [keep.tile([P, T, 2], BF16, name=f"pairs{u}", align_bytes=64) for u in range(2)]
-        picked = [keep.tile([P, 2, N], U32, name=f"picked{b}") for b in range(B)]
-        by_feature = [keep.tile([P, N, PACK], BF16, name=f"by_feature{b}", align_bytes=64) for b in range(B)]
-        slot_codes = [keep.tile([P, D], U32, name=f"slot_codes{b}", align_bytes=64) for b in range(B)]
-        slot_scales = [keep.tile([P, D], U8, name=f"slot_scales{b}", align_bytes=64) for b in range(B)]
+        picked = [keep.tile([P, PACK * N], BF16, name=f"picked{b}", align_bytes=64) for b in range(B)]
         feature_codes = [keep.tile([P, N], U32, name=f"feature_codes{b}", align_bytes=64) for b in range(B)]
         feature_scales = [keep.tile([P, N], U8, name=f"feature_scales{b}", align_bytes=64) for b in range(B)]
-        z_codes = [keep.tile([P, R], U32, name=f"z_codes{b}", align_bytes=64) for b in range(B)]
-        z_scales = [keep.tile([P, R], U8, name=f"z_scales{b}", align_bytes=64) for b in range(B)]
         made = {}
 
-        def round_table(n, engine):
-            u, piece = divmod(n, PIECES_A_PAIR)
-            round_to_bf16(engine, pairs[u][:, PIECE * piece : PIECE * (piece + 1), :], w_raw[n][:].rearrange("p e c -> p c e"))
+        def gather(b, t):
+            nc.vector.tensor_copy(picked[b][:, N * t : N * (t + 1)],
+                                  planes[t][:].indirect(offsets[:, b * LIST_COLS : (b + 1) * LIST_COLS]))
 
-        def gather(b, u):
-            window = pairs[u][:].rearrange("p c e -> p (c e)").bitcast(U32)
-            nc.vector.tensor_copy(picked[b][:, u, :], window.indirect(offsets[:, b * LIST_COLS : (b + 1) * LIST_COLS]))
-
-        def turn_atoms(b, u, engine):
+        def turn_atoms(b, t):
             bank = bank_tile("atom_bank")
-            words = picked[b][:, u, :].bitcast(F32)
-            for s in range(PACK):
-                nc.tensor.transpose(bank[:, s, :], words[:, s:N:PACK], ident[:])
-            src = bank[:].rearrange("m s p -> m (s p)").bitcast(BF16).rearrange("m (s p e) -> m e p s", s=PACK, e=2)
-            made["by_slot", b, u] = ring(engine, [P, HALF, PACK], BF16, "by_slot")
-            move(engine, made["by_slot", b, u][:].rearrange("m (e p) s -> m e p s", e=2), src)
+            words = picked[b][:, N * t : N * (t + 1)].bitcast(F32)
+            for u in range(2):
+                nc.tensor.transpose(bank[:, u, :], words[:, u : N // 2 : 2], ident[:])
+            made["atom_bank", b, t] = bank
 
-        def quantise_by_slot(b, u):
-            cols = slice(HALF * u, HALF * (u + 1))
-            nc.vector.quantize_mx(out=slot_codes[b][:, cols].bitcast(E4M3), scales=slot_scales[b][:, cols],
-                                  in_=made["by_slot", b, u][:].rearrange("m c s -> m (c s)"))
+        def lay_slots(b, t):
+            bank = made["atom_bank", b, t]
+            if (b, t) == (0, PACK - 1):
+                made["by_slot", b, t] = picked[1][:, N * t : N * (t + 1)]
+            else:
+                made["by_slot", b, t] = ring(SCA, [P, N], BF16, "by_slot")[:]
+            nc.scalar.copy(made["by_slot", b, t].bitcast(F32).rearrange("m (p u) -> m p u", u=2),
+                           bank[:, 0:2, :].rearrange("m u p -> m p u"))
 
-        def lay_atoms(b, engine):
-            dst = by_feature[b][:].rearrange("p i t -> p (i t)").bitcast(F32).rearrange("p (i u) -> p i u", u=2)
-            move(engine, dst, picked[b][:].bitcast(F32).rearrange("p u i -> p i u"))
+        def quantise_by_slot(b, t):
+            codes = ring(VEC, [P, P], U32, "slot_codes")
+            scales = keep.tile([P, P], U8, name=f"slot_scales{b}{t}", align_bytes=64)
+            nc.vector.quantize_mx(out=codes[:].bitcast(E4M3), scales=scales[:],
+                                  in_=made["by_slot", b, t])
+            made["slot", b, t] = (codes, scales)
 
-        def quantise_by_feature(b):
-            nc.vector.quantize_mx(out=feature_codes[b][:].bitcast(E4M3), scales=feature_scales[b][:],
-                                  in_=by_feature[b][:].rearrange("p i t -> p (i t)"))
+        def lay_atoms(b, h, engine):
+            made["by_feature", b, h] = ring(engine, [P, HALF, PACK], BF16, "by_feature")
+            runs = HALF // 8
+            move(engine, made["by_feature", b, h][:].rearrange("p (c i) t -> p c t i", i=8),
+                 picked[b][:].rearrange("p (t c i) -> p c t i", t=PACK, i=8)[:, runs * h : runs * (h + 1)])
 
-        def round_coefficients(b, h, engine):
-            made["z_bf", b, h] = ring(engine, [P, HALF, PACK], BF16, "z_bf")
-            runs = HALF // 4
-            round_to_bf16(engine, made["z_bf", b, h][:].rearrange("p (c i) t -> p c t i", i=4),
-                          z_raw[b][:].rearrange("p t (c i) -> p c t i", i=4)[:, runs * h : runs * (h + 1)])
-
-        def quantise_coefficients(b, h):
+        def quantise_by_feature(b, h):
             cols = slice(HALF * h, HALF * (h + 1))
-            nc.vector.quantize_mx(out=z_codes[b][:, cols].bitcast(E4M3), scales=z_scales[b][:, cols],
-                                  in_=made["z_bf", b, h][:].rearrange("p r t -> p (r t)"))
+            nc.vector.quantize_mx(out=feature_codes[b][:, cols].bitcast(E4M3), scales=feature_scales[b][:, cols],
+                                  in_=made["by_feature", b, h][:].rearrange("p i t -> p (i t)"))
+
+        def round_coefficients(k, count, engine):
+            b, j = divmod(k, CHUNKS)
+            made["z_bf", k] = ring(engine, [P, count * P, PACK], BF16, "z_bf")
+            raw = z_raw[b, j // 2].rearrange("p t (m j) -> p t m j", j=2)
+            if count == 1:
+                round_to_bf16(engine, made["z_bf", k][:].rearrange("p (c i) t -> p c t i", i=4),
+                              raw[:, :, :, j % 2].rearrange("p t (c i) -> p c t i", i=4))
+            else:
+                round_to_bf16(engine, made["z_bf", k][:].rearrange("p (j c i) t -> p c t i j", j=2, i=2),
+                              raw.rearrange("p t (c i) j -> p c t i j", i=2))
+
+        def quantise_coefficients(k, count):
+            codes = ring(VEC, [P, count * P], U32, "z_codes")
+            scales = keep.tile([P, count * P], U8, name=f"z_scales{k}", align_bytes=64)
+            nc.vector.quantize_mx(out=codes[:].bitcast(E4M3), scales=scales[:],
+                                  in_=made["z_bf", k][:].rearrange("p r t -> p (r t)"))
+            if k >= CHUNKS:
+                made["spent", (k - CHUNKS) // 2] = made["z_bf", k][:].rearrange("p r t -> p (r t)").bitcast(F32)
+            for i in range(count):
+                made["z", k + i] = (codes[:, P * i : P * (i + 1)], scales[:, P * i : P * (i + 1)])
 
         def rebuild(k):
-            b, j = divmod(k, CHUNKS)
-            rows = slice(P * j, P * (j + 1))
+            b = k // CHUNKS
             made["rec", k] = bank_tile("rec")
-            nc.tensor.matmul_mx(out=made["rec", k][:].rearrange("r t p -> r (t p)"), lhsT=z_codes[b][:, rows].bitcast(E4M3),
-                                lhsT_scale=z_scales[b][:, rows], rhs=slot_codes[b][:].bitcast(E4M3),
-                                rhs_scale=slot_scales[b][:], start=True, stop=True)
+            codes, scales = made["z", k]
+            for t in range(PACK):
+                slot_codes, slot_scales = made["slot", b, t]
+                nc.tensor.matmul_mx(out=made["rec", k][:, t, :], lhsT=codes.bitcast(E4M3), lhsT_scale=scales,
+                                    rhs=slot_codes[:].bitcast(E4M3), rhs_scale=slot_scales[:], start=True, stop=True)
 
         def residual(k):
             b, j = divmod(k, CHUNKS)
@@ -188,35 +200,37 @@ def tile_attend_gdi_cau_z_kernel(tc, zT, wT, xm, wt, cs, offs, out):
             made["gap_sq", k] = ring(SCA, [P, PACK, P], F32, "gap_sq")
             nc.scalar.activation(made["gap_sq", k][:], made["gap_bank", k][:], ACT.Square)
 
-        def weigh(k):
-            made["weighed", k] = ring(VEC, [P, PACK, P], F32, "weighed")
-            nc.vector.tensor_tensor(made["weighed", k][:], made["gap_bank", k][:],
-                                    wt_wide[:, P * k : P * (k + 1)].unsqueeze(1).to_broadcast([P, PACK, P]), ALU.mult)
-
         def root(k):
             made["root", k] = ring(SCA, [P, PACK, P], F32, "root")
             for t in range(PACK):
                 nc.scalar.activation(made["root", k][:, t, :], made["gap_sq", k][:, t, :], ACT.Abs_reciprocal_sqrt,
                                      bias=noise_sq[:, t : t + 1])
 
-        def inverse(k, engine):
-            made["inverse", k] = ring(engine, [P, PACK, P], F32, "inverse")
-            if engine == SCA:
-                nc.scalar.activation(made["inverse", k][:], made["root", k][:], ACT.Square)
-            else:
-                nc.vector.tensor_tensor(made["inverse", k][:], made["root", k][:], made["root", k][:], ALU.mult)
+        def inverse(k):
+            made["inverse", k] = ring(SCA, [P, PACK, P], F32, "inverse")
+            nc.scalar.activation(made["inverse", k][:], made["root", k][:], ACT.Square)
+
+        def weigh(k):
+            made["weighed", k] = made["spent", k] if k not in UNGATED else keep.tile([P, D], F32, name=f"weighed{k}")[:]
+            nc.gpsimd.tensor_scalar(made["weighed", k], made["gap", k][:], wt_cols[:, k : k + 1], 0.0, ALU.mult, ALU.add)
+
+        def turn_weighed(k):
+            made["weighed_bank", k] = bank_tile("weighed_bank")
+            for t in range(PACK):
+                nc.tensor.transpose(made["weighed_bank", k][:, t, :], made["weighed", k][:, P * t : P * (t + 1)], ident[:])
 
         def gradient(k):
-            made["e", k] = ring(VEC, [P, P, PACK], BF16, "e")
-            nc.vector.tensor_tensor(made["e", k][:].rearrange("p (c i) t -> p c t i", i=4),
-                                    made["weighed", k][:].rearrange("p t (c i) -> p c t i", i=4),
+            whole = ring(VEC, [P, D], F32, "e")
+            made["e", k] = whole[:, 0:HALF].bitcast(BF16)
+            made["spent", k + 2 if k < 4 else k + 3] = whole[:]
+            nc.vector.tensor_tensor(made["e", k].rearrange("p (c i t) -> p c t i", i=4, t=PACK),
+                                    made["weighed_bank", k][:].rearrange("p t (c i) -> p c t i", i=4),
                                     made["inverse", k][:].rearrange("p t (c i) -> p c t i", i=4), ALU.mult)
 
         def quantise_gradient(k):
             made["e_codes", k] = ring(VEC, [P, P], U32, "e_codes")
-            made["e_scales", k] = work.tile([P, P], U8, name="e_scales", align_bytes=64)
-            nc.vector.quantize_mx(out=made["e_codes", k][:].bitcast(E5M2), scales=made["e_scales", k][:],
-                                  in_=made["e", k][:].rearrange("p r t -> p (r t)"))
+            made["e_scales", k] = keep.tile([P, P], U8, name=f"e_scales{k}", align_bytes=64)
+            nc.vector.quantize_mx(out=made["e_codes", k][:].bitcast(E5M2), scales=made["e_scales", k][:], in_=made["e", k])
 
         def project(k):
             b = k // CHUNKS
@@ -225,51 +239,87 @@ def tile_attend_gdi_cau_z_kernel(tc, zT, wT, xm, wt, cs, offs, out):
                                 lhsT_scale=made["e_scales", k][:], rhs=feature_codes[b][:].bitcast(E4M3),
                                 rhs_scale=feature_scales[b][:], start=True, stop=True)
 
-        def store(k, engine):
+        def store(k, engines):
             b, j = divmod(k, CHUNKS)
-            staged = ring(engine, [P, N], F32, "staged")
+            rows = out[b, HALF * (j // 2) : HALF * (j // 2 + 1), :].rearrange("(m j) i -> m j i", j=2)[:, j % 2, :]
             sums = made["sums", k][:].rearrange("r a c -> r (a c)")
-            width = N // 2 if k == LAST_CHUNK else N
-            for c0 in range(0, N, width):
-                move(engine, staged[:, c0 : c0 + width], sums[:, c0 : c0 + width])
-                nc.sync.dma_start(out=out[b, P * j : P * (j + 1), c0 : c0 + width], in_=staged[:, c0 : c0 + width])
+            width = N // len(engines)
+            staged = ring(engines[0], [P, N], F32, "staged")
+            for i, engine in enumerate(engines):
+                cols = slice(width * i, width * (i + 1))
+                move(engine, staged[:, cols], sums[:, cols])
+                nc.sync.dma_start(out=rows[:, cols], in_=staged[:, cols])
 
-        loads_behind = {
-            (round_table, 0): (load_table, last_piece, 0),
-            (round_table, 1): (load_coefficients, 0, 1),
-            (round_table, 2): (load_targets, 0, 0, 2),
-            (round_table, 3): (load_targets, 0, 1, 3),
-            (round_table, last_piece): (load_targets, 1, 0, 0),
-            (rebuild, 0): (load_coefficients, 1, 1),
-            (residual, 1): (load_targets, 1, 1, 2),
+        last_plane = PACK - 1
+        early = [(b, t) for t in range(2) for b in range(B)] + [(0, 2)]
+        for b, t in early:
+            gather(b, t)
+            turn_atoms(b, t)
+            lay_slots(b, t)
+        for b, t in early[:-1]:
+            quantise_by_slot(b, t)
+        gather(0, last_plane)
+        turn_atoms(0, last_plane)
+        quantise_by_slot(0, 2)
+        gather(1, 2)
+        turn_atoms(1, 2)
+        round_coefficients(0, 1, SCA)
+        lay_slots(0, last_plane)
+        round_coefficients(1, 1, SCA)
+        quantise_coefficients(0, 1)
+        quantise_by_slot(0, last_plane)
+        rebuild(0)
+        gather(1, last_plane)
+        quantise_coefficients(1, 1)
+        rebuild(1)
+        turn_atoms(1, last_plane)
+        for h in range(2):
+            lay_atoms(0, h, SCA)
+            lay_slots(1, 2 + h)
+
+        residual(0)
+        turn_residual(0)
+        round_coefficients(2, 2, VEC)
+        residual(1)
+        turn_residual(1)
+        quantise_coefficients(2, 2)
+        rebuild(2)
+        rebuild(3)
+        square(0)
+        root(0)
+
+        fillers = {
+            0: [(round_coefficients, 4, 2, VEC), (quantise_by_slot, 1, 2), (quantise_by_slot, 1, 3), (quantise_coefficients, 4, 2)],
+            1: [(round_coefficients, 6, 2, VEC), (quantise_by_feature, 0, 0), (quantise_by_feature, 0, 1), (quantise_coefficients, 6, 2)],
+            2: [(lay_atoms, 1, 0, VEC)],
+            3: [(lay_atoms, 1, 1, VEC), (quantise_by_feature, 1, 0)],
+            4: [(quantise_by_feature, 1, 1)],
         }
-
-        steps = [
-            (round_table, 0, VEC), (round_table, 1, VEC), (round_table, 2, VEC), (round_table, 3, VEC), (gather, 0, 0),
-            (round_table, 4, VEC), (round_coefficients, 0, 1, VEC), (round_table, 5, SCA), (turn_atoms, 0, 0, SCA),
-            (round_table, 6, SCA), (gather, 1, 0), (round_table, 7, VEC), (round_coefficients, 0, 0, VEC), (gather, 0, 1),
-            (gather, 1, 1), (turn_atoms, 1, 0, SCA), (quantise_coefficients, 0, 0), (turn_atoms, 0, 1, SCA),
-            (quantise_by_slot, 0, 0), (quantise_by_slot, 0, 1), (turn_atoms, 1, 1, SCA), (quantise_coefficients, 0, 1),
-            (rebuild, 0), (residual, 0), (rebuild, 1), (residual, 1), (rebuild, 2), (turn_residual, 0),
-            (round_coefficients, 1, 1, VEC), (round_coefficients, 1, 0, SCA), (quantise_coefficients, 1, 0),
-            (turn_residual, 1), (rebuild, 3), (square, 0), (square, 1), (residual, 2), (quantise_by_slot, 1, 0), (root, 0),
-            (lay_atoms, 1, SCA), (residual, 3), (root, 1), (turn_residual, 2), (quantise_by_slot, 1, 1), (rebuild, 4),
-            (inverse, 0, SCA), (rebuild, 5), (quantise_coefficients, 1, 1), (square, 2), (weigh, 0), (inverse, 1, SCA),
-            (turn_residual, 3), (weigh, 1), (residual, 4), (gradient, 0), (rebuild, 6), (turn_residual, 4), (root, 2),
-            (residual, 5), (square, 3), (weigh, 2), (rebuild, 7), (turn_residual, 5), (lay_atoms, 0, SCA), (residual, 6),
-            (square, 4), (inverse, 2, SCA), (quantise_by_feature, 0), (gradient, 1), (turn_residual, 6), (root, 3),
-            (root, 4), (gradient, 2), (inverse, 3, SCA), (quantise_gradient, 0), (quantise_gradient, 1), (weigh, 3),
-            (quantise_gradient, 2), (weigh, 4), (project, 0), (residual, 7), (project, 1), (quantise_by_feature, 1),
-            (square, 5), (store, 0, SCA), (weigh, 5), (gradient, 3), (inverse, 4, SCA), (store, 1, VEC), (root, 5),
-            (inverse, 5, VEC), (quantise_gradient, 3), (turn_residual, 7), (gradient, 4), (gradient, 5), (square, 6),
-            (project, 2), (weigh, 6), (square, 7), (quantise_gradient, 4), (project, 3), (root, 6), (root, 7),
-            (inverse, 6, SCA), (project, 4), (quantise_gradient, 5), (project, 5), (gradient, 6), (weigh, 7),
-            (inverse, 7, SCA), (store, 2, SCA), (quantise_gradient, 6), (gradient, 7), (store, 3, SCA),
-            (quantise_gradient, 7), (store, 4, SCA), (store, 5, SCA), (project, 6), (project, 7), (store, 6, VEC),
-            (store, 7, SCA),
-        ]
-        for step in steps:
-            step[0](*step[1:])
-            if step[:2] in loads_behind:
-                load = loads_behind[step[:2]]
-                load[0](*load[1:])
+        projections = {4: [0], 5: [1, 2], 6: [3, 4], 7: [5], 8: [6], 9: [7]}
+        stores = {5: [(0, [VEC]), (1, [VEC])], 7: [(2, [SCA]), (3, [SCA]), (4, [SCA])], 8: [(5, [VEC])], 9: [(6, [VEC]), (7, [SCA, SCA])]}
+        weighings = {0: [0], 1: [1], 2: [2], 3: [3], 4: [4], 5: [5, 6], 6: [7]}
+        for period in range(0, ALL_CHUNKS + 2):
+            def run(stage, ahead, first=0, last=ALL_CHUNKS):
+                if first <= period + ahead < last:
+                    stage(period + ahead)
+            for filler in fillers.get(period, []):
+                filler[0](*filler[1:])
+            run(quantise_gradient, -2)
+            for k in weighings.get(period, []):
+                weigh(k)
+            for k in projections.get(period, []):
+                project(k)
+            run(rebuild, 4)
+            run(gradient, -1)
+            run(square, 1)
+            run(inverse, 0)
+            run(root, 1)
+            if period == 0:
+                residual(2)
+                turn_residual(2)
+            run(residual, 3)
+            for k in weighings.get(period, []):
+                turn_weighed(k)
+            run(turn_residual, 3)
+            for k, engines in stores.get(period, []):
+                store(k, engines)

@@ -22,9 +22,10 @@ CHUNKS = R // P
 ALL_CHUNKS = B * CHUNKS
 LIST_COLS = N // 16
 HALF = 256
-RING_BUFS = {"vector": 50, "scalar": 20}
+RING_BUFS = {"vector": 48, "scalar": 20}
 STORES_ON_VECTOR = 4
-UNGATED = (6,)
+ON_GPSIMD = 0
+VECTOR_STORES = (6,)
 BANKS = 8
 SMALLEST_SQUARE = 2.0**-120
 VEC, SCA = "vector", "scalar"
@@ -57,13 +58,12 @@ def tile_attend_gdi_cau_z_kernel(tc, zT, wT, xm, wt, cs, offs, out):
 
         offsets = keep.tile([P, B * LIST_COLS], U16, name="offsets")
         nc.sync.dma_start(offsets[:], offs)
-        wt_cols = keep.tile([P, ALL_CHUNKS], F32, name="wt_cols")
+        wt_flat = keep.tile([P, PACK, 2], F32, name="wt_flat")
         ident = keep.tile([P, P], F32, name="ident")
         make_identity(nc, ident[:])
         c_cols = keep.tile([P, PACK], F32, name="c_cols")
         nc.scalar.dma_start(out=c_cols[:], in_=cs[0, :].rearrange("(p t) -> p t", t=PACK))
-        nc.scalar.dma_start(out=wt_cols[:].rearrange("m (g j) -> m g j", j=2),
-                            in_=wt.rearrange("b (h m j) o -> m (b h) (j o)", m=P, j=2))
+        nc.scalar.dma_start(out=wt_flat[:], in_=wt.rearrange("b (q i j) o -> (b q) i (j o)", i=PACK, j=2))
 
         w_planes = wT.rearrange("(p t) c -> p t c", t=PACK)
         planes = {}
@@ -98,7 +98,7 @@ def tile_attend_gdi_cau_z_kernel(tc, zT, wT, xm, wt, cs, offs, out):
         nc.vector.tensor_tensor(c_sq[:], c_cols[:], c_cols[:], ALU.mult)
         c_safe = keep.tile([P, PACK], F32, name="c_safe")
         nc.vector.tensor_scalar(c_safe[:], c_sq[:], SMALLEST_SQUARE, None, ALU.max)
-        seed = keep.tile([P, PACK], F32, name="seed")
+        seed = keep.tile([P, PACK], F32, name="seed", tag="first", bufs=2)
         nc.scalar.activation(seed[:], c_safe[:], ACT.Abs_reciprocal_sqrt)
         seed_sq = keep.tile([P, PACK], F32, name="seed_sq")
         nc.vector.tensor_tensor(seed_sq[:], seed[:], seed[:], ALU.mult)
@@ -110,6 +110,14 @@ def tile_attend_gdi_cau_z_kernel(tc, zT, wT, xm, wt, cs, offs, out):
         nc.vector.tensor_tensor(noise[:], newton[:], seed[:], ALU.mult)
         noise_sq = keep.tile([P, PACK], F32, name="noise_sq")
         nc.vector.tensor_tensor(noise_sq[:], noise[:], noise[:], ALU.mult)
+
+        wt_wide = keep.tile([P, B * R], F32, name="wt_wide", tag="first", bufs=2)
+        for j in range(2):
+            wide_bank = bank_tile("wide_bank")
+            for i in range(PACK):
+                nc.tensor.transpose(wide_bank[:, i, :], wt_flat[:, i, j : j + 1].to_broadcast([P, P]), ident[:])
+            nc.scalar.copy(wt_wide[:].rearrange("p (g j q i) -> p g j q i", j=2, q=P // PACK, i=PACK)[:, :, j],
+                           wide_bank[:].rearrange("p i (g q) -> p g q i", q=P // PACK))
 
         picked = [keep.tile([P, PACK * N], BF16, name=f"picked{b}", align_bytes=64) for b in range(B)]
         feature_codes = [keep.tile([P, N], U32, name=f"feature_codes{b}", align_bytes=64) for b in range(B)]
@@ -129,10 +137,7 @@ def tile_attend_gdi_cau_z_kernel(tc, zT, wT, xm, wt, cs, offs, out):
 
         def lay_slots(b, t):
             bank = made["atom_bank", b, t]
-            if (b, t) == (0, PACK - 1):
-                made["by_slot", b, t] = picked[1][:, N * t : N * (t + 1)]
-            else:
-                made["by_slot", b, t] = ring(SCA, [P, N], BF16, "by_slot")[:]
+            made["by_slot", b, t] = ring(SCA, [P, N], BF16, "by_slot")[:]
             nc.scalar.copy(made["by_slot", b, t].bitcast(F32).rearrange("m (p u) -> m p u", u=2),
                            bank[:, 0:2, :].rearrange("m u p -> m p u"))
 
@@ -210,22 +215,29 @@ def tile_attend_gdi_cau_z_kernel(tc, zT, wT, xm, wt, cs, offs, out):
             made["inverse", k] = ring(SCA, [P, PACK, P], F32, "inverse")
             nc.scalar.activation(made["inverse", k][:], made["root", k][:], ACT.Square)
 
-        def weigh(k):
-            made["weighed", k] = made["spent", k] if k not in UNGATED else keep.tile([P, D], F32, name=f"weighed{k}")[:]
-            nc.gpsimd.tensor_scalar(made["weighed", k], made["gap", k][:], wt_cols[:, k : k + 1], 0.0, ALU.mult, ALU.add)
+        def weights_of(k):
+            return wt_wide[:, P * k : P * (k + 1)].unsqueeze(1).to_broadcast([P, PACK, P])
 
-        def turn_weighed(k):
-            made["weighed_bank", k] = bank_tile("weighed_bank")
-            for t in range(PACK):
-                nc.tensor.transpose(made["weighed_bank", k][:, t, :], made["weighed", k][:, P * t : P * (t + 1)], ident[:])
+        def weigh(k):
+            if k < ON_GPSIMD:
+                weighed = made["spent", k].rearrange("p (t r) -> p t r", t=PACK)
+                nc.gpsimd.tensor_tensor(weighed, made["inverse", k][:], weights_of(k), ALU.mult)
+                made["factors", k] = (made["gap_bank", k][:], weighed)
+
+        def weigh_gap(k):
+            if k >= ON_GPSIMD:
+                weighed = ring(VEC, [P, PACK, P], F32, "weighed")
+                nc.vector.tensor_tensor(weighed[:], made["gap_bank", k][:], weights_of(k), ALU.mult)
+                made["weighed", k] = weighed[:]
 
         def gradient(k):
             whole = ring(VEC, [P, D], F32, "e")
             made["e", k] = whole[:, 0:HALF].bitcast(BF16)
-            made["spent", k + 2 if k < 4 else k + 3] = whole[:]
+            made["spent", k + 2] = whole[:]
+            first, second = made["factors", k] if k < ON_GPSIMD else (made["weighed", k], made["inverse", k][:])
             nc.vector.tensor_tensor(made["e", k].rearrange("p (c i t) -> p c t i", i=4, t=PACK),
-                                    made["weighed_bank", k][:].rearrange("p t (c i) -> p c t i", i=4),
-                                    made["inverse", k][:].rearrange("p t (c i) -> p c t i", i=4), ALU.mult)
+                                    first.rearrange("p t (c i) -> p c t i", i=4),
+                                    second.rearrange("p t (c i) -> p c t i", i=4), ALU.mult)
 
         def quantise_gradient(k):
             made["e_codes", k] = ring(VEC, [P, P], U32, "e_codes")
@@ -251,75 +263,66 @@ def tile_attend_gdi_cau_z_kernel(tc, zT, wT, xm, wt, cs, offs, out):
                 nc.sync.dma_start(out=rows[:, cols], in_=staged[:, cols])
 
         last_plane = PACK - 1
-        early = [(b, t) for t in range(2) for b in range(B)] + [(0, 2)]
-        for b, t in early:
-            gather(b, t)
-            turn_atoms(b, t)
-            lay_slots(b, t)
-        for b, t in early[:-1]:
-            quantise_by_slot(b, t)
+        for t in range(last_plane):
+            for b in range(B):
+                gather(b, t)
+                turn_atoms(b, t)
+                lay_slots(b, t)
+            if t > 0:
+                quantise_by_slot(0, t - 1)
         gather(0, last_plane)
         turn_atoms(0, last_plane)
-        quantise_by_slot(0, 2)
-        gather(1, 2)
-        turn_atoms(1, 2)
+        quantise_by_slot(0, last_plane - 1)
+        gather(1, last_plane)
         round_coefficients(0, 1, SCA)
-        lay_slots(0, last_plane)
         round_coefficients(1, 1, SCA)
+        lay_slots(0, last_plane)
         quantise_coefficients(0, 1)
         quantise_by_slot(0, last_plane)
         rebuild(0)
-        gather(1, last_plane)
         quantise_coefficients(1, 1)
         rebuild(1)
-        turn_atoms(1, last_plane)
-        for h in range(2):
-            lay_atoms(0, h, SCA)
-            lay_slots(1, 2 + h)
-
+        for t in range(last_plane):
+            quantise_by_slot(1, t)
+        lay_atoms(0, 0, SCA)
+        lay_atoms(0, 1, SCA)
         residual(0)
         turn_residual(0)
+        turn_atoms(1, last_plane)
+        lay_atoms(1, 0, SCA)
         round_coefficients(2, 2, VEC)
         residual(1)
         turn_residual(1)
         quantise_coefficients(2, 2)
         rebuild(2)
-        rebuild(3)
-        square(0)
-        root(0)
 
         fillers = {
-            0: [(round_coefficients, 4, 2, VEC), (quantise_by_slot, 1, 2), (quantise_by_slot, 1, 3), (quantise_coefficients, 4, 2)],
-            1: [(round_coefficients, 6, 2, VEC), (quantise_by_feature, 0, 0), (quantise_by_feature, 0, 1), (quantise_coefficients, 6, 2)],
-            2: [(lay_atoms, 1, 0, VEC)],
-            3: [(lay_atoms, 1, 1, VEC), (quantise_by_feature, 1, 0)],
-            4: [(quantise_by_feature, 1, 1)],
+            -1: [(round_coefficients, 4, 2, VEC), (quantise_by_feature, 0, 0), (quantise_coefficients, 4, 2)],
+            0: [(round_coefficients, 6, 2, VEC), (quantise_by_slot, 1, 3), (quantise_by_feature, 0, 1)],
+            1: [(quantise_coefficients, 6, 2), (quantise_by_feature, 1, 0)],
+            4: [(lay_atoms, 1, 1, VEC)], 5: [(quantise_by_feature, 1, 1)],
         }
-        projections = {4: [0], 5: [1, 2], 6: [3, 4], 7: [5], 8: [6], 9: [7]}
-        stores = {5: [(0, [VEC]), (1, [VEC])], 7: [(2, [SCA]), (3, [SCA]), (4, [SCA])], 8: [(5, [VEC])], 9: [(6, [VEC]), (7, [SCA, SCA])]}
-        weighings = {0: [0], 1: [1], 2: [2], 3: [3], 4: [4], 5: [5, 6], 6: [7]}
-        for period in range(0, ALL_CHUNKS + 2):
+        projections = {2: [0], 3: [1], 4: [2], 5: [3], 6: [4], 7: [5], 8: [6], 9: [7]}
+        stores = {3: [(0, [SCA])], 4: [(1, [SCA])], 5: [(2, [SCA])], 7: [(3, [SCA]), (4, [SCA])], 8: [(5, [SCA]), (6, [SCA])], 9: [(7, [SCA, SCA])]}
+        scalar_fillers = {-1: [(lay_slots, 1, 3)]}
+        for period in range(-1, ALL_CHUNKS + 3):
             def run(stage, ahead, first=0, last=ALL_CHUNKS):
                 if first <= period + ahead < last:
                     stage(period + ahead)
+            run(square, 1)
+            for filler in scalar_fillers.get(period, []):
+                filler[0](*filler[1:])
+            run(weigh_gap, 0)
+            run(quantise_gradient, -2)
             for filler in fillers.get(period, []):
                 filler[0](*filler[1:])
-            run(quantise_gradient, -2)
-            for k in weighings.get(period, []):
-                weigh(k)
             for k in projections.get(period, []):
                 project(k)
-            run(rebuild, 4)
-            run(gradient, -1)
-            run(square, 1)
+            run(rebuild, 4, 3)
             run(inverse, 0)
             run(root, 1)
-            if period == 0:
-                residual(2)
-                turn_residual(2)
-            run(residual, 3)
-            for k in weighings.get(period, []):
-                turn_weighed(k)
-            run(turn_residual, 3)
+            run(residual, 3, 2)
+            run(turn_residual, 3, 2)
+            run(gradient, -1)
             for k, engines in stores.get(period, []):
                 store(k, engines)

@@ -22,7 +22,7 @@ CHUNKS = R // P
 ALL_CHUNKS = B * CHUNKS
 LIST_COLS = N // 16
 HALF = 256
-RING_BUFS = {"vector": 48, "scalar": 20}
+RING_BUFS = {"vector": 48, "scalar": 18}
 STORES_ON_VECTOR = 4
 ON_GPSIMD = 0
 VECTOR_STORES = (6,)
@@ -125,8 +125,11 @@ def tile_attend_gdi_cau_z_kernel(tc, zT, wT, xm, wt, cs, offs, out):
         made = {}
 
         def gather(b, t):
-            nc.vector.tensor_copy(picked[b][:, N * t : N * (t + 1)],
-                                  planes[t][:].indirect(offsets[:, b * LIST_COLS : (b + 1) * LIST_COLS]))
+            listed = offsets[:, b * LIST_COLS : (b + 1) * LIST_COLS]
+            if t == 0:
+                nc.scalar.activation(picked[b][:, 0:N], first_plane[:].indirect(listed), ACT.Copy)
+            else:
+                nc.vector.tensor_copy(picked[b][:, N * t : N * (t + 1)], planes[t][:].indirect(listed))
 
         def turn_atoms(b, t):
             bank = bank_tile("atom_bank")
@@ -150,9 +153,9 @@ def tile_attend_gdi_cau_z_kernel(tc, zT, wT, xm, wt, cs, offs, out):
 
         def lay_atoms(b, h, engine):
             made["by_feature", b, h] = ring(engine, [P, HALF, PACK], BF16, "by_feature")
-            runs = HALF // 8
-            move(engine, made["by_feature", b, h][:].rearrange("p (c i) t -> p c t i", i=8),
-                 picked[b][:].rearrange("p (t c i) -> p c t i", t=PACK, i=8)[:, runs * h : runs * (h + 1)])
+            runs = HALF // 4
+            move(engine, made["by_feature", b, h][:].rearrange("p (c i) t -> p c t i", i=4),
+                 picked[b][:].rearrange("p (t c i) -> p c t i", t=PACK, i=4)[:, runs * h : runs * (h + 1)])
 
         def quantise_by_feature(b, h):
             cols = slice(HALF * h, HALF * (h + 1))
@@ -192,14 +195,14 @@ def tile_attend_gdi_cau_z_kernel(tc, zT, wT, xm, wt, cs, offs, out):
         def residual(k):
             b, j = divmod(k, CHUNKS)
             made["gap", k] = ring(VEC, [P, D], F32, "gap")
-            nc.vector.tensor_tensor(made["gap", k][:].rearrange("r (t p) -> r p t", t=PACK),
-                                    made["rec", k][:].rearrange("r t p -> r p t"),
-                                    x_raw[b, j // 2][:, j % 2, :].rearrange("r (p t) -> r p t", t=PACK), ALU.subtract)
+            nc.vector.tensor_tensor(made["gap", k][:].rearrange("r (u p e) -> r p u e", u=2, e=2),
+                                    made["rec", k][:].rearrange("r (u e) p -> r p u e", u=2),
+                                    x_raw[b, j // 2][:, j % 2, :].rearrange("r (p u e) -> r p u e", u=2, e=2), ALU.subtract)
 
         def turn_residual(k):
             made["gap_bank", k] = bank_tile("gap_bank")
             for t in range(PACK):
-                nc.tensor.transpose(made["gap_bank", k][:, t, :], made["gap", k][:, P * t : P * (t + 1)], ident[:])
+                nc.tensor.transpose(made["gap_bank", k][:, t, :], made["gap", k][:, HALF * (t // 2) + t % 2 : HALF * (t // 2 + 1) : 2], ident[:])
 
         def square(k):
             made["gap_sq", k] = ring(SCA, [P, PACK, P], F32, "gap_sq")
@@ -260,12 +263,16 @@ def tile_attend_gdi_cau_z_kernel(tc, zT, wT, xm, wt, cs, offs, out):
             for i, engine in enumerate(engines):
                 cols = slice(width * i, width * (i + 1))
                 move(engine, staged[:, cols], sums[:, cols])
-                nc.sync.dma_start(out=rows[:, cols], in_=staged[:, cols])
+                queue = nc.scalar if k == ALL_CHUNKS - 1 else nc.sync
+                queue.dma_start(out=rows[:, cols], in_=staged[:, cols])
 
         last_plane = PACK - 1
+        first_plane = keep.tile([P, T], BF16, name="first_plane", align_bytes=64)
+        nc.vector.tensor_copy(first_plane[:], planes[0][:])
         for t in range(last_plane):
             for b in range(B):
                 gather(b, t)
+            for b in range(B):
                 turn_atoms(b, t)
                 lay_slots(b, t)
             if t > 0:
@@ -275,8 +282,8 @@ def tile_attend_gdi_cau_z_kernel(tc, zT, wT, xm, wt, cs, offs, out):
         quantise_by_slot(0, last_plane - 1)
         gather(1, last_plane)
         round_coefficients(0, 1, SCA)
-        round_coefficients(1, 1, SCA)
         lay_slots(0, last_plane)
+        round_coefficients(1, 1, SCA)
         quantise_coefficients(0, 1)
         quantise_by_slot(0, last_plane)
         rebuild(0)

@@ -23,9 +23,6 @@ ALL_CHUNKS = B * CHUNKS
 LIST_COLS = N // 16
 HALF = 256
 RING_BUFS = {"vector": 48, "scalar": 18}
-STORES_ON_VECTOR = 4
-ON_GPSIMD = 0
-VECTOR_STORES = (6,)
 BANKS = 8
 SMALLEST_SQUARE = 2.0**-120
 VEC, SCA = "vector", "scalar"
@@ -178,8 +175,6 @@ def tile_attend_gdi_cau_z_kernel(tc, zT, wT, xm, wt, cs, offs, out):
             scales = keep.tile([P, count * P], U8, name=f"z_scales{k}", align_bytes=64)
             nc.vector.quantize_mx(out=codes[:].bitcast(E4M3), scales=scales[:],
                                   in_=made["z_bf", k][:].rearrange("p r t -> p (r t)"))
-            if k >= CHUNKS:
-                made["spent", (k - CHUNKS) // 2] = made["z_bf", k][:].rearrange("p r t -> p (r t)").bitcast(F32)
             for i in range(count):
                 made["z", k + i] = (codes[:, P * i : P * (i + 1)], scales[:, P * i : P * (i + 1)])
 
@@ -215,32 +210,19 @@ def tile_attend_gdi_cau_z_kernel(tc, zT, wT, xm, wt, cs, offs, out):
                                      bias=noise_sq[:, t : t + 1])
 
         def inverse(k):
-            made["inverse", k] = ring(SCA, [P, PACK, P], F32, "inverse")
-            nc.scalar.activation(made["inverse", k][:], made["root", k][:], ACT.Square)
-
-        def weights_of(k):
-            return wt_wide[:, P * k : P * (k + 1)].unsqueeze(1).to_broadcast([P, PACK, P])
-
-        def weigh(k):
-            if k < ON_GPSIMD:
-                weighed = made["spent", k].rearrange("p (t r) -> p t r", t=PACK)
-                nc.gpsimd.tensor_tensor(weighed, made["inverse", k][:], weights_of(k), ALU.mult)
-                made["factors", k] = (made["gap_bank", k][:], weighed)
+            made["inverse", k] = ring(SCA, [P, 2, P, 2], F32, "inverse")
+            nc.scalar.activation(made["inverse", k][:], made["root", k][:].rearrange("p (u e) r -> p u r e", u=2), ACT.Square)
 
         def weigh_gap(k):
-            if k >= ON_GPSIMD:
-                weighed = ring(VEC, [P, PACK, P], F32, "weighed")
-                nc.vector.tensor_tensor(weighed[:], made["gap_bank", k][:], weights_of(k), ALU.mult)
-                made["weighed", k] = weighed[:]
+            made["weighed", k] = ring(VEC, [P, P, PACK], F32, "weighed")
+            nc.vector.tensor_tensor(made["weighed", k][:], made["gap_bank", k][:].rearrange("p t r -> p r t"),
+                                    wt_wide[:, P * k : P * (k + 1)].unsqueeze(2).to_broadcast([P, P, PACK]), ALU.mult)
 
         def gradient(k):
-            whole = ring(VEC, [P, D], F32, "e")
-            made["e", k] = whole[:, 0:HALF].bitcast(BF16)
-            made["spent", k + 2] = whole[:]
-            first, second = made["factors", k] if k < ON_GPSIMD else (made["weighed", k], made["inverse", k][:])
-            nc.vector.tensor_tensor(made["e", k].rearrange("p (c i t) -> p c t i", i=4, t=PACK),
-                                    first.rearrange("p t (c i) -> p c t i", i=4),
-                                    second.rearrange("p t (c i) -> p c t i", i=4), ALU.mult)
+            made["e", k] = ring(VEC, [P, D], BF16, "e")[:]
+            nc.vector.tensor_tensor(made["e", k].rearrange("p (r u e) -> p r u e", u=2, e=2),
+                                    made["weighed", k][:].rearrange("p r (u e) -> p r u e", u=2),
+                                    made["inverse", k][:].rearrange("p u r e -> p r u e"), ALU.mult)
 
         def quantise_gradient(k):
             made["e_codes", k] = ring(VEC, [P, P], U32, "e_codes")
@@ -263,7 +245,7 @@ def tile_attend_gdi_cau_z_kernel(tc, zT, wT, xm, wt, cs, offs, out):
             for i, engine in enumerate(engines):
                 cols = slice(width * i, width * (i + 1))
                 move(engine, staged[:, cols], sums[:, cols])
-                queue = nc.scalar if k == ALL_CHUNKS - 1 else nc.sync
+                queue = nc.scalar if k == ALL_CHUNKS - 1 and i == 1 else nc.sync
                 queue.dma_start(out=rows[:, cols], in_=staged[:, cols])
 
         last_plane = PACK - 1
@@ -287,10 +269,10 @@ def tile_attend_gdi_cau_z_kernel(tc, zT, wT, xm, wt, cs, offs, out):
         quantise_coefficients(0, 1)
         quantise_by_slot(0, last_plane)
         rebuild(0)
-        quantise_coefficients(1, 1)
-        rebuild(1)
         for t in range(last_plane):
             quantise_by_slot(1, t)
+        quantise_coefficients(1, 1)
+        rebuild(1)
         lay_atoms(0, 0, SCA)
         lay_atoms(0, 1, SCA)
         residual(0)
@@ -310,7 +292,7 @@ def tile_attend_gdi_cau_z_kernel(tc, zT, wT, xm, wt, cs, offs, out):
             4: [(lay_atoms, 1, 1, VEC)], 5: [(quantise_by_feature, 1, 1)],
         }
         projections = {2: [0], 3: [1], 4: [2], 5: [3], 6: [4], 7: [5], 8: [6], 9: [7]}
-        stores = {3: [(0, [SCA])], 4: [(1, [SCA])], 5: [(2, [SCA])], 7: [(3, [SCA]), (4, [SCA])], 8: [(5, [SCA]), (6, [SCA])], 9: [(7, [SCA, SCA])]}
+        stores = {3: [(0, [SCA])], 4: [(1, [SCA])], 5: [(2, [SCA])], 7: [(3, [SCA]), (4, [SCA])], 8: [(5, [SCA])], 9: [(6, [VEC]), (7, [SCA, SCA])]}
         scalar_fillers = {-1: [(lay_slots, 1, 3)]}
         for period in range(-1, ALL_CHUNKS + 3):
             def run(stage, ahead, first=0, last=ALL_CHUNKS):

@@ -18,14 +18,18 @@ ACT = mybir.ActivationFunctionType
 
 P = 128
 PACK = 4
+LAST_PLANE = PACK - 1
 CHUNKS = R // P
 ALL_CHUNKS = B * CHUNKS
+LAST_CHUNK = ALL_CHUNKS - 1
 LIST_COLS = N // 16
 HALF = 256
-RING_BUFS = {"vector": 48, "scalar": 18}
-BANKS = 8
-SMALLEST_SQUARE = 2.0**-120
+RUN = 4
 VEC, SCA = "vector", "scalar"
+RING_BUFS = {VEC: 48, SCA: 18}
+BANKS = 8
+WEIGHED_TURNED = (2, 3)
+SMALLEST_SQUARE = 2.0**-120
 
 
 def tile_attend_gdi_cau_z_kernel(tc, zT, wT, xm, wt, cs, offs, out):
@@ -47,20 +51,15 @@ def tile_attend_gdi_cau_z_kernel(tc, zT, wT, xm, wt, cs, offs, out):
             else:
                 nc.vector.tensor_copy(out=dst, in_=src)
 
-        def round_to_bf16(engine, dst, src):
-            if engine == SCA:
-                nc.scalar.activation(dst, src, ACT.Copy)
-            else:
-                nc.vector.tensor_copy(out=dst, in_=src)
-
         offsets = keep.tile([P, B * LIST_COLS], U16, name="offsets")
         nc.sync.dma_start(offsets[:], offs)
-        wt_flat = keep.tile([P, PACK, 2], F32, name="wt_flat")
+        wt_cols = keep.tile([P, ALL_CHUNKS], F32, name="wt_cols")
         ident = keep.tile([P, P], F32, name="ident")
         make_identity(nc, ident[:])
         c_cols = keep.tile([P, PACK], F32, name="c_cols")
         nc.scalar.dma_start(out=c_cols[:], in_=cs[0, :].rearrange("(p t) -> p t", t=PACK))
-        nc.scalar.dma_start(out=wt_flat[:], in_=wt.rearrange("b (q i j) o -> (b q) i (j o)", i=PACK, j=2))
+        nc.scalar.dma_start(out=wt_cols[:].rearrange("m (g j) -> m g j", j=2),
+                            in_=wt.rearrange("b (h m j) o -> m (b h) (j o)", m=P, j=2))
 
         w_planes = wT.rearrange("(p t) c -> p t c", t=PACK)
         planes = {}
@@ -79,7 +78,7 @@ def tile_attend_gdi_cau_z_kernel(tc, zT, wT, xm, wt, cs, offs, out):
 
         def load_targets(b, h):
             x_raw[b, h] = keep.tile([P, 2, D], F32, name=f"x_raw{b}{h}", align_bytes=64)
-            nc.sync.dma_start(out=x_raw[b, h][:], in_=xm[b, HALF * h : HALF * (h + 1), :].rearrange("(p j) d -> p j d", j=2))
+            nc.sync.dma_start(out=x_raw[b, h][:], in_=xm[b, HALF * h : HALF * (h + 1), :].rearrange("(m j) d -> m j d", j=2))
 
         for t in range(PACK):
             load_plane(t)
@@ -108,17 +107,16 @@ def tile_attend_gdi_cau_z_kernel(tc, zT, wT, xm, wt, cs, offs, out):
         noise_sq = keep.tile([P, PACK], F32, name="noise_sq")
         nc.vector.tensor_tensor(noise_sq[:], noise[:], noise[:], ALU.mult)
 
-        wt_wide = keep.tile([P, B * R], F32, name="wt_wide", tag="first", bufs=2)
-        for j in range(2):
-            wide_bank = bank_tile("wide_bank")
-            for i in range(PACK):
-                nc.tensor.transpose(wide_bank[:, i, :], wt_flat[:, i, j : j + 1].to_broadcast([P, P]), ident[:])
-            nc.scalar.copy(wt_wide[:].rearrange("p (g j q i) -> p g j q i", j=2, q=P // PACK, i=PACK)[:, :, j],
-                           wide_bank[:].rearrange("p i (g q) -> p g q i", q=P // PACK))
+        wt_wide = keep.tile([P, len(WEIGHED_TURNED), P], F32, name="wt_wide", tag="first", bufs=2)
+        wide_bank = bank_tile("wide_bank")
+        for n, k in enumerate(WEIGHED_TURNED):
+            nc.tensor.transpose(wide_bank[:, n, :], wt_cols[:, k : k + 1].to_broadcast([P, P]), ident[:])
+        nc.scalar.copy(wt_wide[:], wide_bank[:, 0 : len(WEIGHED_TURNED), :])
 
         picked = [keep.tile([P, PACK * N], BF16, name=f"picked{b}", align_bytes=64) for b in range(B)]
         feature_codes = [keep.tile([P, N], U32, name=f"feature_codes{b}", align_bytes=64) for b in range(B)]
         feature_scales = [keep.tile([P, N], U8, name=f"feature_scales{b}", align_bytes=64) for b in range(B)]
+        first_plane = keep.tile([P, T], BF16, name="first_plane", align_bytes=64)
         made = {}
 
         def gather(b, t):
@@ -129,75 +127,74 @@ def tile_attend_gdi_cau_z_kernel(tc, zT, wT, xm, wt, cs, offs, out):
                 nc.vector.tensor_copy(picked[b][:, N * t : N * (t + 1)], planes[t][:].indirect(listed))
 
         def turn_atoms(b, t):
-            bank = bank_tile("atom_bank")
+            made["atom_bank", b, t] = bank_tile("atom_bank")
             words = picked[b][:, N * t : N * (t + 1)].bitcast(F32)
             for u in range(2):
-                nc.tensor.transpose(bank[:, u, :], words[:, u : N // 2 : 2], ident[:])
-            made["atom_bank", b, t] = bank
+                nc.tensor.transpose(made["atom_bank", b, t][:, u, :], words[:, u : N // 2 : 2], ident[:])
 
         def lay_slots(b, t):
-            bank = made["atom_bank", b, t]
-            made["by_slot", b, t] = ring(SCA, [P, N], BF16, "by_slot")[:]
-            nc.scalar.copy(made["by_slot", b, t].bitcast(F32).rearrange("m (p u) -> m p u", u=2),
-                           bank[:, 0:2, :].rearrange("m u p -> m p u"))
+            made["by_slot", b, t] = ring(SCA, [P, N], BF16, "by_slot")
+            nc.scalar.copy(made["by_slot", b, t][:].bitcast(F32).rearrange("m (p u) -> m p u", u=2),
+                           made["atom_bank", b, t][:, 0:2, :].rearrange("m u p -> m p u"))
 
         def quantise_by_slot(b, t):
             codes = ring(VEC, [P, P], U32, "slot_codes")
             scales = keep.tile([P, P], U8, name=f"slot_scales{b}{t}", align_bytes=64)
-            nc.vector.quantize_mx(out=codes[:].bitcast(E4M3), scales=scales[:],
-                                  in_=made["by_slot", b, t])
+            nc.vector.quantize_mx(out=codes[:].bitcast(E4M3), scales=scales[:], in_=made["by_slot", b, t][:])
             made["slot", b, t] = (codes, scales)
 
-        def lay_atoms(b, h, engine):
+        def lay_features(b, h, engine):
             made["by_feature", b, h] = ring(engine, [P, HALF, PACK], BF16, "by_feature")
-            runs = HALF // 4
-            move(engine, made["by_feature", b, h][:].rearrange("p (c i) t -> p c t i", i=4),
-                 picked[b][:].rearrange("p (t c i) -> p c t i", t=PACK, i=4)[:, runs * h : runs * (h + 1)])
+            runs = HALF // RUN
+            move(engine, made["by_feature", b, h][:].rearrange("p (c i) t -> p c t i", i=RUN),
+                 picked[b][:].rearrange("p (t c i) -> p c t i", t=PACK, i=RUN)[:, runs * h : runs * (h + 1)])
 
         def quantise_by_feature(b, h):
             cols = slice(HALF * h, HALF * (h + 1))
             nc.vector.quantize_mx(out=feature_codes[b][:, cols].bitcast(E4M3), scales=feature_scales[b][:, cols],
                                   in_=made["by_feature", b, h][:].rearrange("p i t -> p (i t)"))
 
-        def round_coefficients(k, count, engine):
-            b, j = divmod(k, CHUNKS)
-            made["z_bf", k] = ring(engine, [P, count * P, PACK], BF16, "z_bf")
-            raw = z_raw[b, j // 2].rearrange("p t (m j) -> p t m j", j=2)
-            if count == 1:
-                round_to_bf16(engine, made["z_bf", k][:].rearrange("p (c i) t -> p c t i", i=4),
-                              raw[:, :, :, j % 2].rearrange("p t (c i) -> p c t i", i=4))
-            else:
-                round_to_bf16(engine, made["z_bf", k][:].rearrange("p (j c i) t -> p c t i j", j=2, i=2),
-                              raw.rearrange("p t (c i) j -> p c t i j", i=2))
+        def round_chunk(k):
+            b, c = divmod(k, CHUNKS)
+            made["z_bf", k] = ring(SCA, [P, P, PACK], BF16, "z_bf")
+            samples = z_raw[b, c // 2].rearrange("p t (m j) -> p t m j", j=2)[:, :, :, c % 2]
+            nc.scalar.activation(made["z_bf", k][:].rearrange("p (c i) t -> p c t i", i=RUN),
+                                 samples.rearrange("p t (c i) -> p c t i", i=RUN), ACT.Copy)
+
+        def round_pair(k):
+            b, c = divmod(k, CHUNKS)
+            made["z_bf", k] = ring(VEC, [P, 2 * P, PACK], BF16, "z_bf")
+            nc.vector.tensor_copy(out=made["z_bf", k][:].rearrange("p (j c i) t -> p c t i j", j=2, i=2),
+                                  in_=z_raw[b, c // 2].rearrange("p t (c i j) -> p c t i j", i=2, j=2))
 
         def quantise_coefficients(k, count):
             codes = ring(VEC, [P, count * P], U32, "z_codes")
             scales = keep.tile([P, count * P], U8, name=f"z_scales{k}", align_bytes=64)
             nc.vector.quantize_mx(out=codes[:].bitcast(E4M3), scales=scales[:],
                                   in_=made["z_bf", k][:].rearrange("p r t -> p (r t)"))
-            for i in range(count):
-                made["z", k + i] = (codes[:, P * i : P * (i + 1)], scales[:, P * i : P * (i + 1)])
+            for n in range(count):
+                made["z", k + n] = (codes[:, P * n : P * (n + 1)], scales[:, P * n : P * (n + 1)])
 
         def rebuild(k):
-            b = k // CHUNKS
             made["rec", k] = bank_tile("rec")
-            codes, scales = made["z", k]
+            z_codes, z_scales = made["z", k]
             for t in range(PACK):
-                slot_codes, slot_scales = made["slot", b, t]
-                nc.tensor.matmul_mx(out=made["rec", k][:, t, :], lhsT=codes.bitcast(E4M3), lhsT_scale=scales,
+                slot_codes, slot_scales = made["slot", k // CHUNKS, t]
+                nc.tensor.matmul_mx(out=made["rec", k][:, t, :], lhsT=z_codes.bitcast(E4M3), lhsT_scale=z_scales,
                                     rhs=slot_codes[:].bitcast(E4M3), rhs_scale=slot_scales[:], start=True, stop=True)
 
         def residual(k):
-            b, j = divmod(k, CHUNKS)
+            b, c = divmod(k, CHUNKS)
             made["gap", k] = ring(VEC, [P, D], F32, "gap")
-            nc.vector.tensor_tensor(made["gap", k][:].rearrange("r (u p e) -> r p u e", u=2, e=2),
-                                    made["rec", k][:].rearrange("r (u e) p -> r p u e", u=2),
-                                    x_raw[b, j // 2][:, j % 2, :].rearrange("r (p u e) -> r p u e", u=2, e=2), ALU.subtract)
+            nc.vector.tensor_tensor(made["gap", k][:].rearrange("m (u p v) -> m p u v", u=2, v=2),
+                                    made["rec", k][:].rearrange("m (u v) p -> m p u v", u=2),
+                                    x_raw[b, c // 2][:, c % 2, :].rearrange("m (p u v) -> m p u v", u=2, v=2), ALU.subtract)
 
         def turn_residual(k):
             made["gap_bank", k] = bank_tile("gap_bank")
             for t in range(PACK):
-                nc.tensor.transpose(made["gap_bank", k][:, t, :], made["gap", k][:, HALF * (t // 2) + t % 2 : HALF * (t // 2 + 1) : 2], ident[:])
+                u, v = divmod(t, 2)
+                nc.tensor.transpose(made["gap_bank", k][:, t, :], made["gap", k][:, HALF * u + v : HALF * (u + 1) : 2], ident[:])
 
         def square(k):
             made["gap_sq", k] = ring(SCA, [P, PACK, P], F32, "gap_sq")
@@ -211,47 +208,59 @@ def tile_attend_gdi_cau_z_kernel(tc, zT, wT, xm, wt, cs, offs, out):
 
         def inverse(k):
             made["inverse", k] = ring(SCA, [P, 2, P, 2], F32, "inverse")
-            nc.scalar.activation(made["inverse", k][:], made["root", k][:].rearrange("p (u e) r -> p u r e", u=2), ACT.Square)
+            nc.scalar.activation(made["inverse", k][:], made["root", k][:].rearrange("p (u v) m -> p u m v", u=2), ACT.Square)
 
-        def weigh_gap(k):
-            made["weighed", k] = ring(VEC, [P, P, PACK], F32, "weighed")
-            nc.vector.tensor_tensor(made["weighed", k][:], made["gap_bank", k][:].rearrange("p t r -> p r t"),
-                                    wt_wide[:, P * k : P * (k + 1)].unsqueeze(2).to_broadcast([P, P, PACK]), ALU.mult)
+        def weigh_turned(k):
+            if k in WEIGHED_TURNED:
+                weighed = ring(VEC, [P, P, PACK], F32, "weighed_turned")
+                weights = wt_wide[:, WEIGHED_TURNED.index(k), :].unsqueeze(2).to_broadcast([P, P, PACK])
+                nc.vector.tensor_tensor(weighed[:], made["gap_bank", k][:].rearrange("p t m -> p m t"), weights, ALU.mult)
+                made["numerator", k] = weighed[:].rearrange("p m (u v) -> p m u v", u=2)
+
+        def weigh(k):
+            if k not in WEIGHED_TURNED:
+                made["weighed", k] = ring(VEC, [P, D], F32, "weighed")
+                nc.vector.tensor_scalar(made["weighed", k][:].rearrange("m (u v p) -> m u v p", u=2, v=2),
+                                        made["gap", k][:].rearrange("m (u p v) -> m u v p", u=2, v=2),
+                                        wt_cols[:, k : k + 1], None, ALU.mult)
+
+        def turn_weighed(k):
+            if k not in WEIGHED_TURNED:
+                weighed_bank = bank_tile("weighed_bank")
+                for t in range(PACK):
+                    nc.tensor.transpose(weighed_bank[:, t, :], made["weighed", k][:, P * t : P * (t + 1)], ident[:])
+                made["numerator", k] = weighed_bank[:].rearrange("p (u v) m -> p m u v", u=2)
 
         def gradient(k):
-            made["e", k] = ring(VEC, [P, D], BF16, "e")[:]
-            nc.vector.tensor_tensor(made["e", k].rearrange("p (r u e) -> p r u e", u=2, e=2),
-                                    made["weighed", k][:].rearrange("p r (u e) -> p r u e", u=2),
-                                    made["inverse", k][:].rearrange("p u r e -> p r u e"), ALU.mult)
+            made["e", k] = ring(VEC, [P, D], BF16, "e")
+            nc.vector.tensor_tensor(made["e", k][:].rearrange("p (m u v) -> p m u v", u=2, v=2), made["numerator", k],
+                                    made["inverse", k][:].rearrange("p u m v -> p m u v"), ALU.mult)
 
         def quantise_gradient(k):
             made["e_codes", k] = ring(VEC, [P, P], U32, "e_codes")
             made["e_scales", k] = keep.tile([P, P], U8, name=f"e_scales{k}", align_bytes=64)
-            nc.vector.quantize_mx(out=made["e_codes", k][:].bitcast(E5M2), scales=made["e_scales", k][:], in_=made["e", k])
+            nc.vector.quantize_mx(out=made["e_codes", k][:].bitcast(E5M2), scales=made["e_scales", k][:], in_=made["e", k][:])
 
         def project(k):
             b = k // CHUNKS
             made["sums", k] = bank_tile("sums")
-            nc.tensor.matmul_mx(out=made["sums", k][:].rearrange("r a c -> r (a c)"), lhsT=made["e_codes", k][:].bitcast(E5M2),
+            nc.tensor.matmul_mx(out=made["sums", k][:].rearrange("m a c -> m (a c)"), lhsT=made["e_codes", k][:].bitcast(E5M2),
                                 lhsT_scale=made["e_scales", k][:], rhs=feature_codes[b][:].bitcast(E4M3),
                                 rhs_scale=feature_scales[b][:], start=True, stop=True)
 
-        def store(k, engines):
-            b, j = divmod(k, CHUNKS)
-            rows = out[b, HALF * (j // 2) : HALF * (j // 2 + 1), :].rearrange("(m j) i -> m j i", j=2)[:, j % 2, :]
-            sums = made["sums", k][:].rearrange("r a c -> r (a c)")
-            width = N // len(engines)
-            staged = ring(engines[0], [P, N], F32, "staged")
-            for i, engine in enumerate(engines):
-                cols = slice(width * i, width * (i + 1))
+        def store(k, engine, queues):
+            b, c = divmod(k, CHUNKS)
+            rows = out[b, HALF * (c // 2) : HALF * (c // 2 + 1), :].rearrange("(m j) i -> m j i", j=2)[:, c % 2, :]
+            sums = made["sums", k][:].rearrange("m a c -> m (a c)")
+            width = N // len(queues)
+            staged = ring(engine, [P, N], F32, "staged")
+            for n, queue in enumerate(queues):
+                cols = slice(width * n, width * (n + 1))
                 move(engine, staged[:, cols], sums[:, cols])
-                queue = nc.scalar if k == ALL_CHUNKS - 1 and i == 1 else nc.sync
                 queue.dma_start(out=rows[:, cols], in_=staged[:, cols])
 
-        last_plane = PACK - 1
-        first_plane = keep.tile([P, T], BF16, name="first_plane", align_bytes=64)
         nc.vector.tensor_copy(first_plane[:], planes[0][:])
-        for t in range(last_plane):
+        for t in range(LAST_PLANE):
             for b in range(B):
                 gather(b, t)
             for b in range(B):
@@ -259,59 +268,76 @@ def tile_attend_gdi_cau_z_kernel(tc, zT, wT, xm, wt, cs, offs, out):
                 lay_slots(b, t)
             if t > 0:
                 quantise_by_slot(0, t - 1)
-        gather(0, last_plane)
-        turn_atoms(0, last_plane)
-        quantise_by_slot(0, last_plane - 1)
-        gather(1, last_plane)
-        round_coefficients(0, 1, SCA)
-        lay_slots(0, last_plane)
-        round_coefficients(1, 1, SCA)
+
+        gather(0, LAST_PLANE)
+        turn_atoms(0, LAST_PLANE)
+        quantise_by_slot(0, LAST_PLANE - 1)
+        gather(1, LAST_PLANE)
+        round_chunk(0)
+        lay_slots(0, LAST_PLANE)
+        round_chunk(1)
         quantise_coefficients(0, 1)
-        quantise_by_slot(0, last_plane)
+        quantise_by_slot(0, LAST_PLANE)
         rebuild(0)
-        for t in range(last_plane):
+        for t in range(LAST_PLANE):
             quantise_by_slot(1, t)
         quantise_coefficients(1, 1)
         rebuild(1)
-        lay_atoms(0, 0, SCA)
-        lay_atoms(0, 1, SCA)
+        lay_features(0, 0, SCA)
+        lay_features(0, 1, SCA)
         residual(0)
         turn_residual(0)
-        turn_atoms(1, last_plane)
-        lay_atoms(1, 0, SCA)
-        round_coefficients(2, 2, VEC)
+        turn_atoms(1, LAST_PLANE)
+        lay_features(1, 0, SCA)
+        round_pair(2)
         residual(1)
         turn_residual(1)
         quantise_coefficients(2, 2)
         rebuild(2)
 
-        fillers = {
-            -1: [(round_coefficients, 4, 2, VEC), (quantise_by_feature, 0, 0), (quantise_coefficients, 4, 2)],
-            0: [(round_coefficients, 6, 2, VEC), (quantise_by_slot, 1, 3), (quantise_by_feature, 0, 1)],
+        preparations = {
+            -1: [(round_pair, 4), (quantise_by_feature, 0, 0), (quantise_coefficients, 4, 2)],
+            0: [(round_pair, 6), (quantise_by_slot, 1, LAST_PLANE), (quantise_by_feature, 0, 1)],
             1: [(quantise_coefficients, 6, 2), (quantise_by_feature, 1, 0)],
-            4: [(lay_atoms, 1, 1, VEC)], 5: [(quantise_by_feature, 1, 1)],
+            4: [(lay_features, 1, 1, VEC)],
+            5: [(quantise_by_feature, 1, 1)],
         }
-        projections = {2: [0], 3: [1], 4: [2], 5: [3], 6: [4], 7: [5], 8: [6], 9: [7]}
-        stores = {3: [(0, [SCA])], 4: [(1, [SCA])], 5: [(2, [SCA])], 7: [(3, [SCA]), (4, [SCA])], 8: [(5, [SCA])], 9: [(6, [VEC]), (7, [SCA, SCA])]}
-        scalar_fillers = {-1: [(lay_slots, 1, 3)]}
-        for period in range(-1, ALL_CHUNKS + 3):
-            def run(stage, ahead, first=0, last=ALL_CHUNKS):
-                if first <= period + ahead < last:
-                    stage(period + ahead)
-            run(square, 1)
-            for filler in scalar_fillers.get(period, []):
-                filler[0](*filler[1:])
-            run(weigh_gap, 0)
-            run(quantise_gradient, -2)
-            for filler in fillers.get(period, []):
-                filler[0](*filler[1:])
-            for k in projections.get(period, []):
-                project(k)
-            run(rebuild, 4, 3)
-            run(inverse, 0)
-            run(root, 1)
-            run(residual, 3, 2)
-            run(turn_residual, 3, 2)
-            run(gradient, -1)
-            for k, engines in stores.get(period, []):
-                store(k, engines)
+
+        def run(stage, k, first=0):
+            if first <= k < ALL_CHUNKS:
+                stage(k)
+
+        residual_lead, gradient_lag, product_lag = 3, 1, 2
+        last_residual = LAST_CHUNK - residual_lead
+        stored = 0
+        for period in range(-1, ALL_CHUNKS + product_lag):
+            run(square, period + 1)
+            if period == -1:
+                lay_slots(1, LAST_PLANE)
+            run(weigh_turned, period)
+            run(weigh, period + 1)
+            run(quantise_gradient, period - product_lag)
+            for step in preparations.get(period, []):
+                step[0](*step[1:])
+            run(project, period - product_lag)
+            run(rebuild, period + residual_lead + 1, first=3)
+            run(inverse, period)
+            run(root, period + 1)
+            run(residual, period + residual_lead, first=2)
+            run(turn_weighed, period + 1)
+            run(turn_residual, period + residual_lead, first=2)
+            run(gradient, period - gradient_lag)
+            if period == product_lag + 1:
+                engine, leaving = SCA, 1
+            elif last_residual < period < LAST_CHUNK:
+                engine, leaving = VEC, 1
+            elif LAST_CHUNK <= period <= ALL_CHUNKS:
+                engine, leaving = SCA, period - product_lag - stored
+            else:
+                engine, leaving = SCA, 0
+            for k in range(stored, stored + leaving):
+                store(k, engine, [nc.sync])
+            stored = stored + leaving
+
+        store(LAST_CHUNK - 1, VEC, [nc.sync])
+        store(LAST_CHUNK, SCA, [nc.sync, nc.scalar])

@@ -28,7 +28,6 @@ RUN = 4
 VEC, SCA = "vector", "scalar"
 RING_BUFS = {VEC: 48, SCA: 18}
 BANKS = 8
-WEIGHED_TURNED = (2, 3)
 SMALLEST_SQUARE = 2.0**-120
 
 
@@ -94,24 +93,14 @@ def tile_attend_gdi_cau_z_kernel(tc, zT, wT, xm, wt, cs, offs, out):
         nc.vector.tensor_tensor(c_sq[:], c_cols[:], c_cols[:], ALU.mult)
         c_safe = keep.tile([P, PACK], F32, name="c_safe")
         nc.vector.tensor_scalar(c_safe[:], c_sq[:], SMALLEST_SQUARE, None, ALU.max)
-        seed = keep.tile([P, PACK], F32, name="seed", tag="first", bufs=2)
+        seed = keep.tile([P, PACK], F32, name="seed")
         nc.scalar.activation(seed[:], c_safe[:], ACT.Abs_reciprocal_sqrt)
         seed_sq = keep.tile([P, PACK], F32, name="seed_sq")
         nc.vector.tensor_tensor(seed_sq[:], seed[:], seed[:], ALU.mult)
-        near_one = keep.tile([P, PACK], F32, name="near_one")
-        nc.vector.tensor_tensor(near_one[:], seed_sq[:], c_safe[:], ALU.mult)
-        newton = keep.tile([P, PACK], F32, name="newton")
-        nc.vector.tensor_scalar(newton[:], near_one[:], -0.5, 1.5, ALU.mult, ALU.add)
-        noise = keep.tile([P, PACK], F32, name="noise")
-        nc.vector.tensor_tensor(noise[:], newton[:], seed[:], ALU.mult)
+        minus_one = keep.tile([P, PACK], F32, name="minus_one")
+        nc.vector.scalar_tensor_tensor(minus_one[:], c_safe[:], -1.0, seed_sq[:], ALU.mult, ALU.mult)
         noise_sq = keep.tile([P, PACK], F32, name="noise_sq")
-        nc.vector.tensor_tensor(noise_sq[:], noise[:], noise[:], ALU.mult)
-
-        wt_wide = keep.tile([P, len(WEIGHED_TURNED), P], F32, name="wt_wide", tag="first", bufs=2)
-        wide_bank = bank_tile("wide_bank")
-        for n, k in enumerate(WEIGHED_TURNED):
-            nc.tensor.transpose(wide_bank[:, n, :], wt_cols[:, k : k + 1].to_broadcast([P, P]), ident[:])
-        nc.scalar.copy(wt_wide[:], wide_bank[:, 0 : len(WEIGHED_TURNED), :])
+        nc.vector.scalar_tensor_tensor(noise_sq[:], minus_one[:], 2.0, seed_sq[:], ALU.add, ALU.mult)
 
         picked = [keep.tile([P, PACK * N], BF16, name=f"picked{b}", align_bytes=64) for b in range(B)]
         feature_codes = [keep.tile([P, N], U32, name=f"feature_codes{b}", align_bytes=64) for b in range(B)]
@@ -210,26 +199,17 @@ def tile_attend_gdi_cau_z_kernel(tc, zT, wT, xm, wt, cs, offs, out):
             made["inverse", k] = ring(SCA, [P, 2, P, 2], F32, "inverse")
             nc.scalar.activation(made["inverse", k][:], made["root", k][:].rearrange("p (u v) m -> p u m v", u=2), ACT.Square)
 
-        def weigh_turned(k):
-            if k in WEIGHED_TURNED:
-                weighed = ring(VEC, [P, P, PACK], F32, "weighed_turned")
-                weights = wt_wide[:, WEIGHED_TURNED.index(k), :].unsqueeze(2).to_broadcast([P, P, PACK])
-                nc.vector.tensor_tensor(weighed[:], made["gap_bank", k][:].rearrange("p t m -> p m t"), weights, ALU.mult)
-                made["numerator", k] = weighed[:].rearrange("p m (u v) -> p m u v", u=2)
-
         def weigh(k):
-            if k not in WEIGHED_TURNED:
-                made["weighed", k] = ring(VEC, [P, D], F32, "weighed")
-                nc.vector.tensor_scalar(made["weighed", k][:].rearrange("m (u v p) -> m u v p", u=2, v=2),
-                                        made["gap", k][:].rearrange("m (u p v) -> m u v p", u=2, v=2),
-                                        wt_cols[:, k : k + 1], None, ALU.mult)
+            made["weighed", k] = ring(VEC, [P, D], F32, "weighed")
+            nc.vector.tensor_scalar(made["weighed", k][:].rearrange("m (u v p) -> m u v p", u=2, v=2),
+                                    made["gap", k][:].rearrange("m (u p v) -> m u v p", u=2, v=2),
+                                    wt_cols[:, k : k + 1], None, ALU.mult)
 
         def turn_weighed(k):
-            if k not in WEIGHED_TURNED:
-                weighed_bank = bank_tile("weighed_bank")
-                for t in range(PACK):
-                    nc.tensor.transpose(weighed_bank[:, t, :], made["weighed", k][:, P * t : P * (t + 1)], ident[:])
-                made["numerator", k] = weighed_bank[:].rearrange("p (u v) m -> p m u v", u=2)
+            weighed_bank = bank_tile("weighed_bank")
+            for t in range(PACK):
+                nc.tensor.transpose(weighed_bank[:, t, :], made["weighed", k][:, P * t : P * (t + 1)], ident[:])
+            made["numerator", k] = weighed_bank[:].rearrange("p (u v) m -> p m u v", u=2)
 
         def gradient(k):
             made["e", k] = ring(VEC, [P, D], BF16, "e")
@@ -314,7 +294,6 @@ def tile_attend_gdi_cau_z_kernel(tc, zT, wT, xm, wt, cs, offs, out):
             run(square, period + 1)
             if period == -1:
                 lay_slots(1, LAST_PLANE)
-            run(weigh_turned, period)
             run(weigh, period + 1)
             run(quantise_gradient, period - product_lag)
             for step in preparations.get(period, []):

@@ -57,8 +57,6 @@ def tile_attend_gdi_cau_z_kernel(tc, zT, wT, xm, wt, cs, offs, out):
         make_identity(nc, ident[:])
         c_cols = keep.tile([P, PACK], F32, name="c_cols")
         nc.scalar.dma_start(out=c_cols[:], in_=cs[0, :].rearrange("(p t) -> p t", t=PACK))
-        nc.scalar.dma_start(out=wt_cols[:].rearrange("m (g j) -> m g j", j=2),
-                            in_=wt.rearrange("b (h m j) o -> m (b h) (j o)", m=P, j=2))
 
         w_planes = wT.rearrange("(p t) c -> p t c", t=PACK)
         planes = {}
@@ -83,6 +81,8 @@ def tile_attend_gdi_cau_z_kernel(tc, zT, wT, xm, wt, cs, offs, out):
             load_plane(t)
         load_coefficients(0, 0, 1)
         load_targets(0, 0)
+        nc.sync.dma_start(out=wt_cols[:].rearrange("m (g j) -> m g j", j=2),
+                          in_=wt.rearrange("b (h m j) o -> m (b h) (j o)", m=P, j=2))
         load_coefficients(0, 1, 1)
         load_coefficients(1, 0, 2)
         load_targets(0, 1)
@@ -103,7 +103,6 @@ def tile_attend_gdi_cau_z_kernel(tc, zT, wT, xm, wt, cs, offs, out):
         nc.vector.scalar_tensor_tensor(noise_sq[:], minus_one[:], 2.0, seed_sq[:], ALU.add, ALU.mult)
 
         picked = [keep.tile([P, PACK * N], BF16, name=f"picked{b}", align_bytes=64) for b in range(B)]
-        feature_codes = [keep.tile([P, N], U32, name=f"feature_codes{b}", align_bytes=64) for b in range(B)]
         feature_scales = [keep.tile([P, N], U8, name=f"feature_scales{b}", align_bytes=64) for b in range(B)]
         first_plane = keep.tile([P, T], BF16, name="first_plane", align_bytes=64)
         made = {}
@@ -140,7 +139,9 @@ def tile_attend_gdi_cau_z_kernel(tc, zT, wT, xm, wt, cs, offs, out):
 
         def quantise_by_feature(b, h):
             cols = slice(HALF * h, HALF * (h + 1))
-            nc.vector.quantize_mx(out=feature_codes[b][:, cols].bitcast(E4M3), scales=feature_scales[b][:, cols],
+            if h == 0:
+                made["feature_codes", b] = ring(VEC, [P, N], U32, "feature_codes")
+            nc.vector.quantize_mx(out=made["feature_codes", b][:, cols].bitcast(E4M3), scales=feature_scales[b][:, cols],
                                   in_=made["by_feature", b, h][:].rearrange("p i t -> p (i t)"))
 
         def round_chunk(k):
@@ -225,7 +226,7 @@ def tile_attend_gdi_cau_z_kernel(tc, zT, wT, xm, wt, cs, offs, out):
             b = k // CHUNKS
             made["sums", k] = bank_tile("sums")
             nc.tensor.matmul_mx(out=made["sums", k][:].rearrange("m a c -> m (a c)"), lhsT=made["e_codes", k][:].bitcast(E5M2),
-                                lhsT_scale=made["e_scales", k][:], rhs=feature_codes[b][:].bitcast(E4M3),
+                                lhsT_scale=made["e_scales", k][:], rhs=made["feature_codes", b][:].bitcast(E4M3),
                                 rhs_scale=feature_scales[b][:], start=True, stop=True)
 
         def store(k, engine, queues):
@@ -246,18 +247,16 @@ def tile_attend_gdi_cau_z_kernel(tc, zT, wT, xm, wt, cs, offs, out):
             for b in range(B):
                 turn_atoms(b, t)
                 lay_slots(b, t)
-            if t > 0:
-                quantise_by_slot(0, t - 1)
 
         gather(0, LAST_PLANE)
         turn_atoms(0, LAST_PLANE)
-        quantise_by_slot(0, LAST_PLANE - 1)
         gather(1, LAST_PLANE)
         round_chunk(0)
         lay_slots(0, LAST_PLANE)
         round_chunk(1)
         quantise_coefficients(0, 1)
-        quantise_by_slot(0, LAST_PLANE)
+        for t in range(PACK):
+            quantise_by_slot(0, t)
         rebuild(0)
         for t in range(LAST_PLANE):
             quantise_by_slot(1, t)

@@ -25,8 +25,11 @@ LAST_CHUNK = ALL_CHUNKS - 1
 LIST_COLS = N // 16
 HALF = 256
 RUN = 4
+LAST_HALVES = [slice(0, P // 2), slice(P // 2, P)]
 VEC, SCA = "vector", "scalar"
-RING_BUFS = {VEC: 48, SCA: 18}
+RING_BUFS = {VEC: 40, SCA: 24}
+WARM_REBUILD = ()
+WARM_PROJECT = ()
 BANKS = 8
 SMALLEST_SQUARE = 2.0**-120
 
@@ -81,11 +84,11 @@ def tile_attend_gdi_cau_z_kernel(tc, zT, wT, xm, wt, cs, offs, out):
             load_plane(t)
         load_coefficients(0, 0, 1)
         load_targets(0, 0)
+        load_coefficients(0, 1, 1)
         nc.sync.dma_start(out=wt_cols[:].rearrange("m (g j) -> m g j", j=2),
                           in_=wt.rearrange("b (h m j) o -> m (b h) (j o)", m=P, j=2))
-        load_coefficients(0, 1, 1)
-        load_coefficients(1, 0, 2)
         load_targets(0, 1)
+        load_coefficients(1, 0, 2)
         load_targets(1, 0)
         load_targets(1, 1)
 
@@ -105,6 +108,7 @@ def tile_attend_gdi_cau_z_kernel(tc, zT, wT, xm, wt, cs, offs, out):
         picked = [keep.tile([P, PACK * N], BF16, name=f"picked{b}", align_bytes=64) for b in range(B)]
         feature_scales = [keep.tile([P, N], U8, name=f"feature_scales{b}", align_bytes=64) for b in range(B)]
         first_plane = keep.tile([P, T], BF16, name="first_plane", align_bytes=64)
+        slot_scales = [keep.tile([P, D], U8, name=f"slot_scales{b}", align_bytes=64) for b in range(B)]
         made = {}
 
         def gather(b, t):
@@ -126,23 +130,24 @@ def tile_attend_gdi_cau_z_kernel(tc, zT, wT, xm, wt, cs, offs, out):
                            made["atom_bank", b, t][:, 0:2, :].rearrange("m u p -> m p u"))
 
         def quantise_by_slot(b, t):
-            codes = ring(VEC, [P, P], U32, "slot_codes")
-            scales = keep.tile([P, P], U8, name=f"slot_scales{b}{t}", align_bytes=64)
-            nc.vector.quantize_mx(out=codes[:].bitcast(E4M3), scales=scales[:], in_=made["by_slot", b, t][:])
-            made["slot", b, t] = (codes, scales)
+            cols = slice(P * t, P * (t + 1))
+            if t == 0:
+                made["slot_codes", b] = ring(VEC, [P, D], U32, "slot_codes")
+            nc.vector.quantize_mx(out=made["slot_codes", b][:, cols].bitcast(E4M3), scales=slot_scales[b][:, cols],
+                                  in_=made["by_slot", b, t][:])
 
-        def lay_features(b, h, engine):
-            made["by_feature", b, h] = ring(engine, [P, HALF, PACK], BF16, "by_feature")
-            runs = HALF // RUN
-            move(engine, made["by_feature", b, h][:].rearrange("p (c i) t -> p c t i", i=RUN),
-                 picked[b][:].rearrange("p (t c i) -> p c t i", t=PACK, i=RUN)[:, runs * h : runs * (h + 1)])
+        def lay_features(b, first, width, engine):
+            made["by_feature", b, first] = ring(engine, [P, width, PACK], BF16, "by_feature")
+            move(engine, made["by_feature", b, first][:].rearrange("p (c i) t -> p c t i", i=RUN),
+                 picked[b][:].rearrange("p (t c i) -> p c t i", t=PACK, i=RUN)[:, first // RUN : (first + width) // RUN])
 
-        def quantise_by_feature(b, h):
-            cols = slice(HALF * h, HALF * (h + 1))
-            if h == 0:
+        def quantise_by_feature(b, first):
+            laid = made["by_feature", b, first]
+            cols = slice(first, first + laid.shape[1])
+            if first == 0:
                 made["feature_codes", b] = ring(VEC, [P, N], U32, "feature_codes")
             nc.vector.quantize_mx(out=made["feature_codes", b][:, cols].bitcast(E4M3), scales=feature_scales[b][:, cols],
-                                  in_=made["by_feature", b, h][:].rearrange("p i t -> p (i t)"))
+                                  in_=laid[:].rearrange("p i t -> p (i t)"))
 
         def round_chunk(k):
             b, c = divmod(k, CHUNKS)
@@ -168,10 +173,15 @@ def tile_attend_gdi_cau_z_kernel(tc, zT, wT, xm, wt, cs, offs, out):
         def rebuild(k):
             made["rec", k] = bank_tile("rec")
             z_codes, z_scales = made["z", k]
-            for t in range(PACK):
-                slot_codes, slot_scales = made["slot", k // CHUNKS, t]
-                nc.tensor.matmul_mx(out=made["rec", k][:, t, :], lhsT=z_codes.bitcast(E4M3), lhsT_scale=z_scales,
-                                    rhs=slot_codes[:].bitcast(E4M3), rhs_scale=slot_scales[:], start=True, stop=True)
+            b = k // CHUNKS
+            width = P if k == 0 else D
+            for repeat in range(2 if k in WARM_REBUILD else 1):
+                for first in range(0, D, width):
+                    cols = slice(first, first + width)
+                    nc.tensor.matmul_mx(out=made["rec", k][:].rearrange("m t p -> m (t p)")[:, cols],
+                                        lhsT=z_codes.bitcast(E4M3), lhsT_scale=z_scales,
+                                        rhs=made["slot_codes", b][:, cols].bitcast(E4M3), rhs_scale=slot_scales[b][:, cols],
+                                        start=True, stop=True)
 
         def residual(k):
             b, c = divmod(k, CHUNKS)
@@ -198,7 +208,13 @@ def tile_attend_gdi_cau_z_kernel(tc, zT, wT, xm, wt, cs, offs, out):
 
         def inverse(k):
             made["inverse", k] = ring(SCA, [P, 2, P, 2], F32, "inverse")
-            nc.scalar.activation(made["inverse", k][:], made["root", k][:].rearrange("p (u v) m -> p u m v", u=2), ACT.Square)
+            root_pairs = made["root", k][:].rearrange("p (u v) m -> p u m v", u=2)
+            if k < LAST_CHUNK:
+                nc.scalar.activation(made["inverse", k][:], root_pairs, ACT.Square)
+            else:
+                for samples in LAST_HALVES:
+                    for u in range(2):
+                        nc.scalar.activation(made["inverse", k][:, u, samples, :], root_pairs[:, u, samples, :], ACT.Square)
 
         def weigh(k):
             made["weighed", k] = ring(VEC, [P, D], F32, "weighed")
@@ -214,8 +230,10 @@ def tile_attend_gdi_cau_z_kernel(tc, zT, wT, xm, wt, cs, offs, out):
 
         def gradient(k):
             made["e", k] = ring(VEC, [P, D], BF16, "e")
-            nc.vector.tensor_tensor(made["e", k][:].rearrange("p (m u v) -> p m u v", u=2, v=2), made["numerator", k],
-                                    made["inverse", k][:].rearrange("p u m v -> p m u v"), ALU.mult)
+            for samples in LAST_HALVES if k == LAST_CHUNK else [slice(0, P)]:
+                nc.vector.tensor_tensor(made["e", k][:].rearrange("p (m u v) -> p m u v", u=2, v=2)[:, samples],
+                                        made["numerator", k][:, samples],
+                                        made["inverse", k][:].rearrange("p u m v -> p m u v")[:, samples], ALU.mult)
 
         def quantise_gradient(k):
             made["e_codes", k] = ring(VEC, [P, P], U32, "e_codes")
@@ -225,9 +243,11 @@ def tile_attend_gdi_cau_z_kernel(tc, zT, wT, xm, wt, cs, offs, out):
         def project(k):
             b = k // CHUNKS
             made["sums", k] = bank_tile("sums")
-            nc.tensor.matmul_mx(out=made["sums", k][:].rearrange("m a c -> m (a c)"), lhsT=made["e_codes", k][:].bitcast(E5M2),
-                                lhsT_scale=made["e_scales", k][:], rhs=made["feature_codes", b][:].bitcast(E4M3),
-                                rhs_scale=feature_scales[b][:], start=True, stop=True)
+            for repeat in range(2 if k in WARM_PROJECT else 1):
+                nc.tensor.matmul_mx(out=made["sums", k][:].rearrange("m a c -> m (a c)"),
+                                    lhsT=made["e_codes", k][:].bitcast(E5M2), lhsT_scale=made["e_scales", k][:],
+                                    rhs=made["feature_codes", b][:].bitcast(E4M3), rhs_scale=feature_scales[b][:],
+                                    start=True, stop=True)
 
         def store(k, engine, queues):
             b, c = divmod(k, CHUNKS)
@@ -252,70 +272,87 @@ def tile_attend_gdi_cau_z_kernel(tc, zT, wT, xm, wt, cs, offs, out):
         turn_atoms(0, LAST_PLANE)
         gather(1, LAST_PLANE)
         round_chunk(0)
-        lay_slots(0, LAST_PLANE)
         round_chunk(1)
+        lay_slots(0, LAST_PLANE)
+        turn_atoms(1, LAST_PLANE)
         quantise_coefficients(0, 1)
-        for t in range(PACK):
+        for t in range(LAST_PLANE):
             quantise_by_slot(0, t)
+        quantise_coefficients(1, 1)
+        quantise_by_slot(0, LAST_PLANE)
         rebuild(0)
+        rebuild(1)
+        lay_features(0, 0, HALF, SCA)
+        lay_features(0, HALF, HALF, SCA)
+        lay_features(1, 0, HALF, SCA)
         for t in range(LAST_PLANE):
             quantise_by_slot(1, t)
-        quantise_coefficients(1, 1)
-        rebuild(1)
-        lay_features(0, 0, SCA)
-        lay_features(0, 1, SCA)
+        lay_features(1, HALF, P, VEC)
         residual(0)
         turn_residual(0)
-        turn_atoms(1, LAST_PLANE)
-        lay_features(1, 0, SCA)
         round_pair(2)
         residual(1)
-        turn_residual(1)
         quantise_coefficients(2, 2)
+        turn_residual(1)
         rebuild(2)
+        rebuild(3)
+        square(0)
+        lay_slots(1, LAST_PLANE)
+        square(1)
+        weigh(0)
+        quantise_by_feature(0, 0)
+        weigh(1)
+        quantise_by_feature(0, HALF)
+        quantise_by_slot(1, LAST_PLANE)
+        lay_features(1, HALF + P, P, VEC)
+        residual(2)
+        turn_weighed(0)
+        turn_residual(2)
+        root(0)
+        root(1)
+        residual(3)
+        round_pair(4)
+        turn_weighed(1)
+        turn_residual(3)
+        inverse(0)
+        weigh(2)
+        quantise_coefficients(4, 2)
+        rebuild(4)
+        rebuild(5)
+        round_pair(6)
+        gradient(0)
 
         preparations = {
-            -1: [(round_pair, 4), (quantise_by_feature, 0, 0), (quantise_coefficients, 4, 2)],
-            0: [(round_pair, 6), (quantise_by_slot, 1, LAST_PLANE), (quantise_by_feature, 0, 1)],
-            1: [(quantise_coefficients, 6, 2), (quantise_by_feature, 1, 0)],
-            4: [(lay_features, 1, 1, VEC)],
-            5: [(quantise_by_feature, 1, 1)],
+            1: [(quantise_coefficients, 6, 2)],
+            2: [(quantise_by_feature, 1, 0)],
+            3: [(quantise_by_feature, 1, HALF), (quantise_by_feature, 1, HALF + P)],
         }
 
         def run(stage, k, first=0):
             if first <= k < ALL_CHUNKS:
                 stage(k)
 
-        residual_lead, gradient_lag, product_lag = 3, 1, 2
-        last_residual = LAST_CHUNK - residual_lead
-        stored = 0
-        for period in range(-1, ALL_CHUNKS + product_lag):
+        last_residual = LAST_CHUNK - 3
+        stores = {3: [(0, SCA)], 4: [(1, VEC)], 5: [(2, VEC)], 6: [(3, VEC)], 7: [(4, SCA), (5, SCA)]}
+        for period in range(1, ALL_CHUNKS + 1):
             run(square, period + 1)
-            if period == -1:
-                lay_slots(1, LAST_PLANE)
-            run(weigh, period + 1)
-            run(quantise_gradient, period - product_lag)
+            run(residual, period + 3)
+            run(quantise_gradient, period - 1)
+            run(weigh, period + 2)
             for step in preparations.get(period, []):
                 step[0](*step[1:])
-            run(project, period - product_lag)
-            run(rebuild, period + residual_lead + 1, first=3)
+            if period <= last_residual:
+                run(turn_weighed, period + 1)
+            run(turn_residual, period + 3)
+            if period >= last_residual:
+                run(turn_weighed, period + 2)
+            run(project, period - 1)
+            run(rebuild, period + 5)
             run(inverse, period)
             run(root, period + 1)
-            run(residual, period + residual_lead, first=2)
-            run(turn_weighed, period + 1)
-            run(turn_residual, period + residual_lead, first=2)
-            run(gradient, period - gradient_lag)
-            if period == product_lag + 1:
-                engine, leaving = SCA, 1
-            elif last_residual < period < LAST_CHUNK:
-                engine, leaving = VEC, 1
-            elif LAST_CHUNK <= period <= ALL_CHUNKS:
-                engine, leaving = SCA, period - product_lag - stored
-            else:
-                engine, leaving = SCA, 0
-            for k in range(stored, stored + leaving):
+            run(gradient, period)
+            for k, engine in stores.get(period, []):
                 store(k, engine, [nc.sync])
-            stored = stored + leaving
 
         store(LAST_CHUNK - 1, VEC, [nc.sync])
         store(LAST_CHUNK, SCA, [nc.sync, nc.scalar])

@@ -54,7 +54,6 @@ def tile_attend_gdi_cau_z_kernel(tc, zT, wT, xm, wt, cs, offs, out):
                 nc.vector.tensor_copy(out=dst, in_=src)
 
         offsets = keep.tile([P, B * LIST_COLS], U16, name="offsets")
-        nc.sync.dma_start(offsets[:], offs)
         wt_cols = keep.tile([P, ALL_CHUNKS], F32, name="wt_cols")
         ident = keep.tile([P, P], F32, name="ident")
         make_identity(nc, ident[:])
@@ -80,7 +79,9 @@ def tile_attend_gdi_cau_z_kernel(tc, zT, wT, xm, wt, cs, offs, out):
             x_raw[b, h] = keep.tile([P, 2, D], F32, name=f"x_raw{b}{h}", align_bytes=64)
             nc.sync.dma_start(out=x_raw[b, h][:], in_=xm[b, HALF * h : HALF * (h + 1), :].rearrange("(m j) d -> m j d", j=2))
 
-        for t in range(PACK):
+        load_plane(0)
+        nc.sync.dma_start(offsets[:], offs)
+        for t in range(1, PACK):
             load_plane(t)
         load_coefficients(0, 0, 1)
         load_targets(0, 0)
@@ -186,15 +187,14 @@ def tile_attend_gdi_cau_z_kernel(tc, zT, wT, xm, wt, cs, offs, out):
         def residual(k):
             b, c = divmod(k, CHUNKS)
             made["gap", k] = ring(VEC, [P, D], F32, "gap")
-            nc.vector.tensor_tensor(made["gap", k][:].rearrange("m (u p v) -> m p u v", u=2, v=2),
-                                    made["rec", k][:].rearrange("m (u v) p -> m p u v", u=2),
-                                    x_raw[b, c // 2][:, c % 2, :].rearrange("m (p u v) -> m p u v", u=2, v=2), ALU.subtract)
+            nc.vector.tensor_tensor(made["gap", k][:].rearrange("m (t c i) -> m c t i", t=PACK, i=2),
+                                    made["rec", k][:].rearrange("m t (c i) -> m c t i", i=2),
+                                    x_raw[b, c // 2][:, c % 2, :].rearrange("m (c i t) -> m c t i", t=PACK, i=2), ALU.subtract)
 
         def turn_residual(k):
             made["gap_bank", k] = bank_tile("gap_bank")
             for t in range(PACK):
-                u, v = divmod(t, 2)
-                nc.tensor.transpose(made["gap_bank", k][:, t, :], made["gap", k][:, HALF * u + v : HALF * (u + 1) : 2], ident[:])
+                nc.tensor.transpose(made["gap_bank", k][:, t, :], made["gap", k][:, P * t : P * (t + 1)], ident[:])
 
         def square(k):
             made["gap_sq", k] = ring(SCA, [P, PACK, P], F32, "gap_sq")
@@ -218,9 +218,7 @@ def tile_attend_gdi_cau_z_kernel(tc, zT, wT, xm, wt, cs, offs, out):
 
         def weigh(k):
             made["weighed", k] = ring(VEC, [P, D], F32, "weighed")
-            nc.vector.tensor_scalar(made["weighed", k][:].rearrange("m (u v p) -> m u v p", u=2, v=2),
-                                    made["gap", k][:].rearrange("m (u p v) -> m u v p", u=2, v=2),
-                                    wt_cols[:, k : k + 1], None, ALU.mult)
+            nc.vector.tensor_scalar(made["weighed", k][:], made["gap", k][:], wt_cols[:, k : k + 1], None, ALU.mult)
 
         def turn_weighed(k):
             weighed_bank = bank_tile("weighed_bank")
@@ -228,12 +226,12 @@ def tile_attend_gdi_cau_z_kernel(tc, zT, wT, xm, wt, cs, offs, out):
                 nc.tensor.transpose(weighed_bank[:, t, :], made["weighed", k][:, P * t : P * (t + 1)], ident[:])
             made["numerator", k] = weighed_bank[:].rearrange("p (u v) m -> p m u v", u=2)
 
-        def gradient(k):
-            made["e", k] = ring(VEC, [P, D], BF16, "e")
-            for samples in LAST_HALVES if k == LAST_CHUNK else [slice(0, P)]:
-                nc.vector.tensor_tensor(made["e", k][:].rearrange("p (m u v) -> p m u v", u=2, v=2)[:, samples],
-                                        made["numerator", k][:, samples],
-                                        made["inverse", k][:].rearrange("p u m v -> p m u v")[:, samples], ALU.mult)
+        def gradient(k, samples=slice(0, P)):
+            if samples.start == 0:
+                made["e", k] = ring(VEC, [P, D], BF16, "e")
+            nc.vector.tensor_tensor(made["e", k][:].rearrange("p (m u v) -> p m u v", u=2, v=2)[:, samples],
+                                    made["numerator", k][:, samples],
+                                    made["inverse", k][:].rearrange("p u m v -> p m u v")[:, samples], ALU.mult)
 
         def quantise_gradient(k):
             made["e_codes", k] = ring(VEC, [P, P], U32, "e_codes")
@@ -249,16 +247,12 @@ def tile_attend_gdi_cau_z_kernel(tc, zT, wT, xm, wt, cs, offs, out):
                                     rhs=made["feature_codes", b][:].bitcast(E4M3), rhs_scale=feature_scales[b][:],
                                     start=True, stop=True)
 
-        def store(k, engine, queues):
+        def store(k, engine, queue, cols=slice(0, N)):
             b, c = divmod(k, CHUNKS)
             rows = out[b, HALF * (c // 2) : HALF * (c // 2 + 1), :].rearrange("(m j) i -> m j i", j=2)[:, c % 2, :]
-            sums = made["sums", k][:].rearrange("m a c -> m (a c)")
-            width = N // len(queues)
-            staged = ring(engine, [P, N], F32, "staged")
-            for n, queue in enumerate(queues):
-                cols = slice(width * n, width * (n + 1))
-                move(engine, staged[:, cols], sums[:, cols])
-                queue.dma_start(out=rows[:, cols], in_=staged[:, cols])
+            staged = ring(engine, [P, cols.stop - cols.start], F32, "staged")
+            move(engine, staged[:], made["sums", k][:].rearrange("m a c -> m (a c)")[:, cols])
+            queue.dma_start(out=rows[:, cols], in_=staged[:])
 
         nc.vector.tensor_copy(first_plane[:], planes[0][:])
         for t in range(LAST_PLANE):
@@ -333,8 +327,8 @@ def tile_attend_gdi_cau_z_kernel(tc, zT, wT, xm, wt, cs, offs, out):
                 stage(k)
 
         last_residual = LAST_CHUNK - 3
-        stores = {3: [(0, SCA)], 4: [(1, VEC)], 5: [(2, VEC)], 6: [(3, VEC)], 7: [(4, SCA), (5, SCA)]}
-        for period in range(1, ALL_CHUNKS + 1):
+        stores = {3: [(0, SCA)], 4: [(1, VEC)], 5: [(2, VEC)]}
+        for period in range(1, LAST_CHUNK):
             run(square, period + 1)
             run(residual, period + 3)
             run(quantise_gradient, period - 1)
@@ -352,7 +346,17 @@ def tile_attend_gdi_cau_z_kernel(tc, zT, wT, xm, wt, cs, offs, out):
             run(root, period + 1)
             run(gradient, period)
             for k, engine in stores.get(period, []):
-                store(k, engine, [nc.sync])
+                store(k, engine, nc.sync)
 
-        store(LAST_CHUNK - 1, VEC, [nc.sync])
-        store(LAST_CHUNK, SCA, [nc.sync, nc.scalar])
+        inverse(LAST_CHUNK)
+        gradient(LAST_CHUNK, LAST_HALVES[0])
+        quantise_gradient(LAST_CHUNK - 1)
+        project(LAST_CHUNK - 1)
+        gradient(LAST_CHUNK, LAST_HALVES[1])
+        for k in range(3, LAST_CHUNK - 1):
+            store(k, SCA, nc.sync)
+        quantise_gradient(LAST_CHUNK)
+        project(LAST_CHUNK)
+        store(LAST_CHUNK - 1, VEC, nc.sync)
+        store(LAST_CHUNK, SCA, nc.sync, slice(0, HALF))
+        store(LAST_CHUNK, SCA, nc.scalar, slice(HALF, N))

@@ -127,8 +127,8 @@ def tile_attend_gdi_cau_z_kernel(tc, zT, wT, xm, wt, cs, offs, out):
 
         def lay_slots(b, t):
             made["by_slot", b, t] = ring(SCA, [P, N], BF16, "by_slot")
-            nc.scalar.copy(made["by_slot", b, t][:].bitcast(F32).rearrange("m (p u) -> m p u", u=2),
-                           made["atom_bank", b, t][:, 0:2, :].rearrange("m u p -> m p u"))
+            nc.scalar.copy(made["by_slot", b, t][:].bitcast(F32).rearrange("m (c i u) -> m c u i", i=2, u=2),
+                           made["atom_bank", b, t][:, 0:2, :].rearrange("m u (c i) -> m c u i", i=2))
 
         def quantise_by_slot(b, t):
             cols = slice(P * t, P * (t + 1))
@@ -207,14 +207,14 @@ def tile_attend_gdi_cau_z_kernel(tc, zT, wT, xm, wt, cs, offs, out):
                                      bias=noise_sq[:, t : t + 1])
 
         def inverse(k):
-            made["inverse", k] = ring(SCA, [P, 2, P, 2], F32, "inverse")
-            root_pairs = made["root", k][:].rearrange("p (u v) m -> p u m v", u=2)
+            made["inverse", k] = ring(SCA, [P, PACK, P], F32, "inverse")
             if k < LAST_CHUNK:
-                nc.scalar.activation(made["inverse", k][:], root_pairs, ACT.Square)
+                nc.scalar.activation(made["inverse", k][:], made["root", k][:], ACT.Square)
             else:
                 for samples in LAST_HALVES:
-                    for u in range(2):
-                        nc.scalar.activation(made["inverse", k][:, u, samples, :], root_pairs[:, u, samples, :], ACT.Square)
+                    for planes_now in (slice(0, 2), slice(2, PACK)):
+                        nc.scalar.activation(made["inverse", k][:, planes_now, samples], made["root", k][:, planes_now, samples],
+                                             ACT.Square)
 
         def weigh(k):
             made["weighed", k] = ring(VEC, [P, D], F32, "weighed")
@@ -224,14 +224,14 @@ def tile_attend_gdi_cau_z_kernel(tc, zT, wT, xm, wt, cs, offs, out):
             weighed_bank = bank_tile("weighed_bank")
             for t in range(PACK):
                 nc.tensor.transpose(weighed_bank[:, t, :], made["weighed", k][:, P * t : P * (t + 1)], ident[:])
-            made["numerator", k] = weighed_bank[:].rearrange("p (u v) m -> p m u v", u=2)
+            made["numerator", k] = weighed_bank
 
         def gradient(k, samples=slice(0, P)):
             if samples.start == 0:
                 made["e", k] = ring(VEC, [P, D], BF16, "e")
-            nc.vector.tensor_tensor(made["e", k][:].rearrange("p (m u v) -> p m u v", u=2, v=2)[:, samples],
-                                    made["numerator", k][:, samples],
-                                    made["inverse", k][:].rearrange("p u m v -> p m u v")[:, samples], ALU.mult)
+            nc.vector.tensor_tensor(made["e", k][:].rearrange("p (m t) -> p m t", t=PACK)[:, samples].rearrange("p (c i) t -> p c t i", i=2),
+                                    made["numerator", k][:, :, samples].rearrange("p t (c i) -> p c t i", i=2),
+                                    made["inverse", k][:, :, samples].rearrange("p t (c i) -> p c t i", i=2), ALU.mult)
 
         def quantise_gradient(k):
             made["e_codes", k] = ring(VEC, [P, P], U32, "e_codes")

@@ -27,11 +27,11 @@ HALF = 256
 RUN = 4
 LAST_HALVES = [slice(0, P // 2), slice(P // 2, P)]
 VEC, SCA = "vector", "scalar"
-RING_BUFS = {VEC: 40, SCA: 24}
+RING_BUFS = {VEC: 36, SCA: 30}
 WARM_REBUILD = ()
 WARM_PROJECT = ()
 BANKS = 8
-SMALLEST_SQUARE = 2.0**-120
+SMALLEST_CS = 2.0**-60
 
 
 def tile_attend_gdi_cau_z_kernel(tc, zT, wT, xm, wt, cs, offs, out):
@@ -58,7 +58,6 @@ def tile_attend_gdi_cau_z_kernel(tc, zT, wT, xm, wt, cs, offs, out):
         ident = keep.tile([P, P], F32, name="ident")
         make_identity(nc, ident[:])
         c_cols = keep.tile([P, PACK], F32, name="c_cols")
-        nc.scalar.dma_start(out=c_cols[:], in_=cs[0, :].rearrange("(p t) -> p t", t=PACK))
 
         w_planes = wT.rearrange("(p t) c -> p t c", t=PACK)
         planes = {}
@@ -80,6 +79,7 @@ def tile_attend_gdi_cau_z_kernel(tc, zT, wT, xm, wt, cs, offs, out):
             nc.sync.dma_start(out=x_raw[b, h][:], in_=xm[b, HALF * h : HALF * (h + 1), :].rearrange("(m j) d -> m j d", j=2))
 
         load_plane(0)
+        nc.sync.dma_start(out=c_cols[:], in_=cs[0, :].rearrange("(p t) -> p t", t=PACK))
         nc.sync.dma_start(offsets[:], offs)
         for t in range(1, PACK):
             load_plane(t)
@@ -93,22 +93,17 @@ def tile_attend_gdi_cau_z_kernel(tc, zT, wT, xm, wt, cs, offs, out):
         load_targets(1, 0)
         load_targets(1, 1)
 
-        c_sq = keep.tile([P, PACK], F32, name="c_sq")
-        nc.vector.tensor_tensor(c_sq[:], c_cols[:], c_cols[:], ALU.mult)
-        c_safe = keep.tile([P, PACK], F32, name="c_safe")
-        nc.vector.tensor_scalar(c_safe[:], c_sq[:], SMALLEST_SQUARE, None, ALU.max)
         seed = keep.tile([P, PACK], F32, name="seed")
-        nc.scalar.activation(seed[:], c_safe[:], ACT.Abs_reciprocal_sqrt)
+        nc.scalar.activation(seed[:], c_cols[:], ACT.Abs_reciprocal_sqrt, bias=SMALLEST_CS)
+        c_sq = keep.tile([P, PACK], F32, name="c_sq")
+        nc.scalar.activation(c_sq[:], c_cols[:], ACT.Square)
         seed_sq = keep.tile([P, PACK], F32, name="seed_sq")
-        nc.vector.tensor_tensor(seed_sq[:], seed[:], seed[:], ALU.mult)
-        minus_one = keep.tile([P, PACK], F32, name="minus_one")
-        nc.vector.scalar_tensor_tensor(minus_one[:], c_safe[:], -1.0, seed_sq[:], ALU.mult, ALU.mult)
-        noise_sq = keep.tile([P, PACK], F32, name="noise_sq")
-        nc.vector.scalar_tensor_tensor(noise_sq[:], minus_one[:], 2.0, seed_sq[:], ALU.add, ALU.mult)
+        nc.scalar.activation(seed_sq[:], seed[:], ACT.Square)
+        guess = keep.tile([P, PACK], F32, name="guess")
+        nc.scalar.activation(guess[:], seed_sq[:], ACT.Square)
 
         picked = [keep.tile([P, PACK * N], BF16, name=f"picked{b}", align_bytes=64) for b in range(B)]
         feature_scales = [keep.tile([P, N], U8, name=f"feature_scales{b}", align_bytes=64) for b in range(B)]
-        first_plane = keep.tile([P, T], BF16, name="first_plane", align_bytes=64)
         slot_scales = [keep.tile([P, D], U8, name=f"slot_scales{b}", align_bytes=64) for b in range(B)]
         made = {}
 
@@ -142,6 +137,12 @@ def tile_attend_gdi_cau_z_kernel(tc, zT, wT, xm, wt, cs, offs, out):
             move(engine, made["by_feature", b, first][:].rearrange("p (c i) t -> p c t i", i=RUN),
                  picked[b][:].rearrange("p (t c i) -> p c t i", t=PACK, i=RUN)[:, first // RUN : (first + width) // RUN])
 
+        def lay_pair(h, u, engine):
+            if u == 0:
+                made["by_feature", 0, HALF * h] = ring(engine, [P, HALF, PACK], BF16, "by_feature")
+            pair = picked[0][:, 2 * N * u : 2 * N * (u + 1)].rearrange("p (v i) -> p i v", v=2)
+            move(engine, made["by_feature", 0, HALF * h][:, :, 2 * u : 2 * u + 2], pair[:, HALF * h : HALF * (h + 1), :])
+
         def quantise_by_feature(b, first):
             laid = made["by_feature", b, first]
             cols = slice(first, first + laid.shape[1])
@@ -157,11 +158,11 @@ def tile_attend_gdi_cau_z_kernel(tc, zT, wT, xm, wt, cs, offs, out):
             nc.scalar.activation(made["z_bf", k][:].rearrange("p (c i) t -> p c t i", i=RUN),
                                  samples.rearrange("p t (c i) -> p c t i", i=RUN), ACT.Copy)
 
-        def round_pair(k):
+        def round_pair(k, engine=VEC):
             b, c = divmod(k, CHUNKS)
-            made["z_bf", k] = ring(VEC, [P, 2 * P, PACK], BF16, "z_bf")
-            nc.vector.tensor_copy(out=made["z_bf", k][:].rearrange("p (j c i) t -> p c t i j", j=2, i=2),
-                                  in_=z_raw[b, c // 2].rearrange("p t (c i j) -> p c t i j", i=2, j=2))
+            made["z_bf", k] = ring(engine, [P, 2 * P, PACK], BF16, "z_bf")
+            move(engine, made["z_bf", k][:].rearrange("p (j c i) t -> p c t i j", j=2, i=2),
+                 z_raw[b, c // 2].rearrange("p t (c i j) -> p c t i j", i=2, j=2))
 
         def quantise_coefficients(k, count):
             codes = ring(VEC, [P, count * P], U32, "z_codes")
@@ -254,13 +255,18 @@ def tile_attend_gdi_cau_z_kernel(tc, zT, wT, xm, wt, cs, offs, out):
             move(engine, staged[:], made["sums", k][:].rearrange("m a c -> m (a c)")[:, cols])
             queue.dma_start(out=rows[:, cols], in_=staged[:])
 
+        first_plane = keep.tile([P, T], BF16, name="first_plane", align_bytes=64)
         nc.vector.tensor_copy(first_plane[:], planes[0][:])
         for t in range(LAST_PLANE):
             for b in range(B):
-                gather(b, t)
+                if (b, t) != (0, 1):
+                    gather(b, t)
             for b in range(B):
                 turn_atoms(b, t)
                 lay_slots(b, t)
+            if t == 0:
+                gather(0, 1)
+                lay_pair(0, 0, SCA)
 
         gather(0, LAST_PLANE)
         turn_atoms(0, LAST_PLANE)
@@ -269,6 +275,7 @@ def tile_attend_gdi_cau_z_kernel(tc, zT, wT, xm, wt, cs, offs, out):
         round_chunk(1)
         lay_slots(0, LAST_PLANE)
         turn_atoms(1, LAST_PLANE)
+        lay_pair(0, 1, VEC)
         quantise_coefficients(0, 1)
         for t in range(LAST_PLANE):
             quantise_by_slot(0, t)
@@ -276,15 +283,18 @@ def tile_attend_gdi_cau_z_kernel(tc, zT, wT, xm, wt, cs, offs, out):
         quantise_by_slot(0, LAST_PLANE)
         rebuild(0)
         rebuild(1)
-        lay_features(0, 0, HALF, SCA)
         lay_features(0, HALF, HALF, SCA)
+        round_pair(2, SCA)
         lay_features(1, 0, HALF, SCA)
+        minus_one = ring(VEC, [P, PACK], F32, "minus_one")
+        nc.vector.scalar_tensor_tensor(minus_one[:], c_sq[:], -1.0, guess[:], ALU.mult, ALU.mult)
         for t in range(LAST_PLANE):
             quantise_by_slot(1, t)
+        noise_sq = keep.tile([P, PACK], F32, name="noise_sq")
+        nc.vector.scalar_tensor_tensor(noise_sq[:], minus_one[:], 2.0, guess[:], ALU.add, ALU.mult)
         lay_features(1, HALF, P, VEC)
         residual(0)
         turn_residual(0)
-        round_pair(2)
         residual(1)
         quantise_coefficients(2, 2)
         turn_residual(1)

@@ -24,12 +24,12 @@ ALL_CHUNKS = B * CHUNKS
 LAST_CHUNK = ALL_CHUNKS - 1
 LIST_COLS = N // 16
 HALF = 256
+SHARE = 320
 RUN = 4
 LAST_HALVES = [slice(0, P // 2), slice(P // 2, P)]
 VEC, SCA = "vector", "scalar"
-RING_BUFS = {VEC: 36, SCA: 30}
-WARM_REBUILD = ()
-WARM_PROJECT = ()
+RING_BUFS = {VEC: 40, SCA: 24}
+PLANE_BUFS = 3
 BANKS = 8
 SMALLEST_CS = 2.0**-60
 
@@ -65,7 +65,7 @@ def tile_attend_gdi_cau_z_kernel(tc, zT, wT, xm, wt, cs, offs, out):
         x_raw = {}
 
         def load_plane(t):
-            planes[t] = keep.tile([P, T], F32, name=f"plane{t}", align_bytes=64)
+            planes[t] = work.tile([P, T], F32, name="plane", tag="plane", bufs=PLANE_BUFS, align_bytes=64)
             nc.sync.dma_start(out=planes[t][:], in_=w_planes[:, t, :])
 
         def load_coefficients(b, h, halves):
@@ -81,38 +81,42 @@ def tile_attend_gdi_cau_z_kernel(tc, zT, wT, xm, wt, cs, offs, out):
         load_plane(0)
         nc.sync.dma_start(out=c_cols[:], in_=cs[0, :].rearrange("(p t) -> p t", t=PACK))
         nc.sync.dma_start(offsets[:], offs)
-        for t in range(1, PACK):
+        for t in range(1, LAST_PLANE):
             load_plane(t)
-        load_coefficients(0, 0, 1)
-        load_targets(0, 0)
-        load_coefficients(0, 1, 1)
-        nc.sync.dma_start(out=wt_cols[:].rearrange("m (g j) -> m g j", j=2),
-                          in_=wt.rearrange("b (h m j) o -> m (b h) (j o)", m=P, j=2))
-        load_targets(0, 1)
-        load_coefficients(1, 0, 2)
-        load_targets(1, 0)
-        load_targets(1, 1)
+
+        def load_the_rest():
+            load_plane(LAST_PLANE)
+            load_coefficients(0, 0, 1)
+            load_targets(0, 0)
+            load_coefficients(0, 1, 1)
+            nc.sync.dma_start(out=wt_cols[:].rearrange("m (g j) -> m g j", j=2),
+                              in_=wt.rearrange("b (h m j) o -> m (b h) (j o)", m=P, j=2))
+            load_targets(0, 1)
+            load_coefficients(1, 0, 2)
+            load_targets(1, 0)
+            load_targets(1, 1)
 
         seed = keep.tile([P, PACK], F32, name="seed")
-        nc.scalar.activation(seed[:], c_cols[:], ACT.Abs_reciprocal_sqrt, bias=SMALLEST_CS)
         c_sq = keep.tile([P, PACK], F32, name="c_sq")
-        nc.scalar.activation(c_sq[:], c_cols[:], ACT.Square)
         seed_sq = keep.tile([P, PACK], F32, name="seed_sq")
-        nc.scalar.activation(seed_sq[:], seed[:], ACT.Square)
         guess = keep.tile([P, PACK], F32, name="guess")
-        nc.scalar.activation(guess[:], seed_sq[:], ACT.Square)
+        nc.scalar.activation(seed[:], c_cols[:], ACT.Abs_reciprocal_sqrt, bias=SMALLEST_CS)
+
+        def small_steps():
+            nc.scalar.activation(c_sq[:], c_cols[:], ACT.Square)
+            nc.scalar.activation(seed_sq[:], seed[:], ACT.Square)
+            nc.scalar.activation(guess[:], seed_sq[:], ACT.Square)
 
         picked = [keep.tile([P, PACK * N], BF16, name=f"picked{b}", align_bytes=64) for b in range(B)]
-        feature_scales = [keep.tile([P, N], U8, name=f"feature_scales{b}", align_bytes=64) for b in range(B)]
-        slot_scales = [keep.tile([P, D], U8, name=f"slot_scales{b}", align_bytes=64) for b in range(B)]
         made = {}
 
-        def gather(b, t):
-            listed = offsets[:, b * LIST_COLS : (b + 1) * LIST_COLS]
-            if t == 0:
-                nc.scalar.activation(picked[b][:, 0:N], first_plane[:].indirect(listed), ACT.Copy)
+        def gather(b, t, engine, first=0, width=N):
+            listed = offsets[:, (b * N + first) // 16 : (b * N + first + width) // 16]
+            dst = picked[b][:, N * t + first : N * t + first + width]
+            if engine == SCA:
+                nc.scalar.activation(dst, planes[t][:].indirect(listed), ACT.Copy)
             else:
-                nc.vector.tensor_copy(picked[b][:, N * t : N * (t + 1)], planes[t][:].indirect(listed))
+                nc.vector.tensor_copy(dst, planes[t][:].indirect(listed))
 
         def turn_atoms(b, t):
             made["atom_bank", b, t] = bank_tile("atom_bank")
@@ -121,42 +125,37 @@ def tile_attend_gdi_cau_z_kernel(tc, zT, wT, xm, wt, cs, offs, out):
                 nc.tensor.transpose(made["atom_bank", b, t][:, u, :], words[:, u : N // 2 : 2], ident[:])
 
         def lay_slots(b, t):
-            made["by_slot", b, t] = ring(SCA, [P, N], BF16, "by_slot")
+            if t == 0:
+                made["by_slot", b, t] = picked[b][:, 2 * N : 3 * N]
+            else:
+                made["by_slot", b, t] = ring(SCA, [P, N], BF16, "by_slot")
             nc.scalar.copy(made["by_slot", b, t][:].bitcast(F32).rearrange("m (c i u) -> m c u i", i=2, u=2),
                            made["atom_bank", b, t][:, 0:2, :].rearrange("m u (c i) -> m c u i", i=2))
 
         def quantise_by_slot(b, t):
-            cols = slice(P * t, P * (t + 1))
-            if t == 0:
-                made["slot_codes", b] = ring(VEC, [P, D], U32, "slot_codes")
-            nc.vector.quantize_mx(out=made["slot_codes", b][:, cols].bitcast(E4M3), scales=slot_scales[b][:, cols],
-                                  in_=made["by_slot", b, t][:])
+            codes = ring(VEC, [P, P], U32, "slot_codes")
+            scales = keep.tile([P, P], U8, name=f"slot_scales{b}{t}", align_bytes=64)
+            nc.vector.quantize_mx(out=codes[:].bitcast(E4M3), scales=scales[:], in_=made["by_slot", b, t][:])
+            made["slot_codes", b, t] = (codes, scales)
 
         def lay_features(b, first, width, engine):
             made["by_feature", b, first] = ring(engine, [P, width, PACK], BF16, "by_feature")
             move(engine, made["by_feature", b, first][:].rearrange("p (c i) t -> p c t i", i=RUN),
                  picked[b][:].rearrange("p (t c i) -> p c t i", t=PACK, i=RUN)[:, first // RUN : (first + width) // RUN])
 
-        def lay_pair(h, u, engine):
-            if u == 0:
-                made["by_feature", 0, HALF * h] = ring(engine, [P, HALF, PACK], BF16, "by_feature")
-            pair = picked[0][:, 2 * N * u : 2 * N * (u + 1)].rearrange("p (v i) -> p i v", v=2)
-            move(engine, made["by_feature", 0, HALF * h][:, :, 2 * u : 2 * u + 2], pair[:, HALF * h : HALF * (h + 1), :])
-
         def quantise_by_feature(b, first):
             laid = made["by_feature", b, first]
-            cols = slice(first, first + laid.shape[1])
-            if first == 0:
-                made["feature_codes", b] = ring(VEC, [P, N], U32, "feature_codes")
-            nc.vector.quantize_mx(out=made["feature_codes", b][:, cols].bitcast(E4M3), scales=feature_scales[b][:, cols],
-                                  in_=laid[:].rearrange("p i t -> p (i t)"))
+            width = laid.shape[1]
+            codes = ring(VEC, [P, width], U32, "feature_codes")
+            scales = keep.tile([P, width], U8, name=f"feature_scales{b}{first}", align_bytes=64)
+            nc.vector.quantize_mx(out=codes[:].bitcast(E4M3), scales=scales[:], in_=laid[:].rearrange("p i t -> p (i t)"))
+            made.setdefault(("feature_codes", b), []).append((slice(first, first + width), codes, scales))
 
-        def round_chunk(k):
+        def round_chunk(k, engine):
             b, c = divmod(k, CHUNKS)
-            made["z_bf", k] = ring(SCA, [P, P, PACK], BF16, "z_bf")
+            made["z_bf", k] = ring(engine, [P, P, PACK], BF16, "z_bf")
             samples = z_raw[b, c // 2].rearrange("p t (m j) -> p t m j", j=2)[:, :, :, c % 2]
-            nc.scalar.activation(made["z_bf", k][:].rearrange("p (c i) t -> p c t i", i=RUN),
-                                 samples.rearrange("p t (c i) -> p c t i", i=RUN), ACT.Copy)
+            move(engine, made["z_bf", k][:].rearrange("p (c i) t -> p c t i", i=RUN), samples.rearrange("p t (c i) -> p c t i", i=RUN))
 
         def round_pair(k, engine=VEC):
             b, c = divmod(k, CHUNKS)
@@ -176,14 +175,10 @@ def tile_attend_gdi_cau_z_kernel(tc, zT, wT, xm, wt, cs, offs, out):
             made["rec", k] = bank_tile("rec")
             z_codes, z_scales = made["z", k]
             b = k // CHUNKS
-            width = P if k == 0 else D
-            for repeat in range(2 if k in WARM_REBUILD else 1):
-                for first in range(0, D, width):
-                    cols = slice(first, first + width)
-                    nc.tensor.matmul_mx(out=made["rec", k][:].rearrange("m t p -> m (t p)")[:, cols],
-                                        lhsT=z_codes.bitcast(E4M3), lhsT_scale=z_scales,
-                                        rhs=made["slot_codes", b][:, cols].bitcast(E4M3), rhs_scale=slot_scales[b][:, cols],
-                                        start=True, stop=True)
+            for t in (0, 1, LAST_PLANE, 2):
+                codes, scales = made["slot_codes", b, t]
+                nc.tensor.matmul_mx(out=made["rec", k][:, t, :], lhsT=z_codes.bitcast(E4M3), lhsT_scale=z_scales,
+                                    rhs=codes[:].bitcast(E4M3), rhs_scale=scales[:], start=True, stop=True)
 
         def residual(k):
             b, c = divmod(k, CHUNKS)
@@ -199,7 +194,8 @@ def tile_attend_gdi_cau_z_kernel(tc, zT, wT, xm, wt, cs, offs, out):
 
         def square(k):
             made["gap_sq", k] = ring(SCA, [P, PACK, P], F32, "gap_sq")
-            nc.scalar.activation(made["gap_sq", k][:], made["gap_bank", k][:], ACT.Square)
+            for planes_now in ([slice(0, 2), slice(2, PACK)] if k == 0 else [slice(0, PACK)]):
+                nc.scalar.activation(made["gap_sq", k][:, planes_now], made["gap_bank", k][:, planes_now], ACT.Square)
 
         def root(k):
             made["root", k] = ring(SCA, [P, PACK, P], F32, "root")
@@ -239,134 +235,180 @@ def tile_attend_gdi_cau_z_kernel(tc, zT, wT, xm, wt, cs, offs, out):
             made["e_scales", k] = keep.tile([P, P], U8, name=f"e_scales{k}", align_bytes=64)
             nc.vector.quantize_mx(out=made["e_codes", k][:].bitcast(E5M2), scales=made["e_scales", k][:], in_=made["e", k][:])
 
-        def project(k):
-            b = k // CHUNKS
-            made["sums", k] = bank_tile("sums")
-            for repeat in range(2 if k in WARM_PROJECT else 1):
-                nc.tensor.matmul_mx(out=made["sums", k][:].rearrange("m a c -> m (a c)"),
-                                    lhsT=made["e_codes", k][:].bitcast(E5M2), lhsT_scale=made["e_scales", k][:],
-                                    rhs=made["feature_codes", b][:].bitcast(E4M3), rhs_scale=feature_scales[b][:],
-                                    start=True, stop=True)
+        def project(k, part=slice(0, N)):
+            made["sums", k, part.start] = bank_tile("sums")
+            for cols, codes, scales in made["feature_codes", k // CHUNKS]:
+                if part.start <= cols.start < part.stop:
+                    nc.tensor.matmul_mx(out=made["sums", k, part.start][:].rearrange("m a c -> m (a c)")[:, cols],
+                                        lhsT=made["e_codes", k][:].bitcast(E5M2), lhsT_scale=made["e_scales", k][:],
+                                        rhs=codes[:].bitcast(E4M3), rhs_scale=scales[:], start=True, stop=True)
 
         def store(k, engine, queue, cols=slice(0, N)):
             b, c = divmod(k, CHUNKS)
             rows = out[b, HALF * (c // 2) : HALF * (c // 2 + 1), :].rearrange("(m j) i -> m j i", j=2)[:, c % 2, :]
             staged = ring(engine, [P, cols.stop - cols.start], F32, "staged")
-            move(engine, staged[:], made["sums", k][:].rearrange("m a c -> m (a c)")[:, cols])
+            move(engine, staged[:], made["sums", k, cols.start][:].rearrange("m a c -> m (a c)")[:, cols])
             queue.dma_start(out=rows[:, cols], in_=staged[:])
 
-        first_plane = keep.tile([P, T], BF16, name="first_plane", align_bytes=64)
-        nc.vector.tensor_copy(first_plane[:], planes[0][:])
-        for t in range(LAST_PLANE):
-            for b in range(B):
-                if (b, t) != (0, 1):
-                    gather(b, t)
-            for b in range(B):
-                turn_atoms(b, t)
-                lay_slots(b, t)
-            if t == 0:
-                gather(0, 1)
-                lay_pair(0, 0, SCA)
-
-        gather(0, LAST_PLANE)
+        gather(0, 0, VEC)
+        gather(1, 0, VEC, 0, P)
+        gather(1, 0, SCA, P, N - P)
+        load_the_rest()
+        small_steps()
+        gather(0, 1, VEC)
+        gather(1, 1, VEC, 0, P)
+        gather(1, 1, SCA, P, N - P)
+        turn_atoms(0, 0)
+        lay_slots(0, 0)
+        turn_atoms(1, 0)
+        lay_slots(1, 0)
+        quantise_by_slot(0, 0)
+        quantise_by_slot(1, 0)
+        turn_atoms(0, 1)
+        lay_slots(0, 1)
+        turn_atoms(1, 1)
+        lay_slots(1, 1)
+        gather(0, 2, VEC)
+        gather(1, 2, VEC, 0, P)
+        gather(1, 2, SCA, P, N - P)
+        quantise_by_slot(0, 1)
+        quantise_by_slot(1, 1)
+        turn_atoms(0, 2)
+        turn_atoms(1, 2)
+        gather(0, LAST_PLANE, VEC, 0, SHARE)
+        gather(0, LAST_PLANE, SCA, SHARE, N - SHARE)
+        gather(1, LAST_PLANE, VEC, 0, HALF)
+        gather(1, LAST_PLANE, SCA, HALF, HALF)
         turn_atoms(0, LAST_PLANE)
-        gather(1, LAST_PLANE)
-        round_chunk(0)
-        round_chunk(1)
         lay_slots(0, LAST_PLANE)
+        lay_slots(0, 2)
+        lay_slots(1, 2)
         turn_atoms(1, LAST_PLANE)
-        lay_pair(0, 1, VEC)
+        lay_features(0, 0, P, VEC)
+        round_chunk(0, VEC)
+        round_chunk(1, VEC)
         quantise_coefficients(0, 1)
-        for t in range(LAST_PLANE):
-            quantise_by_slot(0, t)
-        quantise_coefficients(1, 1)
         quantise_by_slot(0, LAST_PLANE)
+        quantise_by_slot(0, 2)
         rebuild(0)
-        rebuild(1)
-        lay_features(0, HALF, HALF, SCA)
-        round_pair(2, SCA)
-        lay_features(1, 0, HALF, SCA)
+        lay_features(0, P, HALF, VEC)
         minus_one = ring(VEC, [P, PACK], F32, "minus_one")
         nc.vector.scalar_tensor_tensor(minus_one[:], c_sq[:], -1.0, guess[:], ALU.mult, ALU.mult)
-        for t in range(LAST_PLANE):
-            quantise_by_slot(1, t)
-        noise_sq = keep.tile([P, PACK], F32, name="noise_sq")
-        nc.vector.scalar_tensor_tensor(noise_sq[:], minus_one[:], 2.0, guess[:], ALU.add, ALU.mult)
-        lay_features(1, HALF, P, VEC)
+        quantise_coefficients(1, 1)
+        rebuild(1)
+        lay_features(1, 0, HALF, SCA)
+        round_pair(2, SCA)
         residual(0)
         turn_residual(0)
+        noise_sq = ring(VEC, [P, PACK], F32, "noise_sq")
+        nc.vector.scalar_tensor_tensor(noise_sq[:], minus_one[:], 2.0, guess[:], ALU.add, ALU.mult)
+        lay_features(0, P + HALF, P, VEC)
         residual(1)
-        quantise_coefficients(2, 2)
+        lay_slots(1, LAST_PLANE)
+        square(0)
+        root(0)
         turn_residual(1)
+        quantise_coefficients(2, 2)
         rebuild(2)
         rebuild(3)
-        square(0)
-        lay_slots(1, LAST_PLANE)
-        square(1)
         weigh(0)
-        quantise_by_feature(0, 0)
         weigh(1)
-        quantise_by_feature(0, HALF)
+        quantise_by_feature(0, 0)
+        quantise_by_feature(0, P)
+        quantise_by_feature(0, P + HALF)
+        quantise_by_slot(1, 2)
         quantise_by_slot(1, LAST_PLANE)
-        lay_features(1, HALF + P, P, VEC)
-        residual(2)
-        turn_weighed(0)
-        turn_residual(2)
-        root(0)
-        root(1)
-        residual(3)
-        round_pair(4)
-        turn_weighed(1)
-        turn_residual(3)
+        square(1)
         inverse(0)
+        root(1)
+        residual(2)
+        turn_residual(2)
+        turn_weighed(0)
+        residual(3)
+        turn_residual(3)
+        turn_weighed(1)
+        round_pair(4)
         weigh(2)
         quantise_coefficients(4, 2)
         rebuild(4)
         rebuild(5)
-        round_pair(6)
+        square(2)
+        inverse(1)
+        root(2)
         gradient(0)
-
-        preparations = {
-            1: [(quantise_coefficients, 6, 2)],
-            2: [(quantise_by_feature, 1, 0)],
-            3: [(quantise_by_feature, 1, HALF), (quantise_by_feature, 1, HALF + P)],
-        }
-
-        def run(stage, k, first=0):
-            if first <= k < ALL_CHUNKS:
-                stage(k)
-
-        last_residual = LAST_CHUNK - 3
-        stores = {3: [(0, SCA)], 4: [(1, VEC)], 5: [(2, VEC)]}
-        for period in range(1, LAST_CHUNK):
-            run(square, period + 1)
-            run(residual, period + 3)
-            run(quantise_gradient, period - 1)
-            run(weigh, period + 2)
-            for step in preparations.get(period, []):
-                step[0](*step[1:])
-            if period <= last_residual:
-                run(turn_weighed, period + 1)
-            run(turn_residual, period + 3)
-            if period >= last_residual:
-                run(turn_weighed, period + 2)
-            run(project, period - 1)
-            run(rebuild, period + 5)
-            run(inverse, period)
-            run(root, period + 1)
-            run(gradient, period)
-            for k, engine in stores.get(period, []):
-                store(k, engine, nc.sync)
-
+        round_pair(6)
+        quantise_gradient(0)
+        square(3)
+        inverse(2)
+        root(3)
+        residual(4)
+        turn_residual(4)
+        turn_weighed(2)
+        project(0)
+        quantise_coefficients(6, 2)
+        gradient(1)
+        weigh(3)
+        quantise_gradient(1)
+        rebuild(6)
+        square(4)
+        inverse(3)
+        root(4)
+        residual(5)
+        turn_residual(5)
+        turn_weighed(3)
+        project(1)
+        rebuild(7)
+        gradient(2)
+        weigh(4)
+        quantise_gradient(2)
+        lay_features(1, HALF, HALF, VEC)
+        store(0, SCA, nc.sync)
+        square(5)
+        inverse(4)
+        root(5)
+        residual(6)
+        turn_residual(6)
+        turn_weighed(4)
+        project(2)
+        gradient(3)
+        weigh(5)
+        quantise_gradient(3)
+        quantise_by_feature(1, 0)
+        quantise_by_feature(1, HALF)
+        store(1, SCA, nc.sync)
+        square(6)
+        inverse(5)
+        root(6)
+        residual(7)
+        turn_residual(7)
+        turn_weighed(5)
+        project(3)
+        gradient(4)
+        weigh(6)
+        turn_weighed(6)
+        quantise_gradient(4)
+        project(4)
+        square(7)
+        inverse(6)
+        root(7)
+        weigh(7)
+        turn_weighed(7)
+        store(2, VEC, nc.sync)
+        gradient(5)
+        store(3, VEC, nc.sync)
+        quantise_gradient(5)
+        project(5)
+        gradient(6)
         inverse(LAST_CHUNK)
         gradient(LAST_CHUNK, LAST_HALVES[0])
-        quantise_gradient(LAST_CHUNK - 1)
-        project(LAST_CHUNK - 1)
+        quantise_gradient(6)
+        project(6)
         gradient(LAST_CHUNK, LAST_HALVES[1])
-        for k in range(3, LAST_CHUNK - 1):
-            store(k, SCA, nc.sync)
+        store(4, SCA, nc.sync)
+        store(5, SCA, nc.sync)
         quantise_gradient(LAST_CHUNK)
-        project(LAST_CHUNK)
-        store(LAST_CHUNK - 1, VEC, nc.sync)
-        store(LAST_CHUNK, SCA, nc.sync, slice(0, HALF))
-        store(LAST_CHUNK, SCA, nc.scalar, slice(HALF, N))
+        project(LAST_CHUNK, slice(0, HALF))
+        project(LAST_CHUNK, slice(HALF, N))
+        store(6, VEC, nc.sync)
+        store(LAST_CHUNK, SCA, nc.scalar, slice(0, HALF))
+        store(LAST_CHUNK, VEC, nc.sync, slice(HALF, N))

@@ -27,8 +27,8 @@ HALF = 256
 SHARE = 320
 RUN = 4
 LAST_HALVES = [slice(0, P // 2), slice(P // 2, P)]
-VEC, SCA = "vector", "scalar"
-RING_BUFS = {VEC: 40, SCA: 24}
+VEC, SCA, GPS = "vector", "scalar", "gpsimd"
+RING_BUFS = {VEC: 40, SCA: 24, GPS: 3}
 PLANE_BUFS = 3
 BANKS = 8
 SMALLEST_CS = 2.0**-60
@@ -213,9 +213,12 @@ def tile_attend_gdi_cau_z_kernel(tc, zT, wT, xm, wt, cs, offs, out):
                         nc.scalar.activation(made["inverse", k][:, planes_now, samples], made["root", k][:, planes_now, samples],
                                              ACT.Square)
 
-        def weigh(k):
-            made["weighed", k] = ring(VEC, [P, D], F32, "weighed")
-            nc.vector.tensor_scalar(made["weighed", k][:], made["gap", k][:], wt_cols[:, k : k + 1], None, ALU.mult)
+        def weigh(k, engine=VEC):
+            made["weighed", k] = ring(engine, [P, D], F32, "weighed")
+            if engine == VEC:
+                nc.vector.tensor_scalar(made["weighed", k][:], made["gap", k][:], wt_cols[:, k : k + 1], None, ALU.mult)
+            else:
+                nc.gpsimd.tensor_scalar(made["weighed", k][:], made["gap", k][:], wt_cols[:, k : k + 1], 0.0, ALU.mult, ALU.add)
 
         def turn_weighed(k):
             weighed_bank = bank_tile("weighed_bank")
@@ -312,98 +315,99 @@ def tile_attend_gdi_cau_z_kernel(tc, zT, wT, xm, wt, cs, offs, out):
         rebuild(2)
         rebuild(3)
         weigh(0)
+        turn_weighed(0)
         weigh(1)
-        quantise_by_feature(0, 0)
-        quantise_by_feature(0, P)
-        quantise_by_feature(0, P + HALF)
         quantise_by_slot(1, 2)
         quantise_by_slot(1, LAST_PLANE)
+        quantise_by_feature(0, 0)
+        quantise_by_feature(0, P)
         square(1)
         inverse(0)
         root(1)
         residual(2)
+        weigh(2, GPS)
         turn_residual(2)
-        turn_weighed(0)
         residual(3)
         turn_residual(3)
         turn_weighed(1)
+        gradient(0)
         round_pair(4)
-        weigh(2)
+        quantise_gradient(0)
         quantise_coefficients(4, 2)
         rebuild(4)
         rebuild(5)
+        turn_weighed(2)
         square(2)
         inverse(1)
         root(2)
-        gradient(0)
         round_pair(6)
-        quantise_gradient(0)
+        weigh(3)
+        quantise_coefficients(6, 2)
         square(3)
         inverse(2)
         root(3)
         residual(4)
+        weigh(4, GPS)
         turn_residual(4)
-        turn_weighed(2)
-        project(0)
-        quantise_coefficients(6, 2)
+        residual(5)
+        weigh(5, GPS)
+        turn_residual(5)
         gradient(1)
-        weigh(3)
-        quantise_gradient(1)
         rebuild(6)
+        gradient(2)
+        rebuild(7)
+        turn_weighed(3)
+        quantise_gradient(1)
+        quantise_gradient(2)
+        quantise_by_feature(0, P + HALF)
+        lay_features(1, HALF, HALF, VEC)
         square(4)
         inverse(3)
         root(4)
-        residual(5)
-        turn_residual(5)
-        turn_weighed(3)
-        project(1)
-        rebuild(7)
-        gradient(2)
-        weigh(4)
-        quantise_gradient(2)
-        lay_features(1, HALF, HALF, VEC)
-        store(0, SCA, nc.sync)
         square(5)
         inverse(4)
         root(5)
         residual(6)
+        weigh(6, GPS)
         turn_residual(6)
         turn_weighed(4)
-        project(2)
+        residual(7)
+        weigh(7, GPS)
+        turn_residual(7)
+        project(0)
         gradient(3)
-        weigh(5)
+        project(1)
+        gradient(4)
+        turn_weighed(5)
         quantise_gradient(3)
+        quantise_gradient(4)
         quantise_by_feature(1, 0)
         quantise_by_feature(1, HALF)
-        store(1, SCA, nc.sync)
         square(6)
         inverse(5)
         root(6)
-        residual(7)
-        turn_residual(7)
-        turn_weighed(5)
-        project(3)
-        gradient(4)
-        weigh(6)
+        store(0, VEC, nc.sync)
+        project(2)
+        gradient(5)
         turn_weighed(6)
-        quantise_gradient(4)
-        project(4)
+        store(1, VEC, nc.sync)
+        project(3)
+        quantise_gradient(5)
+        turn_weighed(7)
         square(7)
         inverse(6)
         root(7)
-        weigh(7)
-        turn_weighed(7)
         store(2, VEC, nc.sync)
-        gradient(5)
-        store(3, VEC, nc.sync)
-        quantise_gradient(5)
-        project(5)
+        project(4)
         gradient(6)
+        project(5)
+
         inverse(LAST_CHUNK)
         gradient(LAST_CHUNK, LAST_HALVES[0])
         quantise_gradient(6)
         project(6)
         gradient(LAST_CHUNK, LAST_HALVES[1])
+        store(3, SCA, nc.sync)
         store(4, SCA, nc.sync)
         store(5, SCA, nc.sync)
         quantise_gradient(LAST_CHUNK)

@@ -27,8 +27,9 @@ HALF = 256
 SHARE = 320
 RUN = 4
 LAST_HALVES = [slice(0, P // 2), slice(P // 2, P)]
+LOW, HIGH = slice(0, 2), slice(2, PACK)
 VEC, SCA, GPS = "vector", "scalar", "gpsimd"
-RING_BUFS = {VEC: 40, SCA: 24, GPS: 3}
+RING_BUFS = {VEC: 40, SCA: 14, GPS: 4}
 PLANE_BUFS = 3
 BANKS = 8
 SMALLEST_CS = 2.0**-60
@@ -50,6 +51,8 @@ def tile_attend_gdi_cau_z_kernel(tc, zT, wT, xm, wt, cs, offs, out):
         def move(engine, dst, src):
             if engine == SCA:
                 nc.scalar.copy(dst, src)
+            elif engine == GPS:
+                nc.gpsimd.tensor_scalar(dst, src, 1.0, 0.0, ALU.mult, ALU.add)
             else:
                 nc.vector.tensor_copy(out=dst, in_=src)
 
@@ -91,9 +94,10 @@ def tile_attend_gdi_cau_z_kernel(tc, zT, wT, xm, wt, cs, offs, out):
             load_coefficients(0, 1, 1)
             nc.sync.dma_start(out=wt_cols[:].rearrange("m (g j) -> m g j", j=2),
                               in_=wt.rearrange("b (h m j) o -> m (b h) (j o)", m=P, j=2))
+            load_coefficients(1, 0, 1)
             load_targets(0, 1)
-            load_coefficients(1, 0, 2)
             load_targets(1, 0)
+            load_coefficients(1, 1, 1)
             load_targets(1, 1)
 
         seed = keep.tile([P, PACK], F32, name="seed")
@@ -138,8 +142,8 @@ def tile_attend_gdi_cau_z_kernel(tc, zT, wT, xm, wt, cs, offs, out):
             nc.vector.quantize_mx(out=codes[:].bitcast(E4M3), scales=scales[:], in_=made["by_slot", b, t][:])
             made["slot_codes", b, t] = (codes, scales)
 
-        def lay_features(b, first, width, engine):
-            made["by_feature", b, first] = ring(engine, [P, width, PACK], BF16, "by_feature")
+        def lay_features(b, first, width, engine, onto=None):
+            made["by_feature", b, first] = ring(engine, [P, width, PACK], BF16, "by_feature") if onto is None else onto
             move(engine, made["by_feature", b, first][:].rearrange("p (c i) t -> p c t i", i=RUN),
                  picked[b][:].rearrange("p (t c i) -> p c t i", t=PACK, i=RUN)[:, first // RUN : (first + width) // RUN])
 
@@ -192,29 +196,37 @@ def tile_attend_gdi_cau_z_kernel(tc, zT, wT, xm, wt, cs, offs, out):
             for t in range(PACK):
                 nc.tensor.transpose(made["gap_bank", k][:, t, :], made["gap", k][:, P * t : P * (t + 1)], ident[:])
 
-        def square(k):
-            made["gap_sq", k] = ring(SCA, [P, PACK, P], F32, "gap_sq")
+        def square(k, together=1):
+            if k % together == 0:
+                made["gap_sq", k] = ring(SCA, [P, PACK, together, P], F32, "gap_sq")
+            squares = made["gap_sq", k - k % together]
             for planes_now in ([slice(0, 2), slice(2, PACK)] if k == 0 else [slice(0, PACK)]):
-                nc.scalar.activation(made["gap_sq", k][:, planes_now], made["gap_bank", k][:, planes_now], ACT.Square)
+                nc.scalar.activation(squares[:, planes_now, k % together, :], made["gap_bank", k][:, planes_now], ACT.Square)
 
         def root(k):
-            made["root", k] = ring(SCA, [P, PACK, P], F32, "root")
+            made["root", k] = ring(SCA, list(made["gap_sq", k].shape), F32, "root")
             for t in range(PACK):
-                nc.scalar.activation(made["root", k][:, t, :], made["gap_sq", k][:, t, :], ACT.Abs_reciprocal_sqrt,
+                nc.scalar.activation(made["root", k][:, t], made["gap_sq", k][:, t], ACT.Abs_reciprocal_sqrt,
                                      bias=noise_sq[:, t : t + 1])
 
         def inverse(k):
-            made["inverse", k] = ring(SCA, [P, PACK, P], F32, "inverse")
-            if k < LAST_CHUNK:
-                nc.scalar.activation(made["inverse", k][:], made["root", k][:], ACT.Square)
-            else:
-                for samples in LAST_HALVES:
-                    for planes_now in (slice(0, 2), slice(2, PACK)):
-                        nc.scalar.activation(made["inverse", k][:, planes_now, samples], made["root", k][:, planes_now, samples],
-                                             ACT.Square)
+            squared = ring(SCA, list(made["root", k].shape), F32, "inverse")
+            nc.scalar.activation(squared[:], made["root", k][:], ACT.Square)
+            for j in range(squared.shape[2]):
+                made["inverse", k + j] = squared[:, :, j, :]
 
-        def weigh(k, engine=VEC):
-            made["weighed", k] = ring(engine, [P, D], F32, "weighed")
+        def inverse_part(k, planes_now, engine=SCA, samples=slice(0, P)):
+            if ("inverse", k) not in made:
+                made["inverse", k] = ring(SCA, [P, PACK, P], F32, "inverse")
+            dst = made["inverse", k][:, planes_now, samples]
+            src = made["root", k - k % 2][:, planes_now, k % 2, samples]
+            if engine == GPS:
+                nc.gpsimd.tensor_tensor(dst, src, src, ALU.mult)
+            else:
+                nc.scalar.activation(dst, src, ACT.Square)
+
+        def weigh(k, engine=VEC, onto=None):
+            made["weighed", k] = ring(engine, [P, D], F32, "weighed") if onto is None else onto[:].rearrange("p i t -> p (i t)").bitcast(F32)
             if engine == VEC:
                 nc.vector.tensor_scalar(made["weighed", k][:], made["gap", k][:], wt_cols[:, k : k + 1], None, ALU.mult)
             else:
@@ -226,17 +238,23 @@ def tile_attend_gdi_cau_z_kernel(tc, zT, wT, xm, wt, cs, offs, out):
                 nc.tensor.transpose(weighed_bank[:, t, :], made["weighed", k][:, P * t : P * (t + 1)], ident[:])
             made["numerator", k] = weighed_bank
 
-        def gradient(k, samples=slice(0, P)):
-            if samples.start == 0:
-                made["e", k] = ring(VEC, [P, D], BF16, "e")
+        def gradient(k, samples=slice(0, P), together=1):
+            if samples.start == 0 and k % together == 0:
+                made["e_tile", k] = ring(VEC, [P, together * D], BF16, "e")
+                for j in range(together):
+                    made["e", k + j] = made["e_tile", k][:, D * j : D * (j + 1)]
             nc.vector.tensor_tensor(made["e", k][:].rearrange("p (m t) -> p m t", t=PACK)[:, samples].rearrange("p (c i) t -> p c t i", i=2),
                                     made["numerator", k][:, :, samples].rearrange("p t (c i) -> p c t i", i=2),
                                     made["inverse", k][:, :, samples].rearrange("p t (c i) -> p c t i", i=2), ALU.mult)
 
         def quantise_gradient(k):
-            made["e_codes", k] = ring(VEC, [P, P], U32, "e_codes")
-            made["e_scales", k] = keep.tile([P, P], U8, name=f"e_scales{k}", align_bytes=64)
-            nc.vector.quantize_mx(out=made["e_codes", k][:].bitcast(E5M2), scales=made["e_scales", k][:], in_=made["e", k][:])
+            width = made["e_tile", k].shape[1] // PACK
+            codes = ring(VEC, [P, width], U32, "e_codes")
+            scales = keep.tile([P, width], U8, name=f"e_scales{k}", align_bytes=64)
+            nc.vector.quantize_mx(out=codes[:].bitcast(E5M2), scales=scales[:], in_=made["e_tile", k][:])
+            for j in range(width // P):
+                made["e_codes", k + j] = codes[:, P * j : P * (j + 1)]
+                made["e_scales", k + j] = scales[:, P * j : P * (j + 1)]
 
         def project(k, part=slice(0, N)):
             made["sums", k, part.start] = bank_tile("sums")
@@ -315,94 +333,88 @@ def tile_attend_gdi_cau_z_kernel(tc, zT, wT, xm, wt, cs, offs, out):
         rebuild(2)
         rebuild(3)
         weigh(0)
-        turn_weighed(0)
-        weigh(1)
+        round_pair(4)
         quantise_by_slot(1, 2)
+        residual(2)
+        turn_weighed(0)
+        turn_residual(2)
         quantise_by_slot(1, LAST_PLANE)
-        quantise_by_feature(0, 0)
-        quantise_by_feature(0, P)
+        quantise_coefficients(4, 2)
         square(1)
         inverse(0)
         root(1)
-        residual(2)
+        weigh(1, GPS, made["z_bf", 4])
         weigh(2, GPS)
-        turn_residual(2)
         residual(3)
-        turn_residual(3)
-        turn_weighed(1)
-        gradient(0)
-        round_pair(4)
-        quantise_gradient(0)
-        quantise_coefficients(4, 2)
         rebuild(4)
+        weigh(3, GPS)
+        turn_residual(3)
         rebuild(5)
-        turn_weighed(2)
-        square(2)
+        gradient(0)
+        turn_weighed(1)
+        square(2, 2)
+        square(3, 2)
         inverse(1)
         root(2)
-        round_pair(6)
-        weigh(3)
-        quantise_coefficients(6, 2)
-        square(3)
-        inverse(2)
-        root(3)
         residual(4)
-        weigh(4, GPS)
         turn_residual(4)
         residual(5)
-        weigh(5, GPS)
         turn_residual(5)
-        gradient(1)
-        rebuild(6)
-        gradient(2)
-        rebuild(7)
-        turn_weighed(3)
-        quantise_gradient(1)
-        quantise_gradient(2)
+        round_pair(6)
+        quantise_gradient(0)
+        quantise_by_feature(0, 0)
         quantise_by_feature(0, P + HALF)
-        lay_features(1, HALF, HALF, VEC)
-        square(4)
-        inverse(3)
+        quantise_by_feature(0, P)
+        project(0)
+        gradient(1)
+        quantise_coefficients(6, 2)
+        rebuild(6)
+        rebuild(7)
+        quantise_gradient(1)
+        project(1)
+        turn_weighed(2)
+        quantise_by_feature(1, 0)
+        weigh(4, GPS, made["by_feature", 1, 0])
+        weigh(5, GPS)
+        square(4, 2)
+        square(5, 2)
+        inverse(2)
         root(4)
-        square(5)
-        inverse(4)
-        root(5)
+        store(0, VEC, nc.sync)
+        turn_weighed(3)
         residual(6)
         weigh(6, GPS)
         turn_residual(6)
-        turn_weighed(4)
         residual(7)
         weigh(7, GPS)
         turn_residual(7)
-        project(0)
-        gradient(3)
-        project(1)
-        gradient(4)
-        turn_weighed(5)
-        quantise_gradient(3)
-        quantise_gradient(4)
-        quantise_by_feature(1, 0)
-        quantise_by_feature(1, HALF)
-        square(6)
-        inverse(5)
-        root(6)
-        store(0, VEC, nc.sync)
-        project(2)
-        gradient(5)
-        turn_weighed(6)
         store(1, VEC, nc.sync)
+        gradient(2, together=2)
+        turn_weighed(4)
+        gradient(3, together=2)
+        turn_weighed(5)
+        lay_features(1, HALF, HALF, VEC)
+        quantise_gradient(2)
+        project(2)
         project(3)
-        quantise_gradient(5)
+        quantise_by_feature(1, HALF)
+        square(6, 2)
+        square(7, 2)
+        inverse(4)
+        root(6)
+        gradient(4, together=2)
+        turn_weighed(6)
+        gradient(5, together=2)
         turn_weighed(7)
-        square(7)
-        inverse(6)
-        root(7)
         store(2, VEC, nc.sync)
+        inverse_part(6, LOW)
+        inverse_part(6, HIGH)
+        quantise_gradient(4)
         project(4)
-        gradient(6)
         project(5)
-
-        inverse(LAST_CHUNK)
+        gradient(6)
+        inverse_part(7, slice(0, PACK), SCA, LAST_HALVES[0])
+        inverse_part(7, slice(0, PACK), SCA, LAST_HALVES[1])
         gradient(LAST_CHUNK, LAST_HALVES[0])
         quantise_gradient(6)
         project(6)

@@ -48,6 +48,9 @@ def tile_attend_gdi_cau_z_kernel(tc, zT, wT, xm, wt, cs, offs, out):
         def bank_tile(name):
             return psum.tile([P, PACK, P], F32, name=name, tag="bank")
 
+        def as_floats(laid):
+            return laid[:].rearrange("p i t -> p (i t)").bitcast(F32)
+
         def move(engine, dst, src):
             if engine == SCA:
                 nc.scalar.copy(dst, src)
@@ -128,13 +131,13 @@ def tile_attend_gdi_cau_z_kernel(tc, zT, wT, xm, wt, cs, offs, out):
             for u in range(2):
                 nc.tensor.transpose(made["atom_bank", b, t][:, u, :], words[:, u : N // 2 : 2], ident[:])
 
-        def lay_slots(b, t):
+        def lay_slots(b, t, engine=SCA):
             if t == 0:
                 made["by_slot", b, t] = picked[b][:, 2 * N : 3 * N]
             else:
-                made["by_slot", b, t] = ring(SCA, [P, N], BF16, "by_slot")
-            nc.scalar.copy(made["by_slot", b, t][:].bitcast(F32).rearrange("m (c i u) -> m c u i", i=2, u=2),
-                           made["atom_bank", b, t][:, 0:2, :].rearrange("m u (c i) -> m c u i", i=2))
+                made["by_slot", b, t] = ring(engine, [P, N], BF16, "by_slot")
+            move(engine, made["by_slot", b, t][:].bitcast(F32).rearrange("m (c i u) -> m c u i", i=2, u=2),
+                 made["atom_bank", b, t][:, 0:2, :].rearrange("m u (c i) -> m c u i", i=2))
 
         def quantise_by_slot(b, t):
             codes = ring(VEC, [P, P], U32, "slot_codes")
@@ -144,8 +147,12 @@ def tile_attend_gdi_cau_z_kernel(tc, zT, wT, xm, wt, cs, offs, out):
 
         def lay_features(b, first, width, engine, onto=None):
             made["by_feature", b, first] = ring(engine, [P, width, PACK], BF16, "by_feature") if onto is None else onto
-            move(engine, made["by_feature", b, first][:].rearrange("p (c i) t -> p c t i", i=RUN),
-                 picked[b][:].rearrange("p (t c i) -> p c t i", t=PACK, i=RUN)[:, first // RUN : (first + width) // RUN])
+            if engine == GPS:
+                move(engine, made["by_feature", b, first][:],
+                     picked[b][:].rearrange("p (t i) -> p i t", t=PACK)[:, first : first + width])
+            else:
+                move(engine, made["by_feature", b, first][:].rearrange("p (c i) t -> p c t i", i=RUN),
+                     picked[b][:].rearrange("p (t c i) -> p c t i", t=PACK, i=RUN)[:, first // RUN : (first + width) // RUN])
 
         def quantise_by_feature(b, first):
             laid = made["by_feature", b, first]
@@ -184,24 +191,26 @@ def tile_attend_gdi_cau_z_kernel(tc, zT, wT, xm, wt, cs, offs, out):
                 nc.tensor.matmul_mx(out=made["rec", k][:, t, :], lhsT=z_codes.bitcast(E4M3), lhsT_scale=z_scales,
                                     rhs=codes[:].bitcast(E4M3), rhs_scale=scales[:], start=True, stop=True)
 
-        def residual(k):
+        def residual(k, planes_now=slice(0, PACK)):
             b, c = divmod(k, CHUNKS)
-            made["gap", k] = ring(VEC, [P, D], F32, "gap")
-            nc.vector.tensor_tensor(made["gap", k][:].rearrange("m (t c i) -> m c t i", t=PACK, i=2),
-                                    made["rec", k][:].rearrange("m t (c i) -> m c t i", i=2),
-                                    x_raw[b, c // 2][:, c % 2, :].rearrange("m (c i t) -> m c t i", t=PACK, i=2), ALU.subtract)
+            if planes_now.start == 0:
+                made["gap", k] = ring(VEC, [P, D], F32, "gap")
+            nc.vector.tensor_tensor(made["gap", k][:].rearrange("m (t c i) -> m c t i", t=PACK, i=2)[:, :, planes_now],
+                                    made["rec", k][:].rearrange("m t (c i) -> m c t i", i=2)[:, :, planes_now],
+                                    x_raw[b, c // 2][:, c % 2, :].rearrange("m (c i t) -> m c t i", t=PACK, i=2)[:, :, planes_now],
+                                    ALU.subtract)
 
-        def turn_residual(k):
-            made["gap_bank", k] = bank_tile("gap_bank")
-            for t in range(PACK):
-                nc.tensor.transpose(made["gap_bank", k][:, t, :], made["gap", k][:, P * t : P * (t + 1)], ident[:])
+        def turn_residual(k, planes_now=slice(0, PACK)):
+            made["gap_bank", k, planes_now.start] = bank_tile("gap_bank")
+            for t in range(PACK)[planes_now]:
+                nc.tensor.transpose(made["gap_bank", k, planes_now.start][:, t, :], made["gap", k][:, P * t : P * (t + 1)], ident[:])
 
         def square(k, together=1):
             if k % together == 0:
                 made["gap_sq", k] = ring(SCA, [P, PACK, together, P], F32, "gap_sq")
             squares = made["gap_sq", k - k % together]
             for planes_now in ([slice(0, 2), slice(2, PACK)] if k == 0 else [slice(0, PACK)]):
-                nc.scalar.activation(squares[:, planes_now, k % together, :], made["gap_bank", k][:, planes_now], ACT.Square)
+                nc.scalar.activation(squares[:, planes_now, k % together, :], made["gap_bank", k, planes_now.start][:, planes_now], ACT.Square)
 
         def root(k):
             made["root", k] = ring(SCA, list(made["gap_sq", k].shape), F32, "root")
@@ -215,8 +224,10 @@ def tile_attend_gdi_cau_z_kernel(tc, zT, wT, xm, wt, cs, offs, out):
             for j in range(squared.shape[2]):
                 made["inverse", k + j] = squared[:, :, j, :]
 
-        def inverse_part(k, planes_now, engine=SCA, samples=slice(0, P)):
-            if ("inverse", k) not in made:
+        def inverse_part(k, planes_now, engine=SCA, samples=slice(0, P), onto=None):
+            if onto is not None:
+                made["inverse", k] = onto[:].rearrange("p i t -> p (i t)").bitcast(F32).rearrange("p (t m) -> p t m", t=PACK)
+            elif ("inverse", k) not in made:
                 made["inverse", k] = ring(SCA, [P, PACK, P], F32, "inverse")
             dst = made["inverse", k][:, planes_now, samples]
             src = made["root", k - k % 2][:, planes_now, k % 2, samples]
@@ -226,7 +237,7 @@ def tile_attend_gdi_cau_z_kernel(tc, zT, wT, xm, wt, cs, offs, out):
                 nc.scalar.activation(dst, src, ACT.Square)
 
         def weigh(k, engine=VEC, onto=None):
-            made["weighed", k] = ring(engine, [P, D], F32, "weighed") if onto is None else onto[:].rearrange("p i t -> p (i t)").bitcast(F32)
+            made["weighed", k] = ring(engine, [P, D], F32, "weighed") if onto is None else onto
             if engine == VEC:
                 nc.vector.tensor_scalar(made["weighed", k][:], made["gap", k][:], wt_cols[:, k : k + 1], None, ALU.mult)
             else:
@@ -292,8 +303,12 @@ def tile_attend_gdi_cau_z_kernel(tc, zT, wT, xm, wt, cs, offs, out):
         gather(0, 2, VEC)
         gather(1, 2, VEC, 0, P)
         gather(1, 2, SCA, P, N - P)
+        minus_one = ring(VEC, [P, PACK], F32, "minus_one")
+        nc.vector.scalar_tensor_tensor(minus_one[:], c_sq[:], -1.0, guess[:], ALU.mult, ALU.mult)
         quantise_by_slot(0, 1)
         quantise_by_slot(1, 1)
+        noise_sq = ring(VEC, [P, PACK], F32, "noise_sq")
+        nc.vector.scalar_tensor_tensor(noise_sq[:], minus_one[:], 2.0, guess[:], ALU.add, ALU.mult)
         turn_atoms(0, 2)
         turn_atoms(1, 2)
         gather(0, LAST_PLANE, VEC, 0, SHARE)
@@ -311,20 +326,20 @@ def tile_attend_gdi_cau_z_kernel(tc, zT, wT, xm, wt, cs, offs, out):
         quantise_coefficients(0, 1)
         quantise_by_slot(0, LAST_PLANE)
         quantise_by_slot(0, 2)
-        rebuild(0)
-        lay_features(0, P, HALF, VEC)
-        minus_one = ring(VEC, [P, PACK], F32, "minus_one")
-        nc.vector.scalar_tensor_tensor(minus_one[:], c_sq[:], -1.0, guess[:], ALU.mult, ALU.mult)
         quantise_coefficients(1, 1)
+        rebuild(0)
         rebuild(1)
+        lay_features(0, P, HALF, VEC)
+        lay_features(0, P + HALF, P, GPS, made["z_bf", 1])
         lay_features(1, 0, HALF, SCA)
         round_pair(2, SCA)
-        residual(0)
-        turn_residual(0)
-        noise_sq = ring(VEC, [P, PACK], F32, "noise_sq")
-        nc.vector.scalar_tensor_tensor(noise_sq[:], minus_one[:], 2.0, guess[:], ALU.add, ALU.mult)
-        lay_features(0, P + HALF, P, VEC)
+        residual(0, LOW)
+        turn_residual(0, LOW)
+        residual(0, HIGH)
+        turn_residual(0, HIGH)
         residual(1)
+        quantise_by_slot(1, 2)
+        quantise_by_feature(0, 0)
         lay_slots(1, LAST_PLANE)
         square(0)
         root(0)
@@ -332,24 +347,25 @@ def tile_attend_gdi_cau_z_kernel(tc, zT, wT, xm, wt, cs, offs, out):
         quantise_coefficients(2, 2)
         rebuild(2)
         rebuild(3)
-        weigh(0)
-        round_pair(4)
-        quantise_by_slot(1, 2)
-        residual(2)
-        turn_weighed(0)
-        turn_residual(2)
         quantise_by_slot(1, LAST_PLANE)
+        quantise_by_feature(0, P)
+        round_pair(4)
+        weigh(0, GPS, z_raw[1, 0][:, 0:2, :].rearrange("p t c -> p (t c)"))
+        residual(2)
+        turn_residual(2)
+        residual(3)
+        turn_weighed(0)
+        turn_residual(3)
         quantise_coefficients(4, 2)
+        rebuild(4)
+        quantise_by_feature(0, P + HALF)
+        weigh(1)
+        rebuild(5)
         square(1)
         inverse(0)
         root(1)
-        weigh(1, GPS, made["z_bf", 4])
-        weigh(2, GPS)
-        residual(3)
-        rebuild(4)
+        weigh(2, GPS, made["gap", 1])
         weigh(3, GPS)
-        turn_residual(3)
-        rebuild(5)
         gradient(0)
         turn_weighed(1)
         square(2, 2)
@@ -360,40 +376,39 @@ def tile_attend_gdi_cau_z_kernel(tc, zT, wT, xm, wt, cs, offs, out):
         turn_residual(4)
         residual(5)
         turn_residual(5)
+        turn_weighed(2)
         round_pair(6)
         quantise_gradient(0)
-        quantise_by_feature(0, 0)
-        quantise_by_feature(0, P + HALF)
-        quantise_by_feature(0, P)
-        project(0)
-        gradient(1)
         quantise_coefficients(6, 2)
         rebuild(6)
         rebuild(7)
+        project(0)
+        turn_weighed(3)
+        gradient(1)
+        lay_features(1, HALF, HALF, VEC)
         quantise_gradient(1)
-        project(1)
-        turn_weighed(2)
         quantise_by_feature(1, 0)
-        weigh(4, GPS, made["by_feature", 1, 0])
+        weigh(4, GPS, as_floats(made["by_feature", 1, 0]))
         weigh(5, GPS)
         square(4, 2)
         square(5, 2)
         inverse(2)
         root(4)
-        store(0, VEC, nc.sync)
-        turn_weighed(3)
         residual(6)
         weigh(6, GPS)
         turn_residual(6)
         residual(7)
         weigh(7, GPS)
         turn_residual(7)
-        store(1, VEC, nc.sync)
+        project(1)
+        store(0, VEC, nc.sync)
         gradient(2, together=2)
         turn_weighed(4)
         gradient(3, together=2)
         turn_weighed(5)
-        lay_features(1, HALF, HALF, VEC)
+        turn_weighed(6)
+        turn_weighed(7)
+        store(1, VEC, nc.sync)
         quantise_gradient(2)
         project(2)
         project(3)
@@ -403,9 +418,7 @@ def tile_attend_gdi_cau_z_kernel(tc, zT, wT, xm, wt, cs, offs, out):
         inverse(4)
         root(6)
         gradient(4, together=2)
-        turn_weighed(6)
         gradient(5, together=2)
-        turn_weighed(7)
         store(2, VEC, nc.sync)
         inverse_part(6, LOW)
         inverse_part(6, HIGH)

@@ -329,6 +329,7 @@ def tile_attend_gdi_cau_z_kernel(tc, zT, wT, xm, wt, cs, offs, out):
         quantise_coefficients(1, 1)
         rebuild(0)
         rebuild(1)
+        quantise_by_slot(1, 2)
         lay_features(0, P, HALF, VEC)
         lay_features(0, P + HALF, P, GPS, made["z_bf", 1])
         lay_features(1, 0, HALF, SCA)
@@ -338,42 +339,41 @@ def tile_attend_gdi_cau_z_kernel(tc, zT, wT, xm, wt, cs, offs, out):
         residual(0, HIGH)
         turn_residual(0, HIGH)
         residual(1)
-        quantise_by_slot(1, 2)
         quantise_by_feature(0, 0)
+        quantise_coefficients(2, 2)
         lay_slots(1, LAST_PLANE)
         square(0)
         root(0)
         turn_residual(1)
-        quantise_coefficients(2, 2)
         rebuild(2)
         rebuild(3)
-        quantise_by_slot(1, LAST_PLANE)
-        quantise_by_feature(0, P)
         round_pair(4)
-        weigh(0, GPS, z_raw[1, 0][:, 0:2, :].rearrange("p t c -> p (t c)"))
+        quantise_by_slot(1, LAST_PLANE)
+        quantise_by_feature(0, P + HALF)
+        quantise_coefficients(4, 2)
+        weigh(0, GPS, as_floats(made["z_bf", 4]))
         residual(2)
+        rebuild(4)
+        rebuild(5)
         turn_residual(2)
         residual(3)
-        turn_weighed(0)
         turn_residual(3)
-        quantise_coefficients(4, 2)
-        rebuild(4)
-        quantise_by_feature(0, P + HALF)
+        turn_weighed(0)
+        quantise_by_feature(0, P)
         weigh(1)
-        rebuild(5)
         square(1)
         inverse(0)
         root(1)
         weigh(2, GPS, made["gap", 1])
         weigh(3, GPS)
-        gradient(0)
-        turn_weighed(1)
         square(2, 2)
         square(3, 2)
         inverse(1)
         root(2)
         residual(4)
         turn_residual(4)
+        gradient(0)
+        turn_weighed(1)
         residual(5)
         turn_residual(5)
         turn_weighed(2)
@@ -417,13 +417,14 @@ def tile_attend_gdi_cau_z_kernel(tc, zT, wT, xm, wt, cs, offs, out):
         square(7, 2)
         inverse(4)
         root(6)
-        gradient(4, together=2)
-        gradient(5, together=2)
+        gradient(4)
+        gradient(5)
+        quantise_gradient(4)
+        project(4)
         store(2, VEC, nc.sync)
         inverse_part(6, LOW)
         inverse_part(6, HIGH)
-        quantise_gradient(4)
-        project(4)
+        quantise_gradient(5)
         project(5)
         gradient(6)
         inverse_part(7, slice(0, PACK), SCA, LAST_HALVES[0])

@@ -22,12 +22,14 @@ LAST_PLANE = PACK - 1
 CHUNKS = R // P
 ALL_CHUNKS = B * CHUNKS
 LAST_CHUNK = ALL_CHUNKS - 1
-LIST_COLS = N // 16
+BAND = 16
 HALF = 256
-SHARE = 320
+EARLY_SHARE = 128
+LAST_SHARE = 320
 RUN = 4
+ALL_PLANES, LOW, HIGH = slice(0, PACK), slice(0, 2), slice(2, PACK)
+ALL_SAMPLES = slice(0, P)
 LAST_HALVES = [slice(0, P // 2), slice(P // 2, P)]
-LOW, HIGH = slice(0, 2), slice(2, PACK)
 VEC, SCA, GPS = "vector", "scalar", "gpsimd"
 RING_BUFS = {VEC: 40, SCA: 14, GPS: 4}
 PLANE_BUFS = 3
@@ -54,12 +56,10 @@ def tile_attend_gdi_cau_z_kernel(tc, zT, wT, xm, wt, cs, offs, out):
         def move(engine, dst, src):
             if engine == SCA:
                 nc.scalar.copy(dst, src)
-            elif engine == GPS:
-                nc.gpsimd.tensor_scalar(dst, src, 1.0, 0.0, ALU.mult, ALU.add)
             else:
                 nc.vector.tensor_copy(out=dst, in_=src)
 
-        offsets = keep.tile([P, B * LIST_COLS], U16, name="offsets")
+        offsets = keep.tile([P, B * N // BAND], U16, name="offsets")
         wt_cols = keep.tile([P, ALL_CHUNKS], F32, name="wt_cols")
         ident = keep.tile([P, P], F32, name="ident")
         make_identity(nc, ident[:])
@@ -74,11 +74,11 @@ def tile_attend_gdi_cau_z_kernel(tc, zT, wT, xm, wt, cs, offs, out):
             planes[t] = work.tile([P, T], F32, name="plane", tag="plane", bufs=PLANE_BUFS, align_bytes=64)
             nc.sync.dma_start(out=planes[t][:], in_=w_planes[:, t, :])
 
-        def load_coefficients(b, h, halves):
-            raw = keep.tile([P, PACK, halves * HALF], F32, name=f"z_raw{b}{h}", align_bytes=64)
-            nc.sync.dma_start(out=raw[:], in_=zT[b].rearrange("(p t) r -> p t r", t=PACK)[:, :, HALF * h : HALF * (h + halves)])
-            for i in range(halves):
-                z_raw[b, h + i] = raw[:, :, HALF * i : HALF * (i + 1)]
+        def load_coefficients(b):
+            raw = keep.tile([P, PACK, R], F32, name=f"z_raw{b}", align_bytes=64)
+            nc.sync.dma_start(out=raw[:], in_=zT[b].rearrange("(p t) r -> p t r", t=PACK))
+            for h in range(2):
+                z_raw[b, h] = raw[:, :, HALF * h : HALF * (h + 1)]
 
         def load_targets(b, h):
             x_raw[b, h] = keep.tile([P, 2, D], F32, name=f"x_raw{b}{h}", align_bytes=64)
@@ -92,15 +92,13 @@ def tile_attend_gdi_cau_z_kernel(tc, zT, wT, xm, wt, cs, offs, out):
 
         def load_the_rest():
             load_plane(LAST_PLANE)
-            load_coefficients(0, 0, 1)
+            load_coefficients(0)
             load_targets(0, 0)
-            load_coefficients(0, 1, 1)
+            load_coefficients(1)
+            load_targets(0, 1)
             nc.sync.dma_start(out=wt_cols[:].rearrange("m (g j) -> m g j", j=2),
                               in_=wt.rearrange("b (h m j) o -> m (b h) (j o)", m=P, j=2))
-            load_coefficients(1, 0, 1)
-            load_targets(0, 1)
             load_targets(1, 0)
-            load_coefficients(1, 1, 1)
             load_targets(1, 1)
 
         seed = keep.tile([P, PACK], F32, name="seed")
@@ -109,7 +107,7 @@ def tile_attend_gdi_cau_z_kernel(tc, zT, wT, xm, wt, cs, offs, out):
         guess = keep.tile([P, PACK], F32, name="guess")
         nc.scalar.activation(seed[:], c_cols[:], ACT.Abs_reciprocal_sqrt, bias=SMALLEST_CS)
 
-        def small_steps():
+        def guess_noise():
             nc.scalar.activation(c_sq[:], c_cols[:], ACT.Square)
             nc.scalar.activation(seed_sq[:], seed[:], ACT.Square)
             nc.scalar.activation(guess[:], seed_sq[:], ACT.Square)
@@ -118,12 +116,17 @@ def tile_attend_gdi_cau_z_kernel(tc, zT, wT, xm, wt, cs, offs, out):
         made = {}
 
         def gather(b, t, engine, first=0, width=N):
-            listed = offsets[:, (b * N + first) // 16 : (b * N + first + width) // 16]
+            listed = offsets[:, (b * N + first) // BAND : (b * N + first + width) // BAND]
             dst = picked[b][:, N * t + first : N * t + first + width]
             if engine == SCA:
                 nc.scalar.activation(dst, planes[t][:].indirect(listed), ACT.Copy)
             else:
                 nc.vector.tensor_copy(dst, planes[t][:].indirect(listed))
+
+        def gather_early_plane(t):
+            gather(0, t, VEC)
+            gather(1, t, VEC, 0, EARLY_SHARE)
+            gather(1, t, SCA, EARLY_SHARE, N - EARLY_SHARE)
 
         def turn_atoms(b, t):
             made["atom_bank", b, t] = bank_tile("atom_bank")
@@ -131,13 +134,13 @@ def tile_attend_gdi_cau_z_kernel(tc, zT, wT, xm, wt, cs, offs, out):
             for u in range(2):
                 nc.tensor.transpose(made["atom_bank", b, t][:, u, :], words[:, u : N // 2 : 2], ident[:])
 
-        def lay_slots(b, t, engine=SCA):
+        def lay_slots(b, t):
             if t == 0:
                 made["by_slot", b, t] = picked[b][:, 2 * N : 3 * N]
             else:
-                made["by_slot", b, t] = ring(engine, [P, N], BF16, "by_slot")
-            move(engine, made["by_slot", b, t][:].bitcast(F32).rearrange("m (c i u) -> m c u i", i=2, u=2),
-                 made["atom_bank", b, t][:, 0:2, :].rearrange("m u (c i) -> m c u i", i=2))
+                made["by_slot", b, t] = ring(SCA, [P, N], BF16, "by_slot")
+            nc.scalar.copy(made["by_slot", b, t][:].bitcast(F32).rearrange("m (c i u) -> m c u i", i=2, u=2),
+                           made["atom_bank", b, t][:, 0:2, :].rearrange("m u (c i) -> m c u i", i=2))
 
         def quantise_by_slot(b, t):
             codes = ring(VEC, [P, P], U32, "slot_codes")
@@ -145,14 +148,15 @@ def tile_attend_gdi_cau_z_kernel(tc, zT, wT, xm, wt, cs, offs, out):
             nc.vector.quantize_mx(out=codes[:].bitcast(E4M3), scales=scales[:], in_=made["by_slot", b, t][:])
             made["slot_codes", b, t] = (codes, scales)
 
-        def lay_features(b, first, width, engine, onto=None):
-            made["by_feature", b, first] = ring(engine, [P, width, PACK], BF16, "by_feature") if onto is None else onto
-            if engine == GPS:
-                move(engine, made["by_feature", b, first][:],
-                     picked[b][:].rearrange("p (t i) -> p i t", t=PACK)[:, first : first + width])
-            else:
-                move(engine, made["by_feature", b, first][:].rearrange("p (c i) t -> p c t i", i=RUN),
-                     picked[b][:].rearrange("p (t c i) -> p c t i", t=PACK, i=RUN)[:, first // RUN : (first + width) // RUN])
+        def lay_features(b, first, width, engine):
+            made["by_feature", b, first] = ring(engine, [P, width, PACK], BF16, "by_feature")
+            move(engine, made["by_feature", b, first][:].rearrange("p (c i) t -> p c t i", i=RUN),
+                 picked[b][:].rearrange("p (t c i) -> p c t i", t=PACK, i=RUN)[:, first // RUN : (first + width) // RUN])
+
+        def lay_features_beside(b, first, onto):
+            made["by_feature", b, first] = onto
+            nc.gpsimd.tensor_scalar(onto, picked[b][:].rearrange("p (t i) -> p i t", t=PACK)[:, first : first + onto.shape[1]],
+                                    1.0, 0.0, ALU.mult, ALU.add)
 
         def quantise_by_feature(b, first):
             laid = made["by_feature", b, first]
@@ -162,19 +166,21 @@ def tile_attend_gdi_cau_z_kernel(tc, zT, wT, xm, wt, cs, offs, out):
             nc.vector.quantize_mx(out=codes[:].bitcast(E4M3), scales=scales[:], in_=laid[:].rearrange("p i t -> p (i t)"))
             made.setdefault(("feature_codes", b), []).append((slice(first, first + width), codes, scales))
 
-        def round_chunk(k, engine):
+        def round_chunk(k):
             b, c = divmod(k, CHUNKS)
-            made["z_bf", k] = ring(engine, [P, P, PACK], BF16, "z_bf")
+            made["z_bf", k] = ring(VEC, [P, P, PACK], BF16, "z_bf")
             samples = z_raw[b, c // 2].rearrange("p t (m j) -> p t m j", j=2)[:, :, :, c % 2]
-            move(engine, made["z_bf", k][:].rearrange("p (c i) t -> p c t i", i=RUN), samples.rearrange("p t (c i) -> p c t i", i=RUN))
+            nc.vector.tensor_copy(out=made["z_bf", k][:].rearrange("p (c i) t -> p c t i", i=RUN),
+                                  in_=samples.rearrange("p t (c i) -> p c t i", i=RUN))
 
-        def round_pair(k, engine=VEC):
+        def round_pair(k, engine):
             b, c = divmod(k, CHUNKS)
             made["z_bf", k] = ring(engine, [P, 2 * P, PACK], BF16, "z_bf")
             move(engine, made["z_bf", k][:].rearrange("p (j c i) t -> p c t i j", j=2, i=2),
                  z_raw[b, c // 2].rearrange("p t (c i j) -> p c t i j", i=2, j=2))
 
-        def quantise_coefficients(k, count):
+        def quantise_coefficients(k):
+            count = made["z_bf", k].shape[1] // P
             codes = ring(VEC, [P, count * P], U32, "z_codes")
             scales = keep.tile([P, count * P], U8, name=f"z_scales{k}", align_bytes=64)
             nc.vector.quantize_mx(out=codes[:].bitcast(E4M3), scales=scales[:],
@@ -191,26 +197,28 @@ def tile_attend_gdi_cau_z_kernel(tc, zT, wT, xm, wt, cs, offs, out):
                 nc.tensor.matmul_mx(out=made["rec", k][:, t, :], lhsT=z_codes.bitcast(E4M3), lhsT_scale=z_scales,
                                     rhs=codes[:].bitcast(E4M3), rhs_scale=scales[:], start=True, stop=True)
 
-        def residual(k, planes_now=slice(0, PACK)):
+        def residual(k, planes_now=ALL_PLANES):
             b, c = divmod(k, CHUNKS)
             if planes_now.start == 0:
                 made["gap", k] = ring(VEC, [P, D], F32, "gap")
+            targets = x_raw[b, c // 2][:, c % 2, :]
             nc.vector.tensor_tensor(made["gap", k][:].rearrange("m (t c i) -> m c t i", t=PACK, i=2)[:, :, planes_now],
                                     made["rec", k][:].rearrange("m t (c i) -> m c t i", i=2)[:, :, planes_now],
-                                    x_raw[b, c // 2][:, c % 2, :].rearrange("m (c i t) -> m c t i", t=PACK, i=2)[:, :, planes_now],
-                                    ALU.subtract)
+                                    targets.rearrange("m (c i t) -> m c t i", t=PACK, i=2)[:, :, planes_now], ALU.subtract)
 
-        def turn_residual(k, planes_now=slice(0, PACK)):
-            made["gap_bank", k, planes_now.start] = bank_tile("gap_bank")
+        def turn_residual(k, planes_now=ALL_PLANES):
+            gap_bank = bank_tile("gap_bank")
             for t in range(PACK)[planes_now]:
-                nc.tensor.transpose(made["gap_bank", k, planes_now.start][:, t, :], made["gap", k][:, P * t : P * (t + 1)], ident[:])
+                nc.tensor.transpose(gap_bank[:, t, :], made["gap", k][:, P * t : P * (t + 1)], ident[:])
+            made["gap_bank", k, planes_now.start] = gap_bank
 
-        def square(k, together=1):
+        def square(k, together):
             if k % together == 0:
                 made["gap_sq", k] = ring(SCA, [P, PACK, together, P], F32, "gap_sq")
             squares = made["gap_sq", k - k % together]
-            for planes_now in ([slice(0, 2), slice(2, PACK)] if k == 0 else [slice(0, PACK)]):
-                nc.scalar.activation(squares[:, planes_now, k % together, :], made["gap_bank", k, planes_now.start][:, planes_now], ACT.Square)
+            for planes_now in [LOW, HIGH] if k == 0 else [ALL_PLANES]:
+                nc.scalar.activation(squares[:, planes_now, k % together, :],
+                                     made["gap_bank", k, planes_now.start][:, planes_now], ACT.Square)
 
         def root(k):
             made["root", k] = ring(SCA, list(made["gap_sq", k].shape), F32, "root")
@@ -224,24 +232,25 @@ def tile_attend_gdi_cau_z_kernel(tc, zT, wT, xm, wt, cs, offs, out):
             for j in range(squared.shape[2]):
                 made["inverse", k + j] = squared[:, :, j, :]
 
-        def inverse_part(k, planes_now, engine=SCA, samples=slice(0, P), onto=None):
-            if onto is not None:
-                made["inverse", k] = onto[:].rearrange("p i t -> p (i t)").bitcast(F32).rearrange("p (t m) -> p t m", t=PACK)
-            elif ("inverse", k) not in made:
-                made["inverse", k] = ring(SCA, [P, PACK, P], F32, "inverse")
-            dst = made["inverse", k][:, planes_now, samples]
-            src = made["root", k - k % 2][:, planes_now, k % 2, samples]
-            if engine == GPS:
-                nc.gpsimd.tensor_tensor(dst, src, src, ALU.mult)
-            else:
-                nc.scalar.activation(dst, src, ACT.Square)
+        def inverse_in_parts(k, parts):
+            made["inverse", k] = ring(SCA, [P, PACK, P], F32, "inverse")
+            for planes_now, samples in parts:
+                nc.scalar.activation(made["inverse", k][:, planes_now, samples],
+                                     made["root", k - k % 2][:, planes_now, k % 2, samples], ACT.Square)
 
-        def weigh(k, engine=VEC, onto=None):
-            made["weighed", k] = ring(engine, [P, D], F32, "weighed") if onto is None else onto
-            if engine == VEC:
-                nc.vector.tensor_scalar(made["weighed", k][:], made["gap", k][:], wt_cols[:, k : k + 1], None, ALU.mult)
-            else:
-                nc.gpsimd.tensor_scalar(made["weighed", k][:], made["gap", k][:], wt_cols[:, k : k + 1], 0.0, ALU.mult, ALU.add)
+        def scalar_steps(chunks, previous):
+            for k in chunks:
+                square(k, len(chunks))
+            inverse(previous)
+            root(chunks[0])
+
+        def weigh(k):
+            made["weighed", k] = ring(VEC, [P, D], F32, "weighed")
+            nc.vector.tensor_scalar(made["weighed", k][:], made["gap", k][:], wt_cols[:, k : k + 1], None, ALU.mult)
+
+        def weigh_beside(k, onto=None):
+            made["weighed", k] = ring(GPS, [P, D], F32, "weighed") if onto is None else onto
+            nc.gpsimd.tensor_scalar(made["weighed", k][:], made["gap", k][:], wt_cols[:, k : k + 1], 0.0, ALU.mult, ALU.add)
 
         def turn_weighed(k):
             weighed_bank = bank_tile("weighed_bank")
@@ -249,12 +258,13 @@ def tile_attend_gdi_cau_z_kernel(tc, zT, wT, xm, wt, cs, offs, out):
                 nc.tensor.transpose(weighed_bank[:, t, :], made["weighed", k][:, P * t : P * (t + 1)], ident[:])
             made["numerator", k] = weighed_bank
 
-        def gradient(k, samples=slice(0, P), together=1):
+        def gradient(k, samples=ALL_SAMPLES, together=1):
             if samples.start == 0 and k % together == 0:
                 made["e_tile", k] = ring(VEC, [P, together * D], BF16, "e")
                 for j in range(together):
                     made["e", k + j] = made["e_tile", k][:, D * j : D * (j + 1)]
-            nc.vector.tensor_tensor(made["e", k][:].rearrange("p (m t) -> p m t", t=PACK)[:, samples].rearrange("p (c i) t -> p c t i", i=2),
+            e_now = made["e", k].rearrange("p (m t) -> p m t", t=PACK)[:, samples]
+            nc.vector.tensor_tensor(e_now.rearrange("p (c i) t -> p c t i", i=2),
                                     made["numerator", k][:, :, samples].rearrange("p t (c i) -> p c t i", i=2),
                                     made["inverse", k][:, :, samples].rearrange("p t (c i) -> p c t i", i=2), ALU.mult)
 
@@ -272,86 +282,81 @@ def tile_attend_gdi_cau_z_kernel(tc, zT, wT, xm, wt, cs, offs, out):
             for cols, codes, scales in made["feature_codes", k // CHUNKS]:
                 if part.start <= cols.start < part.stop:
                     nc.tensor.matmul_mx(out=made["sums", k, part.start][:].rearrange("m a c -> m (a c)")[:, cols],
-                                        lhsT=made["e_codes", k][:].bitcast(E5M2), lhsT_scale=made["e_scales", k][:],
+                                        lhsT=made["e_codes", k].bitcast(E5M2), lhsT_scale=made["e_scales", k],
                                         rhs=codes[:].bitcast(E4M3), rhs_scale=scales[:], start=True, stop=True)
 
-        def store(k, engine, queue, cols=slice(0, N)):
+        def store(k, engine, cols=slice(0, N), queue=nc.sync):
             b, c = divmod(k, CHUNKS)
             rows = out[b, HALF * (c // 2) : HALF * (c // 2 + 1), :].rearrange("(m j) i -> m j i", j=2)[:, c % 2, :]
             staged = ring(engine, [P, cols.stop - cols.start], F32, "staged")
             move(engine, staged[:], made["sums", k, cols.start][:].rearrange("m a c -> m (a c)")[:, cols])
             queue.dma_start(out=rows[:, cols], in_=staged[:])
 
-        gather(0, 0, VEC)
-        gather(1, 0, VEC, 0, P)
-        gather(1, 0, SCA, P, N - P)
+        gather_early_plane(0)
         load_the_rest()
-        small_steps()
-        gather(0, 1, VEC)
-        gather(1, 1, VEC, 0, P)
-        gather(1, 1, SCA, P, N - P)
-        turn_atoms(0, 0)
-        lay_slots(0, 0)
-        turn_atoms(1, 0)
-        lay_slots(1, 0)
-        quantise_by_slot(0, 0)
-        quantise_by_slot(1, 0)
-        turn_atoms(0, 1)
-        lay_slots(0, 1)
-        turn_atoms(1, 1)
-        lay_slots(1, 1)
-        gather(0, 2, VEC)
-        gather(1, 2, VEC, 0, P)
-        gather(1, 2, SCA, P, N - P)
+        guess_noise()
+        gather_early_plane(1)
+        for b in range(B):
+            turn_atoms(b, 0)
+            lay_slots(b, 0)
+        for b in range(B):
+            quantise_by_slot(b, 0)
+        for b in range(B):
+            turn_atoms(b, 1)
+            lay_slots(b, 1)
+        gather_early_plane(2)
         minus_one = ring(VEC, [P, PACK], F32, "minus_one")
         nc.vector.scalar_tensor_tensor(minus_one[:], c_sq[:], -1.0, guess[:], ALU.mult, ALU.mult)
-        quantise_by_slot(0, 1)
-        quantise_by_slot(1, 1)
+        for b in range(B):
+            quantise_by_slot(b, 1)
         noise_sq = ring(VEC, [P, PACK], F32, "noise_sq")
         nc.vector.scalar_tensor_tensor(noise_sq[:], minus_one[:], 2.0, guess[:], ALU.add, ALU.mult)
-        turn_atoms(0, 2)
-        turn_atoms(1, 2)
-        gather(0, LAST_PLANE, VEC, 0, SHARE)
-        gather(0, LAST_PLANE, SCA, SHARE, N - SHARE)
+        for b in range(B):
+            turn_atoms(b, 2)
+
+        gather(0, LAST_PLANE, VEC, 0, LAST_SHARE)
+        gather(0, LAST_PLANE, SCA, LAST_SHARE, N - LAST_SHARE)
         gather(1, LAST_PLANE, VEC, 0, HALF)
         gather(1, LAST_PLANE, SCA, HALF, HALF)
         turn_atoms(0, LAST_PLANE)
         lay_slots(0, LAST_PLANE)
-        lay_slots(0, 2)
-        lay_slots(1, 2)
+        for b in range(B):
+            lay_slots(b, 2)
         turn_atoms(1, LAST_PLANE)
         lay_features(0, 0, P, VEC)
-        round_chunk(0, VEC)
-        round_chunk(1, VEC)
-        quantise_coefficients(0, 1)
+        lay_features(0, P, HALF, VEC)
+
+        round_chunk(0)
         quantise_by_slot(0, LAST_PLANE)
         quantise_by_slot(0, 2)
-        quantise_coefficients(1, 1)
+        quantise_coefficients(0)
         rebuild(0)
-        rebuild(1)
+        round_chunk(1)
         quantise_by_slot(1, 2)
-        lay_features(0, P, HALF, VEC)
-        lay_features(0, P + HALF, P, GPS, made["z_bf", 1])
-        lay_features(1, 0, HALF, SCA)
-        round_pair(2, SCA)
-        residual(0, LOW)
-        turn_residual(0, LOW)
-        residual(0, HIGH)
-        turn_residual(0, HIGH)
-        residual(1)
         quantise_by_feature(0, 0)
-        quantise_coefficients(2, 2)
+        quantise_coefficients(1)
+        rebuild(1)
+        round_pair(2, SCA)
+        quantise_coefficients(2)
+
+        lay_features_beside(0, P + HALF, made["z_bf", 2][:, 0:P, :])
+        lay_features(1, 0, HALF, SCA)
+        rebuild(2)
+        for planes_now in (LOW, HIGH):
+            residual(0, planes_now)
+            turn_residual(0, planes_now)
+        residual(1)
         lay_slots(1, LAST_PLANE)
-        square(0)
+        square(0, 1)
         root(0)
         turn_residual(1)
-        rebuild(2)
         rebuild(3)
-        round_pair(4)
+        round_pair(4, VEC)
         quantise_by_slot(1, LAST_PLANE)
         quantise_by_feature(0, P + HALF)
-        quantise_coefficients(4, 2)
-        weigh(0, GPS, as_floats(made["z_bf", 4]))
+        quantise_coefficients(4)
+
+        weigh_beside(0, as_floats(made["z_bf", 4]))
         residual(2)
         rebuild(4)
         rebuild(5)
@@ -361,15 +366,11 @@ def tile_attend_gdi_cau_z_kernel(tc, zT, wT, xm, wt, cs, offs, out):
         turn_weighed(0)
         quantise_by_feature(0, P)
         weigh(1)
-        square(1)
-        inverse(0)
-        root(1)
-        weigh(2, GPS, made["gap", 1])
-        weigh(3, GPS)
-        square(2, 2)
-        square(3, 2)
-        inverse(1)
-        root(2)
+        scalar_steps([1], 0)
+
+        weigh_beside(2, made["gap", 1])
+        weigh_beside(3)
+        scalar_steps([2, 3], 1)
         residual(4)
         turn_residual(4)
         gradient(0)
@@ -377,9 +378,9 @@ def tile_attend_gdi_cau_z_kernel(tc, zT, wT, xm, wt, cs, offs, out):
         residual(5)
         turn_residual(5)
         turn_weighed(2)
-        round_pair(6)
+        round_pair(6, VEC)
         quantise_gradient(0)
-        quantise_coefficients(6, 2)
+        quantise_coefficients(6)
         rebuild(6)
         rebuild(7)
         project(0)
@@ -388,57 +389,51 @@ def tile_attend_gdi_cau_z_kernel(tc, zT, wT, xm, wt, cs, offs, out):
         lay_features(1, HALF, HALF, VEC)
         quantise_gradient(1)
         quantise_by_feature(1, 0)
-        weigh(4, GPS, as_floats(made["by_feature", 1, 0]))
-        weigh(5, GPS)
-        square(4, 2)
-        square(5, 2)
-        inverse(2)
-        root(4)
+
+        weigh_beside(4, as_floats(made["by_feature", 1, 0]))
+        weigh_beside(5)
+        scalar_steps([4, 5], 2)
         residual(6)
-        weigh(6, GPS)
+        weigh_beside(6)
         turn_residual(6)
         residual(7)
-        weigh(7, GPS)
         turn_residual(7)
         project(1)
-        store(0, VEC, nc.sync)
+        store(0, VEC)
         gradient(2, together=2)
         turn_weighed(4)
         gradient(3, together=2)
         turn_weighed(5)
         turn_weighed(6)
-        turn_weighed(7)
-        store(1, VEC, nc.sync)
+        store(1, VEC)
         quantise_gradient(2)
         project(2)
         project(3)
         quantise_by_feature(1, HALF)
-        square(6, 2)
-        square(7, 2)
-        inverse(4)
-        root(6)
+
+        weigh_beside(LAST_CHUNK, as_floats(made["by_feature", 1, HALF]))
+        scalar_steps([6, 7], 4)
         gradient(4)
         gradient(5)
         quantise_gradient(4)
+        turn_weighed(LAST_CHUNK)
         project(4)
-        store(2, VEC, nc.sync)
-        inverse_part(6, LOW)
-        inverse_part(6, HIGH)
+        store(2, VEC)
+        inverse_in_parts(6, [(LOW, ALL_SAMPLES), (HIGH, ALL_SAMPLES)])
         quantise_gradient(5)
         project(5)
         gradient(6)
-        inverse_part(7, slice(0, PACK), SCA, LAST_HALVES[0])
-        inverse_part(7, slice(0, PACK), SCA, LAST_HALVES[1])
+
+        inverse_in_parts(LAST_CHUNK, [(ALL_PLANES, samples) for samples in LAST_HALVES])
         gradient(LAST_CHUNK, LAST_HALVES[0])
         quantise_gradient(6)
         project(6)
         gradient(LAST_CHUNK, LAST_HALVES[1])
-        store(3, SCA, nc.sync)
-        store(4, SCA, nc.sync)
-        store(5, SCA, nc.sync)
+        for k in (3, 4, 5):
+            store(k, SCA)
         quantise_gradient(LAST_CHUNK)
         project(LAST_CHUNK, slice(0, HALF))
         project(LAST_CHUNK, slice(HALF, N))
-        store(6, VEC, nc.sync)
-        store(LAST_CHUNK, SCA, nc.scalar, slice(0, HALF))
-        store(LAST_CHUNK, VEC, nc.sync, slice(HALF, N))
+        store(6, VEC)
+        store(LAST_CHUNK, SCA, slice(0, HALF), nc.scalar)
+        store(LAST_CHUNK, VEC, slice(HALF, N))

@@ -33,6 +33,7 @@ LAST_HALVES = [slice(0, P // 2), slice(P // 2, P)]
 VEC, SCA, GPS = "vector", "scalar", "gpsimd"
 RING_BUFS = {VEC: 40, SCA: 14, GPS: 4}
 PLANE_BUFS = 3
+NO_INVERSE = []
 BANKS = 8
 SMALLEST_CS = 2.0**-60
 
@@ -74,11 +75,11 @@ def tile_attend_gdi_cau_z_kernel(tc, zT, wT, xm, wt, cs, offs, out):
             planes[t] = work.tile([P, T], F32, name="plane", tag="plane", bufs=PLANE_BUFS, align_bytes=64)
             nc.sync.dma_start(out=planes[t][:], in_=w_planes[:, t, :])
 
-        def load_coefficients(b):
-            raw = keep.tile([P, PACK, R], F32, name=f"z_raw{b}", align_bytes=64)
-            nc.sync.dma_start(out=raw[:], in_=zT[b].rearrange("(p t) r -> p t r", t=PACK))
-            for h in range(2):
-                z_raw[b, h] = raw[:, :, HALF * h : HALF * (h + 1)]
+        def load_coefficients(b, halves):
+            raw = keep.tile([P, PACK, HALF * len(halves)], F32, name=f"z_raw{b}{halves[0]}", align_bytes=64)
+            nc.sync.dma_start(out=raw[:], in_=zT[b].rearrange("(p t) r -> p t r", t=PACK)[:, :, HALF * halves[0] : HALF * (halves[-1] + 1)])
+            for n, h in enumerate(halves):
+                z_raw[b, h] = raw[:, :, HALF * n : HALF * (n + 1)]
 
         def load_targets(b, h):
             x_raw[b, h] = keep.tile([P, 2, D], F32, name=f"x_raw{b}{h}", align_bytes=64)
@@ -92,13 +93,15 @@ def tile_attend_gdi_cau_z_kernel(tc, zT, wT, xm, wt, cs, offs, out):
 
         def load_the_rest():
             load_plane(LAST_PLANE)
-            load_coefficients(0)
+            load_coefficients(0, [0])
             load_targets(0, 0)
-            load_coefficients(1)
+            load_coefficients(0, [1])
             load_targets(0, 1)
+            load_coefficients(1, [0])
             nc.sync.dma_start(out=wt_cols[:].rearrange("m (g j) -> m g j", j=2),
                               in_=wt.rearrange("b (h m j) o -> m (b h) (j o)", m=P, j=2))
             load_targets(1, 0)
+            load_coefficients(1, [1])
             load_targets(1, 1)
 
         seed = keep.tile([P, PACK], F32, name="seed")
@@ -115,43 +118,42 @@ def tile_attend_gdi_cau_z_kernel(tc, zT, wT, xm, wt, cs, offs, out):
         picked = [keep.tile([P, PACK * N], BF16, name=f"picked{b}", align_bytes=64) for b in range(B)]
         made = {}
 
+        def plane_of(b, t):
+            return picked[b][:, N * t : N * (t + 1)]
+
         def gather(b, t, engine, first=0, width=N):
             listed = offsets[:, (b * N + first) // BAND : (b * N + first + width) // BAND]
-            dst = picked[b][:, N * t + first : N * t + first + width]
+            dst = plane_of(b, t)[:, first : first + width]
             if engine == SCA:
                 nc.scalar.activation(dst, planes[t][:].indirect(listed), ACT.Copy)
             else:
                 nc.vector.tensor_copy(dst, planes[t][:].indirect(listed))
 
-        def gather_early_plane(t):
-            gather(0, t, VEC)
-            gather(1, t, VEC, 0, EARLY_SHARE)
-            gather(1, t, SCA, EARLY_SHARE, N - EARLY_SHARE)
-
         def turn_atoms(b, t):
             made["atom_bank", b, t] = bank_tile("atom_bank")
-            words = picked[b][:, N * t : N * (t + 1)].bitcast(F32)
+            words = plane_of(b, t).bitcast(F32)
             for u in range(2):
                 nc.tensor.transpose(made["atom_bank", b, t][:, u, :], words[:, u : N // 2 : 2], ident[:])
 
-        def lay_slots(b, t):
-            if t == 0:
-                made["by_slot", b, t] = picked[b][:, 2 * N : 3 * N]
-            else:
-                made["by_slot", b, t] = ring(SCA, [P, N], BF16, "by_slot")
-            nc.scalar.copy(made["by_slot", b, t][:].bitcast(F32).rearrange("m (c i u) -> m c u i", i=2, u=2),
-                           made["atom_bank", b, t][:, 0:2, :].rearrange("m u (c i) -> m c u i", i=2))
+        def lay_slots(b, t, engine, onto=None):
+            if onto is None:
+                made["slot_room", b, t] = ring(engine, [P, 2 * N], BF16, "by_slot")
+                onto = made["slot_room", b, t][:, 0:N]
+            made["by_slot", b, t] = onto
+            move(engine, made["by_slot", b, t].bitcast(F32).rearrange("m (c i u) -> m c u i", i=2, u=2),
+                 made["atom_bank", b, t][:, 0:2, :].rearrange("m u (c i) -> m c u i", i=2))
 
         def quantise_by_slot(b, t):
             codes = ring(VEC, [P, P], U32, "slot_codes")
             scales = keep.tile([P, P], U8, name=f"slot_scales{b}{t}", align_bytes=64)
-            nc.vector.quantize_mx(out=codes[:].bitcast(E4M3), scales=scales[:], in_=made["by_slot", b, t][:])
+            nc.vector.quantize_mx(out=codes[:].bitcast(E4M3), scales=scales[:], in_=made["by_slot", b, t])
             made["slot_codes", b, t] = (codes, scales)
 
-        def lay_features(b, first, width, engine):
-            made["by_feature", b, first] = ring(engine, [P, width, PACK], BF16, "by_feature")
-            move(engine, made["by_feature", b, first][:].rearrange("p (c i) t -> p c t i", i=RUN),
-                 picked[b][:].rearrange("p (t c i) -> p c t i", t=PACK, i=RUN)[:, first // RUN : (first + width) // RUN])
+        def lay_features(b, first, width, planes_now, engine):
+            if planes_now.start == 0:
+                made["by_feature", b, first] = ring(engine, [P, width, PACK], BF16, "by_feature")
+            move(engine, made["by_feature", b, first][:, :, planes_now].rearrange("p (c i) t -> p c t i", i=RUN),
+                 picked[b][:].rearrange("p (t c i) -> p c t i", t=PACK, i=RUN)[:, first // RUN : (first + width) // RUN, planes_now])
 
         def lay_features_beside(b, first, onto):
             made["by_feature", b, first] = onto
@@ -166,12 +168,13 @@ def tile_attend_gdi_cau_z_kernel(tc, zT, wT, xm, wt, cs, offs, out):
             nc.vector.quantize_mx(out=codes[:].bitcast(E4M3), scales=scales[:], in_=laid[:].rearrange("p i t -> p (i t)"))
             made.setdefault(("feature_codes", b), []).append((slice(first, first + width), codes, scales))
 
-        def round_chunk(k):
+        def round_chunk(k, engine=VEC):
             b, c = divmod(k, CHUNKS)
-            made["z_bf", k] = ring(VEC, [P, P, PACK], BF16, "z_bf")
+            made["z_room", k] = ring(engine, [P, 2 * D], BF16, "z_bf")
+            made["z_bf", k] = made["z_room", k][:, 0:D].rearrange("p (m t) -> p m t", t=PACK)
             samples = z_raw[b, c // 2].rearrange("p t (m j) -> p t m j", j=2)[:, :, :, c % 2]
-            nc.vector.tensor_copy(out=made["z_bf", k][:].rearrange("p (c i) t -> p c t i", i=RUN),
-                                  in_=samples.rearrange("p t (c i) -> p c t i", i=RUN))
+            move(engine, made["z_bf", k][:].rearrange("p (c i) t -> p c t i", i=RUN),
+                 samples.rearrange("p t (c i) -> p c t i", i=RUN))
 
         def round_pair(k, engine):
             b, c = divmod(k, CHUNKS)
@@ -188,13 +191,12 @@ def tile_attend_gdi_cau_z_kernel(tc, zT, wT, xm, wt, cs, offs, out):
             for n in range(count):
                 made["z", k + n] = (codes[:, P * n : P * (n + 1)], scales[:, P * n : P * (n + 1)])
 
-        def rebuild(k):
-            made["rec", k] = bank_tile("rec")
+        def rebuild(k, planes_now=ALL_PLANES):
+            made["rec", k, planes_now.start] = bank_tile("rec")
             z_codes, z_scales = made["z", k]
-            b = k // CHUNKS
-            for t in (0, 1, LAST_PLANE, 2):
-                codes, scales = made["slot_codes", b, t]
-                nc.tensor.matmul_mx(out=made["rec", k][:, t, :], lhsT=z_codes.bitcast(E4M3), lhsT_scale=z_scales,
+            for t in range(PACK)[planes_now]:
+                codes, scales = made["slot_codes", k // CHUNKS, t]
+                nc.tensor.matmul_mx(out=made["rec", k, planes_now.start][:, t, :], lhsT=z_codes.bitcast(E4M3), lhsT_scale=z_scales,
                                     rhs=codes[:].bitcast(E4M3), rhs_scale=scales[:], start=True, stop=True)
 
         def residual(k, planes_now=ALL_PLANES):
@@ -203,7 +205,7 @@ def tile_attend_gdi_cau_z_kernel(tc, zT, wT, xm, wt, cs, offs, out):
                 made["gap", k] = ring(VEC, [P, D], F32, "gap")
             targets = x_raw[b, c // 2][:, c % 2, :]
             nc.vector.tensor_tensor(made["gap", k][:].rearrange("m (t c i) -> m c t i", t=PACK, i=2)[:, :, planes_now],
-                                    made["rec", k][:].rearrange("m t (c i) -> m c t i", i=2)[:, :, planes_now],
+                                    made["rec", k, planes_now.start][:].rearrange("m t (c i) -> m c t i", i=2)[:, :, planes_now],
                                     targets.rearrange("m (c i t) -> m c t i", t=PACK, i=2)[:, :, planes_now], ALU.subtract)
 
         def turn_residual(k, planes_now=ALL_PLANES):
@@ -236,12 +238,13 @@ def tile_attend_gdi_cau_z_kernel(tc, zT, wT, xm, wt, cs, offs, out):
             made["inverse", k] = ring(SCA, [P, PACK, P], F32, "inverse")
             for planes_now, samples in parts:
                 nc.scalar.activation(made["inverse", k][:, planes_now, samples],
-                                     made["root", k - k % 2][:, planes_now, k % 2, samples], ACT.Square)
+                                     made["root", k][:, planes_now, 0, samples], ACT.Square)
 
         def scalar_steps(chunks, previous):
             for k in chunks:
                 square(k, len(chunks))
-            inverse(previous)
+            if previous not in NO_INVERSE:
+                inverse(previous)
             root(chunks[0])
 
         def weigh(k):
@@ -259,8 +262,9 @@ def tile_attend_gdi_cau_z_kernel(tc, zT, wT, xm, wt, cs, offs, out):
             made["numerator", k] = weighed_bank
 
         def gradient(k, samples=ALL_SAMPLES, together=1):
-            if samples.start == 0 and k % together == 0:
-                made["e_tile", k] = ring(VEC, [P, together * D], BF16, "e")
+            if samples.start == 0 and together:
+                made["e_room", k] = ring(VEC, [P, 2 * D], BF16, "e")
+                made["e_tile", k] = made["e_room", k][:, 0 : together * D]
                 for j in range(together):
                     made["e", k + j] = made["e_tile", k][:, D * j : D * (j + 1)]
             e_now = made["e", k].rearrange("p (m t) -> p m t", t=PACK)[:, samples]
@@ -268,11 +272,21 @@ def tile_attend_gdi_cau_z_kernel(tc, zT, wT, xm, wt, cs, offs, out):
                                     made["numerator", k][:, :, samples].rearrange("p t (c i) -> p c t i", i=2),
                                     made["inverse", k][:, :, samples].rearrange("p t (c i) -> p c t i", i=2), ALU.mult)
 
+        def halfway(k):
+            once = ring(VEC, [P, PACK, P], F32, "once")
+            nc.vector.tensor_tensor(once[:], made["numerator", k][:], made["root", k][:, :, 0, :], ALU.mult)
+            made["numerator", k] = once
+            made["inverse", k] = made["root", k][:, :, 0, :]
+
+        def inverse_beside(k, onto):
+            nc.gpsimd.tensor_tensor(onto, made["root", k][:].rearrange("p t j m -> p (t j m)"), made["root", k][:].rearrange("p t j m -> p (t j m)"), ALU.mult)
+            made["inverse", k] = onto.rearrange("p (t m) -> p t m", t=PACK)
+
         def quantise_gradient(k):
             width = made["e_tile", k].shape[1] // PACK
             codes = ring(VEC, [P, width], U32, "e_codes")
             scales = keep.tile([P, width], U8, name=f"e_scales{k}", align_bytes=64)
-            nc.vector.quantize_mx(out=codes[:].bitcast(E5M2), scales=scales[:], in_=made["e_tile", k][:])
+            nc.vector.quantize_mx(out=codes[:].bitcast(E5M2), scales=scales[:], in_=made["e_tile", k])
             for j in range(width // P):
                 made["e_codes", k + j] = codes[:, P * j : P * (j + 1)]
                 made["e_scales", k + j] = scales[:, P * j : P * (j + 1)]
@@ -292,148 +306,164 @@ def tile_attend_gdi_cau_z_kernel(tc, zT, wT, xm, wt, cs, offs, out):
             move(engine, staged[:], made["sums", k, cols.start][:].rearrange("m a c -> m (a c)")[:, cols])
             queue.dma_start(out=rows[:, cols], in_=staged[:])
 
-        gather_early_plane(0)
+        gather(0, 0, VEC)
+        gather(1, 0, VEC, 0, EARLY_SHARE)
+        gather(1, 0, SCA, EARLY_SHARE, N - EARLY_SHARE)
         load_the_rest()
         guess_noise()
-        gather_early_plane(1)
+        gather(0, 1, VEC)
+        gather(1, 1, VEC, 0, EARLY_SHARE)
+        gather(1, 1, SCA, EARLY_SHARE, N - EARLY_SHARE)
         for b in range(B):
             turn_atoms(b, 0)
-            lay_slots(b, 0)
+            lay_slots(b, 0, SCA, plane_of(b, 2))
         for b in range(B):
             quantise_by_slot(b, 0)
+        lay_features(0, P, HALF, LOW, VEC)
+        lay_features(0, P + HALF, P, LOW, VEC)
         for b in range(B):
             turn_atoms(b, 1)
-            lay_slots(b, 1)
-        gather_early_plane(2)
+            lay_slots(b, 1, SCA, plane_of(b, 3))
+        gather(0, 2, VEC)
+        gather(1, 2, VEC, 0, EARLY_SHARE)
+        gather(1, 2, SCA, EARLY_SHARE, N - EARLY_SHARE)
         minus_one = ring(VEC, [P, PACK], F32, "minus_one")
         nc.vector.scalar_tensor_tensor(minus_one[:], c_sq[:], -1.0, guess[:], ALU.mult, ALU.mult)
         for b in range(B):
             quantise_by_slot(b, 1)
         noise_sq = ring(VEC, [P, PACK], F32, "noise_sq")
         nc.vector.scalar_tensor_tensor(noise_sq[:], minus_one[:], 2.0, guess[:], ALU.add, ALU.mult)
-        for b in range(B):
-            turn_atoms(b, 2)
-
-        gather(0, LAST_PLANE, VEC, 0, LAST_SHARE)
+        turn_atoms(0, 2)
+        gather(0, LAST_PLANE, VEC, 0, LAST_SHARE - P)
+        gather(0, LAST_PLANE, VEC, LAST_SHARE - P, P)
         gather(0, LAST_PLANE, SCA, LAST_SHARE, N - LAST_SHARE)
-        gather(1, LAST_PLANE, VEC, 0, HALF)
-        gather(1, LAST_PLANE, SCA, HALF, HALF)
+        gather(1, LAST_PLANE, SCA)
+        turn_atoms(1, 2)
         turn_atoms(0, LAST_PLANE)
-        lay_slots(0, LAST_PLANE)
-        for b in range(B):
-            lay_slots(b, 2)
-        turn_atoms(1, LAST_PLANE)
-        lay_features(0, 0, P, VEC)
-        lay_features(0, P, HALF, VEC)
-
+        lay_features(0, 0, P, ALL_PLANES, VEC)
+        lay_slots(0, 2, VEC)
         round_chunk(0)
-        quantise_by_slot(0, LAST_PLANE)
-        quantise_by_slot(0, 2)
-        quantise_coefficients(0)
-        rebuild(0)
         round_chunk(1)
-        quantise_by_slot(1, 2)
-        quantise_by_feature(0, 0)
+        lay_slots(0, LAST_PLANE, SCA)
+        quantise_coefficients(0)
+        quantise_by_slot(0, 2)
+        lay_features(0, P + HALF, P, HIGH, VEC)
+        quantise_by_slot(0, LAST_PLANE)
+        turn_atoms(1, LAST_PLANE)
+        rebuild(0, LOW)
         quantise_coefficients(1)
+        rebuild(0, HIGH)
         rebuild(1)
-        round_pair(2, SCA)
-        quantise_coefficients(2)
-
-        lay_features_beside(0, P + HALF, made["z_bf", 2][:, 0:P, :])
-        lay_features(1, 0, HALF, SCA)
-        rebuild(2)
-        for planes_now in (LOW, HIGH):
-            residual(0, planes_now)
-            turn_residual(0, planes_now)
+        lay_slots(1, 2, SCA)
+        lay_features(1, 0, P, ALL_PLANES, SCA)
+        lay_slots(1, LAST_PLANE, SCA)
+        lay_features(1, P, P, ALL_PLANES, SCA)
+        round_chunk(2, SCA)
+        lay_features(0, P, HALF, HIGH, VEC)
+        quantise_by_slot(1, 2)
+        lay_features_beside(1, HALF, made["slot_room", 1, 2][:].rearrange("p (s t) -> p s t", t=PACK))
+        residual(0, LOW)
+        turn_residual(0, LOW)
+        residual(0, HIGH)
+        turn_residual(0, HIGH)
         residual(1)
-        lay_slots(1, LAST_PLANE)
+        turn_residual(1)
+        quantise_coefficients(2)
+        round_chunk(3)
+        rebuild(2)
+        quantise_by_slot(1, LAST_PLANE)
+        quantise_by_feature(0, 0)
+        quantise_coefficients(3)
+        rebuild(3)
         square(0, 1)
         root(0)
-        turn_residual(1)
-        rebuild(3)
-        round_pair(4, VEC)
-        quantise_by_slot(1, LAST_PLANE)
         quantise_by_feature(0, P + HALF)
-        quantise_coefficients(4)
 
-        weigh_beside(0, as_floats(made["z_bf", 4]))
+        weigh_beside(0, made["z_room", 3][:].bitcast(F32))
         residual(2)
-        rebuild(4)
-        rebuild(5)
         turn_residual(2)
         residual(3)
-        turn_residual(3)
-        turn_weighed(0)
-        quantise_by_feature(0, P)
-        weigh(1)
         scalar_steps([1], 0)
+        turn_weighed(0)
+        turn_residual(3)
+        round_chunk(4)
+        round_chunk(5)
+        quantise_coefficients(4)
+        rebuild(4)
+        gradient(0)
+        quantise_coefficients(5)
+        rebuild(5)
+        quantise_by_feature(0, P)
+        quantise_gradient(0)
+        project(0)
 
-        weigh_beside(2, made["gap", 1])
-        weigh_beside(3)
-        scalar_steps([2, 3], 1)
+        weigh_beside(1, as_floats(made["by_feature", 0, P]))
+        scalar_steps([2], 1)
         residual(4)
         turn_residual(4)
-        gradient(0)
-        turn_weighed(1)
         residual(5)
+        turn_weighed(1)
         turn_residual(5)
-        turn_weighed(2)
+        scalar_steps([3], 2)
         round_pair(6, VEC)
-        quantise_gradient(0)
+        quantise_by_feature(1, HALF)
         quantise_coefficients(6)
         rebuild(6)
         rebuild(7)
-        project(0)
-        turn_weighed(3)
-        gradient(1)
-        lay_features(1, HALF, HALF, VEC)
-        quantise_gradient(1)
         quantise_by_feature(1, 0)
 
-        weigh_beside(4, as_floats(made["by_feature", 1, 0]))
-        weigh_beside(5)
-        scalar_steps([4, 5], 2)
+        weigh_beside(2, as_floats(made["z_bf", 6]))
+        weigh_beside(3)
+        weigh_beside(4)
+        scalar_steps([4], 3)
+        gradient(1)
+        store(0, VEC)
+        turn_weighed(2)
         residual(6)
-        weigh_beside(6)
         turn_residual(6)
         residual(7)
+        turn_weighed(3)
+        scalar_steps([5], 4)
+        quantise_gradient(1)
+        quantise_by_feature(1, P)
         turn_residual(7)
-        project(1)
-        store(0, VEC)
-        gradient(2, together=2)
         turn_weighed(4)
-        gradient(3, together=2)
+        project(1)
+
+        weigh_beside(5, made["e_room", 1][:].bitcast(F32))
+        gradient(2)
+        gradient(3)
         turn_weighed(5)
-        turn_weighed(6)
-        store(1, VEC)
         quantise_gradient(2)
         project(2)
+        quantise_gradient(3)
         project(3)
-        quantise_by_feature(1, HALF)
+        scalar_steps([6], 5)
 
-        weigh_beside(LAST_CHUNK, as_floats(made["by_feature", 1, HALF]))
-        scalar_steps([6, 7], 4)
+        weigh_beside(6, made["e_room", 2][:].bitcast(F32))
+        weigh_beside(7)
         gradient(4)
+        turn_weighed(6)
         gradient(5)
+        store(1, VEC)
+        turn_weighed(7)
+        scalar_steps([7], 6)
         quantise_gradient(4)
-        turn_weighed(LAST_CHUNK)
         project(4)
-        store(2, VEC)
-        inverse_in_parts(6, [(LOW, ALL_SAMPLES), (HIGH, ALL_SAMPLES)])
         quantise_gradient(5)
         project(5)
+        store(2, SCA)
         gradient(6)
-
         inverse_in_parts(LAST_CHUNK, [(ALL_PLANES, samples) for samples in LAST_HALVES])
-        gradient(LAST_CHUNK, LAST_HALVES[0])
+        store(3, VEC)
         quantise_gradient(6)
         project(6)
+        gradient(LAST_CHUNK, LAST_HALVES[0])
         gradient(LAST_CHUNK, LAST_HALVES[1])
-        for k in (3, 4, 5):
+        for k in (4, 5, 6):
             store(k, SCA)
         quantise_gradient(LAST_CHUNK)
         project(LAST_CHUNK, slice(0, HALF))
         project(LAST_CHUNK, slice(HALF, N))
-        store(6, VEC)
-        store(LAST_CHUNK, SCA, slice(0, HALF), nc.scalar)
-        store(LAST_CHUNK, VEC, slice(HALF, N))
+        store(LAST_CHUNK, VEC, slice(0, HALF))
+        store(LAST_CHUNK, SCA, slice(HALF, N), nc.scalar)

@@ -341,13 +341,14 @@ def tile_attend_gdi_cau_z_kernel(tc, zT, wT, xm, wt, cs, offs, out):
         turn_atoms(1, 2)
         turn_atoms(0, LAST_PLANE)
         lay_features(0, 0, P, ALL_PLANES, VEC)
-        lay_slots(0, 2, VEC)
+        lay_features(0, P + HALF, P, HIGH, VEC)
+        lay_features(0, P, HALF, HIGH, VEC)
         round_chunk(0)
-        round_chunk(1)
+        lay_slots(0, 2, VEC)
         lay_slots(0, LAST_PLANE, SCA)
         quantise_coefficients(0)
+        round_chunk(1)
         quantise_by_slot(0, 2)
-        lay_features(0, P + HALF, P, HIGH, VEC)
         quantise_by_slot(0, LAST_PLANE)
         turn_atoms(1, LAST_PLANE)
         rebuild(0, LOW)
@@ -359,7 +360,6 @@ def tile_attend_gdi_cau_z_kernel(tc, zT, wT, xm, wt, cs, offs, out):
         lay_slots(1, LAST_PLANE, SCA)
         lay_features(1, P, P, ALL_PLANES, SCA)
         round_chunk(2, SCA)
-        lay_features(0, P, HALF, HIGH, VEC)
         quantise_by_slot(1, 2)
         lay_features_beside(1, HALF, made["slot_room", 1, 2][:].rearrange("p (s t) -> p s t", t=PACK))
         residual(0, LOW)

@@ -413,8 +413,8 @@ def tile_attend_gdi_cau_z_kernel(tc, zT, wT, xm, wt, cs, offs, out):
         quantise_by_feature(1, 0)
 
         weigh_beside(2, as_floats(made["z_bf", 6]))
-        weigh_beside(3)
-        weigh_beside(4)
+        weigh_beside(3, made["gap", 2])
+        weigh_beside(4, made["gap", 3])
         scalar_steps([4], 3)
         gradient(1)
         store(0, VEC)
@@ -441,7 +441,7 @@ def tile_attend_gdi_cau_z_kernel(tc, zT, wT, xm, wt, cs, offs, out):
         scalar_steps([6], 5)
 
         weigh_beside(6, made["e_room", 2][:].bitcast(F32))
-        weigh_beside(7)
+        weigh_beside(7, made["gap", 6])
         gradient(4)
         turn_weighed(6)
         gradient(5)

@@ -34,6 +34,7 @@ VEC, SCA, GPS = "vector", "scalar", "gpsimd"
 RING_BUFS = {VEC: 40, SCA: 14, GPS: 4}
 PLANE_BUFS = 3
 NO_INVERSE = []
+IN_HALVES = (0, 2)
 BANKS = 8
 SMALLEST_CS = 2.0**-60
 
@@ -218,7 +219,7 @@ def tile_attend_gdi_cau_z_kernel(tc, zT, wT, xm, wt, cs, offs, out):
             if k % together == 0:
                 made["gap_sq", k] = ring(SCA, [P, PACK, together, P], F32, "gap_sq")
             squares = made["gap_sq", k - k % together]
-            for planes_now in [LOW, HIGH] if k == 0 else [ALL_PLANES]:
+            for planes_now in [LOW, HIGH] if k in IN_HALVES else [ALL_PLANES]:
                 nc.scalar.activation(squares[:, planes_now, k % together, :],
                                      made["gap_bank", k, planes_now.start][:, planes_now], ACT.Square)
 
@@ -370,7 +371,8 @@ def tile_attend_gdi_cau_z_kernel(tc, zT, wT, xm, wt, cs, offs, out):
         turn_residual(1)
         quantise_coefficients(2)
         round_chunk(3)
-        rebuild(2)
+        rebuild(2, LOW)
+        rebuild(2, HIGH)
         quantise_by_slot(1, LAST_PLANE)
         quantise_by_feature(0, 0)
         quantise_coefficients(3)
@@ -378,34 +380,34 @@ def tile_attend_gdi_cau_z_kernel(tc, zT, wT, xm, wt, cs, offs, out):
         square(0, 1)
         root(0)
         quantise_by_feature(0, P + HALF)
-
-        weigh_beside(0, made["z_room", 3][:].bitcast(F32))
-        residual(2)
-        turn_residual(2)
-        residual(3)
+        quantise_by_feature(0, P)
+        for planes_now in (LOW, HIGH):
+            residual(2, planes_now)
+            turn_residual(2, planes_now)
         scalar_steps([1], 0)
-        turn_weighed(0)
-        turn_residual(3)
         round_chunk(4)
         round_chunk(5)
         quantise_coefficients(4)
         rebuild(4)
-        gradient(0)
         quantise_coefficients(5)
         rebuild(5)
-        quantise_by_feature(0, P)
-        quantise_gradient(0)
-        project(0)
 
-        weigh_beside(1, as_floats(made["by_feature", 0, P]))
+        weigh_beside(0, made["z_room", 5][:].bitcast(F32))
+        weigh_beside(1, made["gap", 0])
         scalar_steps([2], 1)
+        residual(3)
+        turn_residual(3)
         residual(4)
-        turn_residual(4)
+        turn_weighed(0)
         residual(5)
+        turn_residual(4)
+        gradient(0)
+        scalar_steps([3], 2)
         turn_weighed(1)
         turn_residual(5)
-        scalar_steps([3], 2)
         round_pair(6, VEC)
+        quantise_gradient(0)
+        project(0)
         quantise_by_feature(1, HALF)
         quantise_coefficients(6)
         rebuild(6)

@@ -34,7 +34,7 @@ VEC, SCA, GPS = "vector", "scalar", "gpsimd"
 RING_BUFS = {VEC: 40, SCA: 14, GPS: 4}
 PLANE_BUFS = 3
 NO_INVERSE = []
-IN_HALVES = (0, 2)
+IN_HALVES = (0, 2, 3)
 BANKS = 8
 SMALLEST_CS = 2.0**-60
 
@@ -206,7 +206,7 @@ def tile_attend_gdi_cau_z_kernel(tc, zT, wT, xm, wt, cs, offs, out):
                 made["gap", k] = ring(VEC, [P, D], F32, "gap")
             targets = x_raw[b, c // 2][:, c % 2, :]
             nc.vector.tensor_tensor(made["gap", k][:].rearrange("m (t c i) -> m c t i", t=PACK, i=2)[:, :, planes_now],
-                                    made["rec", k, planes_now.start][:].rearrange("m t (c i) -> m c t i", i=2)[:, :, planes_now],
+                                    made.get(("rec", k, planes_now.start), made["rec", k, 0])[:].rearrange("m t (c i) -> m c t i", i=2)[:, :, planes_now],
                                     targets.rearrange("m (c i t) -> m c t i", t=PACK, i=2)[:, :, planes_now], ALU.subtract)
 
         def turn_residual(k, planes_now=ALL_PLANES):
@@ -304,7 +304,7 @@ def tile_attend_gdi_cau_z_kernel(tc, zT, wT, xm, wt, cs, offs, out):
             b, c = divmod(k, CHUNKS)
             rows = out[b, HALF * (c // 2) : HALF * (c // 2 + 1), :].rearrange("(m j) i -> m j i", j=2)[:, c % 2, :]
             staged = ring(engine, [P, cols.stop - cols.start], F32, "staged")
-            move(engine, staged[:], made["sums", k, cols.start][:].rearrange("m a c -> m (a c)")[:, cols])
+            move(engine, staged[:], made.get(("sums", k, cols.start), made["sums", k, 0])[:].rearrange("m a c -> m (a c)")[:, cols])
             queue.dma_start(out=rows[:, cols], in_=staged[:])
 
         gather(0, 0, VEC)
@@ -361,14 +361,14 @@ def tile_attend_gdi_cau_z_kernel(tc, zT, wT, xm, wt, cs, offs, out):
         lay_slots(1, LAST_PLANE, SCA)
         lay_features(1, P, P, ALL_PLANES, SCA)
         round_chunk(2, SCA)
-        quantise_by_slot(1, 2)
-        lay_features_beside(1, HALF, made["slot_room", 1, 2][:].rearrange("p (s t) -> p s t", t=PACK))
+        lay_features_beside(1, HALF, made["z_room", 1][:].rearrange("p (s t) -> p s t", t=PACK))
         residual(0, LOW)
         turn_residual(0, LOW)
         residual(0, HIGH)
         turn_residual(0, HIGH)
         residual(1)
         turn_residual(1)
+        quantise_by_slot(1, 2)
         quantise_coefficients(2)
         round_chunk(3)
         rebuild(2, LOW)
@@ -379,7 +379,6 @@ def tile_attend_gdi_cau_z_kernel(tc, zT, wT, xm, wt, cs, offs, out):
         rebuild(3)
         square(0, 1)
         root(0)
-        quantise_by_feature(0, P + HALF)
         quantise_by_feature(0, P)
         for planes_now in (LOW, HIGH):
             residual(2, planes_now)
@@ -391,12 +390,15 @@ def tile_attend_gdi_cau_z_kernel(tc, zT, wT, xm, wt, cs, offs, out):
         rebuild(4)
         quantise_coefficients(5)
         rebuild(5)
+        quantise_by_feature(0, P + HALF)
 
         weigh_beside(0, made["z_room", 5][:].bitcast(F32))
         weigh_beside(1, made["gap", 0])
+        weigh_beside(2, made["gap", 1])
         scalar_steps([2], 1)
-        residual(3)
-        turn_residual(3)
+        for planes_now in (LOW, HIGH):
+            residual(3, planes_now)
+            turn_residual(3, planes_now)
         residual(4)
         turn_weighed(0)
         residual(5)
@@ -414,8 +416,7 @@ def tile_attend_gdi_cau_z_kernel(tc, zT, wT, xm, wt, cs, offs, out):
         rebuild(7)
         quantise_by_feature(1, 0)
 
-        weigh_beside(2, as_floats(made["z_bf", 6]))
-        weigh_beside(3, made["gap", 2])
+        weigh_beside(3, as_floats(made["z_bf", 6]))
         weigh_beside(4, made["gap", 3])
         scalar_steps([4], 3)
         gradient(1)

@@ -98,9 +98,9 @@ def tile_attend_gdi_cau_z_kernel(tc, zT, wT, xm, wt, cs, offs, out):
             load_targets(0, 0)
             load_coefficients(0, [1])
             load_targets(0, 1)
-            load_coefficients(1, [0])
             nc.sync.dma_start(out=wt_cols[:].rearrange("m (g j) -> m g j", j=2),
                               in_=wt.rearrange("b (h m j) o -> m (b h) (j o)", m=P, j=2))
+            load_coefficients(1, [0])
             load_targets(1, 0)
             load_coefficients(1, [1])
             load_targets(1, 1)
@@ -263,7 +263,7 @@ def tile_attend_gdi_cau_z_kernel(tc, zT, wT, xm, wt, cs, offs, out):
             made["numerator", k] = weighed_bank
 
         def gradient(k, samples=ALL_SAMPLES, together=1):
-            if samples.start == 0 and together:
+            if ("e", k) not in made and together:
                 made["e_room", k] = ring(VEC, [P, 2 * D], BF16, "e")
                 made["e_tile", k] = made["e_room", k][:, 0 : together * D]
                 for j in range(together):
@@ -278,6 +278,16 @@ def tile_attend_gdi_cau_z_kernel(tc, zT, wT, xm, wt, cs, offs, out):
             nc.vector.tensor_tensor(once[:], made["numerator", k][:], made["root", k][:, :, 0, :], ALU.mult)
             made["numerator", k] = once
             made["inverse", k] = made["root", k][:, :, 0, :]
+
+        def times_root(k, samples):
+            made["once", k] = ring(VEC, [P, PACK, samples.stop - samples.start], F32, "once")
+            nc.vector.tensor_tensor(made["once", k][:], made["numerator", k][:, :, samples], made["root", k][:, :, 0, samples], ALU.mult)
+
+        def gradient_by_roots(k, samples):
+            e_now = made["e", k].rearrange("p (m t) -> p m t", t=PACK)[:, samples]
+            nc.vector.tensor_tensor(e_now.rearrange("p (c i) t -> p c t i", i=2),
+                                    made["once", k][:].rearrange("p t (c i) -> p c t i", i=2),
+                                    made["root", k][:, :, 0, samples].rearrange("p t (c i) -> p c t i", i=2), ALU.mult)
 
         def inverse_beside(k, onto):
             nc.gpsimd.tensor_tensor(onto, made["root", k][:].rearrange("p t j m -> p (t j m)"), made["root", k][:].rearrange("p t j m -> p (t j m)"), ALU.mult)
@@ -362,13 +372,13 @@ def tile_attend_gdi_cau_z_kernel(tc, zT, wT, xm, wt, cs, offs, out):
         lay_features(1, P, P, ALL_PLANES, SCA)
         round_chunk(2, SCA)
         lay_features_beside(1, HALF, made["z_room", 1][:].rearrange("p (s t) -> p s t", t=PACK))
+        quantise_by_slot(1, 2)
         residual(0, LOW)
         turn_residual(0, LOW)
         residual(0, HIGH)
         turn_residual(0, HIGH)
         residual(1)
         turn_residual(1)
-        quantise_by_slot(1, 2)
         quantise_coefficients(2)
         round_chunk(3)
         rebuild(2, LOW)
@@ -380,9 +390,11 @@ def tile_attend_gdi_cau_z_kernel(tc, zT, wT, xm, wt, cs, offs, out):
         square(0, 1)
         root(0)
         quantise_by_feature(0, P)
+        weigh(0)
         for planes_now in (LOW, HIGH):
             residual(2, planes_now)
             turn_residual(2, planes_now)
+        turn_weighed(0)
         scalar_steps([1], 0)
         round_chunk(4)
         round_chunk(5)
@@ -392,15 +404,13 @@ def tile_attend_gdi_cau_z_kernel(tc, zT, wT, xm, wt, cs, offs, out):
         rebuild(5)
         quantise_by_feature(0, P + HALF)
 
-        weigh_beside(0, made["z_room", 5][:].bitcast(F32))
-        weigh_beside(1, made["gap", 0])
+        weigh_beside(1, made["z_room", 5][:].bitcast(F32))
         weigh_beside(2, made["gap", 1])
         scalar_steps([2], 1)
         for planes_now in (LOW, HIGH):
             residual(3, planes_now)
             turn_residual(3, planes_now)
         residual(4)
-        turn_weighed(0)
         residual(5)
         turn_residual(4)
         gradient(0)
@@ -428,7 +438,6 @@ def tile_attend_gdi_cau_z_kernel(tc, zT, wT, xm, wt, cs, offs, out):
         turn_weighed(3)
         scalar_steps([5], 4)
         quantise_gradient(1)
-        quantise_by_feature(1, P)
         turn_residual(7)
         turn_weighed(4)
         project(1)
@@ -437,6 +446,7 @@ def tile_attend_gdi_cau_z_kernel(tc, zT, wT, xm, wt, cs, offs, out):
         gradient(2)
         gradient(3)
         turn_weighed(5)
+        quantise_by_feature(1, P)
         quantise_gradient(2)
         project(2)
         quantise_gradient(3)
@@ -457,16 +467,19 @@ def tile_attend_gdi_cau_z_kernel(tc, zT, wT, xm, wt, cs, offs, out):
         project(5)
         store(2, SCA)
         gradient(6)
-        inverse_in_parts(LAST_CHUNK, [(ALL_PLANES, samples) for samples in LAST_HALVES])
-        store(3, VEC)
+        inverse_in_parts(LAST_CHUNK, [(ALL_PLANES, LAST_HALVES[0])])
+        times_root(LAST_CHUNK, LAST_HALVES[1])
         quantise_gradient(6)
         project(6)
+        made["e_room", LAST_CHUNK] = ring(VEC, [P, D], BF16, "e")
+        made["e_tile", LAST_CHUNK] = made["e", LAST_CHUNK] = made["e_room", LAST_CHUNK][:]
+        gradient_by_roots(LAST_CHUNK, LAST_HALVES[1])
         gradient(LAST_CHUNK, LAST_HALVES[0])
-        gradient(LAST_CHUNK, LAST_HALVES[1])
-        for k in (4, 5, 6):
+        for k in (3, 4, 5):
             store(k, SCA)
         quantise_gradient(LAST_CHUNK)
         project(LAST_CHUNK, slice(0, HALF))
         project(LAST_CHUNK, slice(HALF, N))
-        store(LAST_CHUNK, VEC, slice(0, HALF))
-        store(LAST_CHUNK, SCA, slice(HALF, N), nc.scalar)
+        store(6, VEC)
+        store(LAST_CHUNK, SCA, slice(0, HALF), nc.scalar)
+        store(LAST_CHUNK, VEC, slice(HALF, N))

from contextlib import ExitStack

import concourse.mybir as mybir
from concourse.masks import make_identity

B, N, T, D, R = 2, 512, 2048, 512, 512
FLOPS = 2 * 2 * B * R * N * D

F32 = mybir.dt.float32
BF16 = mybir.dt.bfloat16
U32 = mybir.dt.uint32
U16 = mybir.dt.uint16
U8 = mybir.dt.uint8
E4M3 = mybir.dt.float8_e4m3fn_x4
E5M2 = mybir.dt.float8_e5m2_x4
ALU = mybir.AluOpType
ACT = mybir.ActivationFunctionType

P = 128
PACK = 4
LAST_PLANE = PACK - 1
CHUNKS = R // P
ALL_CHUNKS = B * CHUNKS
LAST_CHUNK = ALL_CHUNKS - 1
BAND = 16
HALF = 256
EARLY_SHARE = 128
LAST_SHARE = 320
RUN = 4
ALL_PLANES, LOW, HIGH = slice(0, PACK), slice(0, 2), slice(2, PACK)
ALL_SAMPLES = slice(0, P)
LAST_HALVES = [slice(0, P // 2), slice(P // 2, P)]
VEC, SCA, GPS = "vector", "scalar", "gpsimd"
RING_BUFS = {VEC: 40, SCA: 14, GPS: 4}
PLANE_BUFS = 3
NO_INVERSE = []
IN_HALVES = (0, 2, 3)
BANKS = 8
SMALLEST_CS = 2.0**-60


def tile_attend_gdi_cau_z_kernel(tc, zT, wT, xm, wt, cs, offs, out):
    nc = tc.nc
    with ExitStack() as ctx:
        keep = ctx.enter_context(tc.tile_pool(name="keep", bufs=1))
        work = ctx.enter_context(tc.tile_pool(name="work", bufs=1))
        psum = ctx.enter_context(tc.psum_pool(name="psum", bufs=BANKS))

        def ring(engine, shape, dtype, name):
            return work.tile(shape, dtype, name=name, tag=engine, bufs=RING_BUFS[engine], align_bytes=64)

        def bank_tile(name):
            return psum.tile([P, PACK, P], F32, name=name, tag="bank")

        def as_floats(laid):
            return laid[:].rearrange("p i t -> p (i t)").bitcast(F32)

        def move(engine, dst, src):
            if engine == SCA:
                nc.scalar.copy(dst, src)
            else:
                nc.vector.tensor_copy(out=dst, in_=src)

        offsets = keep.tile([P, B * N // BAND], U16, name="offsets")
        wt_cols = keep.tile([P, ALL_CHUNKS], F32, name="wt_cols")
        ident = keep.tile([P, P], F32, name="ident")
        make_identity(nc, ident[:])
        c_cols = keep.tile([P, PACK], F32, name="c_cols")

        w_planes = wT.rearrange("(p t) c -> p t c", t=PACK)
        planes = {}
        z_raw = {}
        x_raw = {}

        def load_plane(t):
            planes[t] = work.tile([P, T], F32, name="plane", tag="plane", bufs=PLANE_BUFS, align_bytes=64)
            nc.sync.dma_start(out=planes[t][:], in_=w_planes[:, t, :])

        def load_coefficients(b, halves):
            raw = keep.tile([P, PACK, HALF * len(halves)], F32, name=f"z_raw{b}{halves[0]}", align_bytes=64)
            nc.sync.dma_start(out=raw[:], in_=zT[b].rearrange("(p t) r -> p t r", t=PACK)[:, :, HALF * halves[0] : HALF * (halves[-1] + 1)])
            for n, h in enumerate(halves):
                z_raw[b, h] = raw[:, :, HALF * n : HALF * (n + 1)]

        def load_targets(b, h):
            x_raw[b, h] = keep.tile([P, 2, D], F32, name=f"x_raw{b}{h}", align_bytes=64)
            nc.sync.dma_start(out=x_raw[b, h][:], in_=xm[b, HALF * h : HALF * (h + 1), :].rearrange("(m j) d -> m j d", j=2))

        load_plane(0)
        nc.sync.dma_start(out=c_cols[:], in_=cs[0, :].rearrange("(p t) -> p t", t=PACK))
        nc.sync.dma_start(offsets[:], offs)
        for t in range(1, LAST_PLANE):
            load_plane(t)

        def load_the_rest():
            load_plane(LAST_PLANE)
            load_coefficients(0, [0])
            load_targets(0, 0)
            load_coefficients(0, [1])
            load_targets(0, 1)
            nc.sync.dma_start(out=wt_cols[:].rearrange("m (g j) -> m g j", j=2),
                              in_=wt.rearrange("b (h m j) o -> m (b h) (j o)", m=P, j=2))
            load_coefficients(1, [0])
            load_targets(1, 0)
            load_coefficients(1, [1])
            load_targets(1, 1)

        seed = keep.tile([P, PACK], F32, name="seed")
        c_sq = keep.tile([P, PACK], F32, name="c_sq")
        seed_sq = keep.tile([P, PACK], F32, name="seed_sq")
        guess = keep.tile([P, PACK], F32, name="guess")
        nc.scalar.activation(seed[:], c_cols[:], ACT.Abs_reciprocal_sqrt, bias=SMALLEST_CS)

        def guess_noise():
            nc.scalar.activation(c_sq[:], c_cols[:], ACT.Square)
            nc.scalar.activation(seed_sq[:], seed[:], ACT.Square)
            nc.scalar.activation(guess[:], seed_sq[:], ACT.Square)

        picked = [keep.tile([P, PACK * N], BF16, name=f"picked{b}", align_bytes=64) for b in range(B)]
        made = {}

        def plane_of(b, t):
            return picked[b][:, N * t : N * (t + 1)]

        def gather(b, t, engine, first=0, width=N):
            listed = offsets[:, (b * N + first) // BAND : (b * N + first + width) // BAND]
            dst = plane_of(b, t)[:, first : first + width]
            if engine == SCA:
                nc.scalar.activation(dst, planes[t][:].indirect(listed), ACT.Copy)
            else:
                nc.vector.tensor_copy(dst, planes[t][:].indirect(listed))

        def turn_atoms(b, t):
            made["atom_bank", b, t] = bank_tile("atom_bank")
            words = plane_of(b, t).bitcast(F32)
            for u in range(2):
                nc.tensor.transpose(made["atom_bank", b, t][:, u, :], words[:, u : N // 2 : 2], ident[:])

        def lay_slots(b, t, engine, onto=None):
            if onto is None:
                made["slot_room", b, t] = ring(engine, [P, 2 * N], BF16, "by_slot")
                onto = made["slot_room", b, t][:, 0:N]
            made["by_slot", b, t] = onto
            move(engine, made["by_slot", b, t].bitcast(F32).rearrange("m (c i u) -> m c u i", i=2, u=2),
                 made["atom_bank", b, t][:, 0:2, :].rearrange("m u (c i) -> m c u i", i=2))

        def quantise_by_slot(b, t):
            codes = ring(VEC, [P, P], U32, "slot_codes")
            scales = keep.tile([P, P], U8, name=f"slot_scales{b}{t}", align_bytes=64)
            nc.vector.quantize_mx(out=codes[:].bitcast(E4M3), scales=scales[:], in_=made["by_slot", b, t])
            made["slot_codes", b, t] = (codes, scales)

        def lay_features(b, first, width, planes_now, engine):
            if planes_now.start == 0:
                made["by_feature", b, first] = ring(engine, [P, width, PACK], BF16, "by_feature")
            move(engine, made["by_feature", b, first][:, :, planes_now].rearrange("p (c i) t -> p c t i", i=RUN),
                 picked[b][:].rearrange("p (t c i) -> p c t i", t=PACK, i=RUN)[:, first // RUN : (first + width) // RUN, planes_now])

        def lay_features_beside(b, first, onto):
            made["by_feature", b, first] = onto
            nc.gpsimd.tensor_scalar(onto, picked[b][:].rearrange("p (t i) -> p i t", t=PACK)[:, first : first + onto.shape[1]],
                                    1.0, 0.0, ALU.mult, ALU.add)

        def quantise_by_feature(b, first):
            laid = made["by_feature", b, first]
            width = laid.shape[1]
            codes = ring(VEC, [P, width], U32, "feature_codes")
            scales = keep.tile([P, width], U8, name=f"feature_scales{b}{first}", align_bytes=64)
            nc.vector.quantize_mx(out=codes[:].bitcast(E4M3), scales=scales[:], in_=laid[:].rearrange("p i t -> p (i t)"))
            made.setdefault(("feature_codes", b), []).append((slice(first, first + width), codes, scales))

        def round_chunk(k, engine=VEC):
            b, c = divmod(k, CHUNKS)
            made["z_room", k] = ring(engine, [P, 2 * D], BF16, "z_bf")
            made["z_bf", k] = made["z_room", k][:, 0:D].rearrange("p (m t) -> p m t", t=PACK)
            samples = z_raw[b, c // 2].rearrange("p t (m j) -> p t m j", j=2)[:, :, :, c % 2]
            move(engine, made["z_bf", k][:].rearrange("p (c i) t -> p c t i", i=RUN),
                 samples.rearrange("p t (c i) -> p c t i", i=RUN))

        def round_pair(k, engine):
            b, c = divmod(k, CHUNKS)
            made["z_bf", k] = ring(engine, [P, 2 * P, PACK], BF16, "z_bf")
            move(engine, made["z_bf", k][:].rearrange("p (j c i) t -> p c t i j", j=2, i=2),
                 z_raw[b, c // 2].rearrange("p t (c i j) -> p c t i j", i=2, j=2))

        def quantise_coefficients(k):
            count = made["z_bf", k].shape[1] // P
            codes = ring(VEC, [P, count * P], U32, "z_codes")
            scales = keep.tile([P, count * P], U8, name=f"z_scales{k}", align_bytes=64)
            nc.vector.quantize_mx(out=codes[:].bitcast(E4M3), scales=scales[:],
                                  in_=made["z_bf", k][:].rearrange("p r t -> p (r t)"))
            for n in range(count):
                made["z", k + n] = (codes[:, P * n : P * (n + 1)], scales[:, P * n : P * (n + 1)])

        def rebuild(k, planes_now=ALL_PLANES):
            made["rec", k, planes_now.start] = bank_tile("rec")
            z_codes, z_scales = made["z", k]
            for t in range(PACK)[planes_now]:
                codes, scales = made["slot_codes", k // CHUNKS, t]
                nc.tensor.matmul_mx(out=made["rec", k, planes_now.start][:, t, :], lhsT=z_codes.bitcast(E4M3), lhsT_scale=z_scales,
                                    rhs=codes[:].bitcast(E4M3), rhs_scale=scales[:], start=True, stop=True)

        def residual(k, planes_now=ALL_PLANES):
            b, c = divmod(k, CHUNKS)
            if planes_now.start == 0:
                made["gap", k] = ring(VEC, [P, D], F32, "gap")
            targets = x_raw[b, c // 2][:, c % 2, :]
            nc.vector.tensor_tensor(made["gap", k][:].rearrange("m (t c i) -> m c t i", t=PACK, i=2)[:, :, planes_now],
                                    made.get(("rec", k, planes_now.start), made["rec", k, 0])[:].rearrange("m t (c i) -> m c t i", i=2)[:, :, planes_now],
                                    targets.rearrange("m (c i t) -> m c t i", t=PACK, i=2)[:, :, planes_now], ALU.subtract)

        def turn_residual(k, planes_now=ALL_PLANES):
            gap_bank = bank_tile("gap_bank")
            for t in range(PACK)[planes_now]:
                nc.tensor.transpose(gap_bank[:, t, :], made["gap", k][:, P * t : P * (t + 1)], ident[:])
            made["gap_bank", k, planes_now.start] = gap_bank

        def square(k, together):
            if k % together == 0:
                made["gap_sq", k] = ring(SCA, [P, PACK, together, P], F32, "gap_sq")
            squares = made["gap_sq", k - k % together]
            for planes_now in [LOW, HIGH] if k in IN_HALVES else [ALL_PLANES]:
                nc.scalar.activation(squares[:, planes_now, k % together, :],
                                     made["gap_bank", k, planes_now.start][:, planes_now], ACT.Square)

        def root(k):
            made["root", k] = ring(SCA, list(made["gap_sq", k].shape), F32, "root")
            for t in range(PACK):
                nc.scalar.activation(made["root", k][:, t], made["gap_sq", k][:, t], ACT.Abs_reciprocal_sqrt,
                                     bias=noise_sq[:, t : t + 1])

        def inverse(k):
            squared = ring(SCA, list(made["root", k].shape), F32, "inverse")
            nc.scalar.activation(squared[:], made["root", k][:], ACT.Square)
            for j in range(squared.shape[2]):
                made["inverse", k + j] = squared[:, :, j, :]

        def inverse_in_parts(k, parts):
            made["inverse", k] = ring(SCA, [P, PACK, P], F32, "inverse")
            for planes_now, samples in parts:
                nc.scalar.activation(made["inverse", k][:, planes_now, samples],
                                     made["root", k][:, planes_now, 0, samples], ACT.Square)

        def scalar_steps(chunks, previous):
            for k in chunks:
                square(k, len(chunks))
            if previous not in NO_INVERSE:
                inverse(previous)
            root(chunks[0])

        def weigh(k):
            made["weighed", k] = ring(VEC, [P, D], F32, "weighed")
            nc.vector.tensor_scalar(made["weighed", k][:], made["gap", k][:], wt_cols[:, k : k + 1], None, ALU.mult)

        def weigh_beside(k, onto=None):
            made["weighed", k] = ring(GPS, [P, D], F32, "weighed") if onto is None else onto
            nc.gpsimd.tensor_scalar(made["weighed", k][:], made["gap", k][:], wt_cols[:, k : k + 1], 0.0, ALU.mult, ALU.add)

        def turn_weighed(k):
            weighed_bank = bank_tile("weighed_bank")
            for t in range(PACK):
                nc.tensor.transpose(weighed_bank[:, t, :], made["weighed", k][:, P * t : P * (t + 1)], ident[:])
            made["numerator", k] = weighed_bank

        def gradient(k, samples=ALL_SAMPLES, together=1):
            if ("e", k) not in made and together:
                made["e_room", k] = ring(VEC, [P, 2 * D], BF16, "e")
                made["e_tile", k] = made["e_room", k][:, 0 : together * D]
                for j in range(together):
                    made["e", k + j] = made["e_tile", k][:, D * j : D * (j + 1)]
            e_now = made["e", k].rearrange("p (m t) -> p m t", t=PACK)[:, samples]
            nc.vector.tensor_tensor(e_now.rearrange("p (c i) t -> p c t i", i=2),
                                    made["numerator", k][:, :, samples].rearrange("p t (c i) -> p c t i", i=2),
                                    made["inverse", k][:, :, samples].rearrange("p t (c i) -> p c t i", i=2), ALU.mult)

        def halfway(k):
            once = ring(VEC, [P, PACK, P], F32, "once")
            nc.vector.tensor_tensor(once[:], made["numerator", k][:], made["root", k][:, :, 0, :], ALU.mult)
            made["numerator", k] = once
            made["inverse", k] = made["root", k][:, :, 0, :]

        def times_root(k, samples):
            made["once", k] = ring(VEC, [P, PACK, samples.stop - samples.start], F32, "once")
            nc.vector.tensor_tensor(made["once", k][:], made["numerator", k][:, :, samples], made["root", k][:, :, 0, samples], ALU.mult)

        def gradient_by_roots(k, samples):
            e_now = made["e", k].rearrange("p (m t) -> p m t", t=PACK)[:, samples]
            nc.vector.tensor_tensor(e_now.rearrange("p (c i) t -> p c t i", i=2),
                                    made["once", k][:].rearrange("p t (c i) -> p c t i", i=2),
                                    made["root", k][:, :, 0, samples].rearrange("p t (c i) -> p c t i", i=2), ALU.mult)

        def inverse_beside(k, onto):
            nc.gpsimd.tensor_tensor(onto, made["root", k][:].rearrange("p t j m -> p (t j m)"), made["root", k][:].rearrange("p t j m -> p (t j m)"), ALU.mult)
            made["inverse", k] = onto.rearrange("p (t m) -> p t m", t=PACK)

        def quantise_gradient(k):
            width = made["e_tile", k].shape[1] // PACK
            codes = ring(VEC, [P, width], U32, "e_codes")
            scales = keep.tile([P, width], U8, name=f"e_scales{k}", align_bytes=64)
            nc.vector.quantize_mx(out=codes[:].bitcast(E5M2), scales=scales[:], in_=made["e_tile", k])
            for j in range(width // P):
                made["e_codes", k + j] = codes[:, P * j : P * (j + 1)]
                made["e_scales", k + j] = scales[:, P * j : P * (j + 1)]

        def project(k, part=slice(0, N)):
            made["sums", k, part.start] = bank_tile("sums")
            for cols, codes, scales in made["feature_codes", k // CHUNKS]:
                if part.start <= cols.start < part.stop:
                    nc.tensor.matmul_mx(out=made["sums", k, part.start][:].rearrange("m a c -> m (a c)")[:, cols],
                                        lhsT=made["e_codes", k].bitcast(E5M2), lhsT_scale=made["e_scales", k],
                                        rhs=codes[:].bitcast(E4M3), rhs_scale=scales[:], start=True, stop=True)

        def store(k, engine, cols=slice(0, N), queue=nc.sync):
            b, c = divmod(k, CHUNKS)
            rows = out[b, HALF * (c // 2) : HALF * (c // 2 + 1), :].rearrange("(m j) i -> m j i", j=2)[:, c % 2, :]
            staged = ring(engine, [P, cols.stop - cols.start], F32, "staged")
            move(engine, staged[:], made.get(("sums", k, cols.start), made["sums", k, 0])[:].rearrange("m a c -> m (a c)")[:, cols])
            queue.dma_start(out=rows[:, cols], in_=staged[:])

        gather(0, 0, VEC)
        gather(1, 0, VEC, 0, EARLY_SHARE)
        gather(1, 0, SCA, EARLY_SHARE, N - EARLY_SHARE)
        load_the_rest()
        guess_noise()
        gather(0, 1, VEC)
        gather(1, 1, VEC, 0, EARLY_SHARE)
        gather(1, 1, SCA, EARLY_SHARE, N - EARLY_SHARE)
        for b in range(B):
            turn_atoms(b, 0)
            lay_slots(b, 0, SCA, plane_of(b, 2))
        for b in range(B):
            quantise_by_slot(b, 0)
        lay_features(0, P, HALF, LOW, VEC)
        lay_features(0, P + HALF, P, LOW, VEC)
        for b in range(B):
            turn_atoms(b, 1)
            lay_slots(b, 1, SCA, plane_of(b, 3))
        gather(0, 2, VEC)
        gather(1, 2, VEC, 0, EARLY_SHARE)
        gather(1, 2, SCA, EARLY_SHARE, N - EARLY_SHARE)
        minus_one = ring(VEC, [P, PACK], F32, "minus_one")
        nc.vector.scalar_tensor_tensor(minus_one[:], c_sq[:], -1.0, guess[:], ALU.mult, ALU.mult)
        for b in range(B):
            quantise_by_slot(b, 1)
        noise_sq = ring(VEC, [P, PACK], F32, "noise_sq")
        nc.vector.scalar_tensor_tensor(noise_sq[:], minus_one[:], 2.0, guess[:], ALU.add, ALU.mult)
        turn_atoms(0, 2)
        gather(0, LAST_PLANE, VEC, 0, LAST_SHARE - P)
        gather(0, LAST_PLANE, VEC, LAST_SHARE - P, P)
        gather(0, LAST_PLANE, SCA, LAST_SHARE, N - LAST_SHARE)
        gather(1, LAST_PLANE, SCA)
        turn_atoms(1, 2)
        turn_atoms(0, LAST_PLANE)
        lay_features(0, 0, P, ALL_PLANES, VEC)
        lay_features(0, P + HALF, P, HIGH, VEC)
        lay_features(0, P, HALF, HIGH, VEC)
        round_chunk(0)
        lay_slots(0, 2, VEC)
        lay_slots(0, LAST_PLANE, SCA)
        quantise_coefficients(0)
        round_chunk(1)
        quantise_by_slot(0, 2)
        quantise_by_slot(0, LAST_PLANE)
        turn_atoms(1, LAST_PLANE)
        rebuild(0, LOW)
        quantise_coefficients(1)
        rebuild(0, HIGH)
        rebuild(1)
        lay_slots(1, 2, SCA)
        lay_features(1, 0, P, ALL_PLANES, SCA)
        lay_slots(1, LAST_PLANE, SCA)
        lay_features(1, P, P, ALL_PLANES, SCA)
        round_chunk(2, SCA)
        lay_features_beside(1, HALF, made["z_room", 1][:].rearrange("p (s t) -> p s t", t=PACK))
        quantise_by_slot(1, 2)
        residual(0, LOW)
        turn_residual(0, LOW)
        residual(0, HIGH)
        turn_residual(0, HIGH)
        residual(1)
        turn_residual(1)
        quantise_coefficients(2)
        round_chunk(3)
        rebuild(2, LOW)
        rebuild(2, HIGH)
        quantise_by_slot(1, LAST_PLANE)
        quantise_by_feature(0, 0)
        quantise_coefficients(3)
        rebuild(3)
        square(0, 1)
        root(0)
        quantise_by_feature(0, P)
        weigh(0)
        for planes_now in (LOW, HIGH):
            residual(2, planes_now)
            turn_residual(2, planes_now)
        turn_weighed(0)
        scalar_steps([1], 0)
        round_chunk(4)
        round_chunk(5)
        quantise_coefficients(4)
        rebuild(4)
        quantise_coefficients(5)
        rebuild(5)
        quantise_by_feature(0, P + HALF)

        weigh_beside(1, made["z_room", 5][:].bitcast(F32))
        weigh_beside(2, made["gap", 1])
        scalar_steps([2], 1)
        for planes_now in (LOW, HIGH):
            residual(3, planes_now)
            turn_residual(3, planes_now)
        residual(4)
        residual(5)
        turn_residual(4)
        gradient(0)
        scalar_steps([3], 2)
        turn_weighed(1)
        turn_residual(5)
        round_pair(6, VEC)
        quantise_gradient(0)
        project(0)
        quantise_by_feature(1, HALF)
        quantise_coefficients(6)
        rebuild(6)
        rebuild(7)
        quantise_by_feature(1, 0)

        weigh_beside(3, as_floats(made["z_bf", 6]))
        weigh_beside(4, made["gap", 3])
        scalar_steps([4], 3)
        gradient(1)
        store(0, VEC)
        turn_weighed(2)
        residual(6)
        turn_residual(6)
        residual(7)
        turn_weighed(3)
        scalar_steps([5], 4)
        quantise_gradient(1)
        turn_residual(7)
        turn_weighed(4)
        project(1)

        weigh_beside(5, made["e_room", 1][:].bitcast(F32))
        gradient(2)
        gradient(3)
        turn_weighed(5)
        quantise_by_feature(1, P)
        quantise_gradient(2)
        project(2)
        quantise_gradient(3)
        project(3)
        scalar_steps([6], 5)

        weigh_beside(6, made["e_room", 2][:].bitcast(F32))
        weigh_beside(7, made["gap", 6])
        gradient(4)
        turn_weighed(6)
        gradient(5)
        store(1, VEC)
        turn_weighed(7)
        scalar_steps([7], 6)
        quantise_gradient(4)
        project(4)
        quantise_gradient(5)
        project(5)
        store(2, SCA)
        gradient(6)
        inverse_in_parts(LAST_CHUNK, [(ALL_PLANES, LAST_HALVES[0])])
        times_root(LAST_CHUNK, LAST_HALVES[1])
        quantise_gradient(6)
        project(6)
        made["e_room", LAST_CHUNK] = ring(VEC, [P, D], BF16, "e")
        made["e_tile", LAST_CHUNK] = made["e", LAST_CHUNK] = made["e_room", LAST_CHUNK][:]
        gradient_by_roots(LAST_CHUNK, LAST_HALVES[1])
        gradient(LAST_CHUNK, LAST_HALVES[0])
        for k in (3, 4, 5):
            store(k, SCA)
        quantise_gradient(LAST_CHUNK)
        project(LAST_CHUNK, slice(0, HALF))
        project(LAST_CHUNK, slice(HALF, N))
        store(6, VEC)
        store(LAST_CHUNK, SCA, slice(0, HALF), nc.scalar)
        store(LAST_CHUNK, VEC, slice(HALF, N))
